import numpy as np
import ml_dtypes


def mxq(x, axis, fmt="e4m3"):
    dtype, down = {"e4m3": (ml_dtypes.float8_e4m3fn, 7), "e5m2": (ml_dtypes.float8_e5m2, 14)}[fmt]
    v = np.moveaxis(np.asarray(x, np.float32).astype(ml_dtypes.bfloat16).astype(np.float64), axis, -1)
    blocks = v.reshape(v.shape[:-1] + (-1, 32))
    amax = np.abs(blocks).max(-1, keepdims=True)
    byte = np.maximum(np.where(amax > 0, np.frexp(amax)[1] - 1 + 127, 0) - down, 1)
    scale = np.exp2(byte - 127.0)
    codes = (blocks / scale).astype(np.float32).astype(dtype).astype(np.float64)
    return np.moveaxis((codes * scale).reshape(v.shape), -1, axis)


WIDE = False


def mx_kscale(k):
    if not WIDE:
        return np.ones(k)
    levels = np.array([10, -10, 5, -5, 0])
    if k % 512:
        return np.exp2(np.random.permutation(np.resize(levels, k // 32))).repeat(32)
    a = np.empty((k // 512, 16))
    for p in range(k // 512):
        a[p, :8] = np.random.permutation(np.resize(levels, 8))
        for g in range(8):
            far = levels[np.abs(levels - a[p, g]) >= 10]
            a[p, g + 8] = far[np.random.randint(len(far))]
    return np.exp2(a.ravel()).repeat(32)


def f64(x):
    return np.asarray(x).astype(np.float64)


def striped(idx):
    return np.tile(idx.reshape(-1, 16).T, (8, 1)).astype(np.uint16)


def unstriped(offs):
    return offs[:16].T.reshape(-1).astype(np.int64)


E2M1 = np.array([0.0, 0.5, 1.0, 1.5, 2.0, 3.0, 4.0, 6.0, -0.0, -0.5, -1.0, -1.5, -2.0, -3.0, -4.0, -6.0])


def pack_weight(w, fmt):
    k, n = w.shape
    w = f64(np.asarray(w, np.float32).astype(ml_dtypes.bfloat16)).reshape(k // 32, 32, n)
    amax = np.abs(w).max(1)
    if fmt == "e4m3":
        byte = np.frexp(amax)[1] - 1 + 127 - 7
    else:
        mant, ex = np.frexp(amax / 6.0)
        byte = np.where(mant > 0.5, ex, ex - 1) + 127
    byte = np.clip(np.where(amax > 0, byte, 1), 1, 254)
    scaled = (w * np.exp2(127.0 - byte)[:, None, :]).reshape(k, n).astype(np.float32)
    by_word = np.ascontiguousarray(scaled.reshape(k // 512, 128, 4, n).transpose(0, 1, 3, 2))
    if fmt == "e4m3":
        words = by_word.astype(ml_dtypes.float8_e4m3fn).view(np.uint8)
    else:
        c = by_word.astype(ml_dtypes.float4_e2m1fn).view(np.uint8) & 0xF
        words = (c[..., 0::2] | (c[..., 1::2] << 4)).reshape(k // 512, 128, 2 * n)
    return np.ascontiguousarray(words), np.ascontiguousarray(byte.astype(np.uint8).reshape(k // 512, 16, n))


def unpack_weight(words, scales, fmt):
    g, _, n = scales.shape
    words = np.ascontiguousarray(words).reshape(g, 128, n, -1)
    if fmt == "e4m3":
        vals = words.view(ml_dtypes.float8_e4m3fn).astype(np.float64)
    else:
        nib = np.empty((g, 128, n, 4), np.uint8)
        nib[..., 0::2] = words & 0xF
        nib[..., 1::2] = words >> 4
        vals = E2M1[nib]
    vals = vals * np.repeat(np.exp2(scales.astype(np.float64) - 127.0), 8, axis=1)[..., None]
    return vals.transpose(0, 1, 3, 2).reshape(g * 512, n)


def gelu(v):
    return 0.5 * v * (1.0 + np.tanh(np.sqrt(2.0 / np.pi) * (v + 0.044715 * v**3)))


K, K2, K3, H, N, T, T2, T3, S = 1024, 512, 512, 1024, 512, 2048, 2048, 1024, 512

def setup_inputs():
    n = np.random.standard_normal
    f32 = np.float32
    s, s2, s3 = mx_kscale(K)[:, None], mx_kscale(K2)[:, None], mx_kscale(K3)[:, None]
    u = mx_kscale(H)[:, None]
    tab_words, tab_scales = pack_weight(n((K, T)) * s, "e4m3")
    tab2_words, tab2_scales = pack_weight(n((K2, T2)) * s2, "e4m3")
    tab3_words, tab3_scales = pack_weight(n((K3, T3)) * s3, "e2m1")
    w1_words, w1_scales = pack_weight(n((K, H)) / np.sqrt(K) / s, "e2m1")
    w4_words, w4_scales = pack_weight(n((H, N)) / np.sqrt(H) / u, "e4m3")
    return {
        "tab_words": tab_words, "tab_scales": tab_scales,
        "tab2_words": tab2_words, "tab2_scales": tab2_scales,
        "tab3_words": tab3_words, "tab3_scales": tab3_scales,
        "offs": striped(np.random.permutation(T)[:S]),
        "offs2": striped(np.random.permutation(T2)[:S]),
        "offs3": striped(np.random.permutation(T3)[:S]),
        "w1_words": w1_words, "w1_scales": w1_scales,
        "w2": (n((K2, H)) / np.sqrt(K2) / s2).astype(f32),
        "w3": (n((H, N)) / np.sqrt(H) / u).astype(f32),
        "w4_words": w4_words, "w4_scales": w4_scales,
        "w5": (n((K3, N)) / np.sqrt(K3) / s3).astype(f32),
        "g1": (np.exp(0.3 * n(H)) * u[:, 0]).astype(f32),
        "g2": (np.exp(0.3 * n(H)) * u[:, 0]).astype(f32),
    }

def reference(tab_words, tab_scales, tab2_words, tab2_scales, tab3_words, tab3_scales, offs, offs2, offs3,
              w1_words, w1_scales, w2, w3, w4_words, w4_scales, w5, g1, g2):
    v = unpack_weight(tab_words, tab_scales, "e4m3")[:, unstriped(offs)]
    v2 = unpack_weight(tab2_words, tab2_scales, "e4m3")[:, unstriped(offs2)]
    v3 = unpack_weight(tab3_words, tab3_scales, "e2m1")[:, unstriped(offs3)]
    h1 = np.tanh(unpack_weight(w1_words, w1_scales, "e2m1").T @ v) * f64(g1)[:, None]
    h2 = np.tanh(mxq(f64(w2), 0, "e4m3").T @ v2) * f64(g2)[:, None]
    y1 = mxq(f64(w3), 0, "e4m3").T @ mxq(h1, 0, "e4m3")
    y2 = unpack_weight(w4_words, w4_scales, "e4m3").T @ mxq(h2, 0, "e4m3")
    y3 = mxq(f64(w5), 0, "e4m3").T @ v3
    return np.maximum(y1, y2) - y3

@@ -1,0 +1,285 @@
+from contextlib import ExitStack
+
+import concourse.mybir as mybir
+from concourse.masks import make_identity
+
+FLOPS = 2952790016
+
+F32 = mybir.dt.float32
+BF16 = mybir.dt.bfloat16
+I32 = mybir.dt.int32
+U32 = mybir.dt.uint32
+U16 = mybir.dt.uint16
+U8 = mybir.dt.uint8
+FP8X4 = mybir.dt.float8_e4m3fn_x4
+FP4X4 = mybir.dt.float4_e2m1fn_x4
+ACT = mybir.ActivationFunctionType
+ALU = mybir.AluOpType
+
+P = 128
+S = 512
+N = 512
+H = 1024
+T1, T2, T3 = 2048, 2048, 1024
+TAB2_ROW = 4
+W4_ROW = 8
+
+
+def tile_list_volleyball_rally_commentary_kernel(
+    tc, tab_words, tab_scales, tab2_words, tab2_scales, tab3_words, tab3_scales, offs, offs2, offs3,
+    w1_words, w1_scales, w2, w3, w4_words, w4_scales, w5, g1, g2, out,
+):
+    nc = tc.nc
+    with ExitStack() as ctx:
+        keep = ctx.enter_context(tc.tile_pool(name="keep", bufs=1))
+        ring = ctx.enter_context(tc.tile_pool(name="ring", bufs=5))
+        psum = ctx.enter_context(tc.psum_pool(name="psum", bufs=8))
+
+        def held(shape, dtype, name):
+            return keep.tile(shape, dtype, name=name, align_bytes=64)
+
+        def staged(shape, dtype, name, tag):
+            return keep.tile(shape, dtype, name=name, tag=tag, align_bytes=64)
+
+        list1 = held([P, S // 16], U16, "list1")
+        list2 = held([P, S // 16], U16, "list2")
+        list3 = held([P, S // 16], U16, "list3")
+        t1w = [staged([P, T1], U32, "t1w0", "t1w0"), held([P, T1], U32, "t1w1")]
+        t2w = held([P, T2], U32, "t2w")
+        t3w = held([P, T3], U16, "t3w")
+        t1s = held([P, T1], U8, "t1s")
+        t2s = held([P, T2], U8, "t2s")
+        t3s = held([P, T3], U8, "t3s")
+        v1s_second = held([P, S], U8, "v1s_second")
+        w1w = held([P, 2, 2 * H], U8, "w1w")
+        w1s = held([P, 2, H], U8, "w1s")
+        w4w = held([P, 2, N], U32, "w4w")
+        w4s = held([P, N], U8, "w4s")
+        w2raw = [held([P, 4, 256], F32, f"w2raw{c}") for c in range(4)]
+        w5raw = held([P, 4, N], F32, "w5raw")
+        w3raw = [held([P, 4, N], F32, f"w3raw{b}") for b in range(2)]
+        g1rows = held([P, 2 * P], F32, "g1rows")
+        g1c = held([P, 2, 4], F32, "g1c")
+        g2c = held([P, 2, 4], F32, "g2c")
+        ident = held([P, P], F32, "ident")
+        zero_in = held([P, 1], F32, "zero_in")
+        zero = held([P, 1], F32, "zero")
+
+        nc.vector.memset(zero_in[:], 0.0)
+        nc.scalar.activation(zero[:], zero_in[:], ACT.Tanh)
+        nc.gpsimd.memset(t2s[:].bitcast(I32), 0)
+        nc.vector.memset(t1s[:].bitcast(I32), 0)
+        nc.gpsimd.memset(t3s[:].bitcast(I32), 0)
+        nc.gpsimd.memset(g1rows[:], 0.0)
+        make_identity(nc, ident[:])
+        nc.vector.memset(w1s[:].bitcast(I32), 0)
+        nc.vector.memset(w4s[:].bitcast(I32), 0)
+        nc.vector.memset(v1s_second[:].bitcast(I32), 0)
+
+        def load_rows(queue, plane, scales, row0):
+            rows = 4 * scales.shape[0]
+            for quad in range(4):
+                queue.dma_start(
+                    plane[32 * quad + row0 : 32 * quad + row0 + rows, :].bitcast(I32),
+                    scales[:, 4 * quad : 4 * quad + 4, :].bitcast(I32),
+                )
+
+        w2v = w2.rearrange("(p j) c -> p j c", j=4)
+
+        def load_w2(c):
+            nc.sync.dma_start(w2raw[c][:], w2v[:, :, 256 * c : 256 * (c + 1)])
+
+        def load_words(dst, words):
+            nc.sync.dma_start(dst.bitcast(I32), words.rearrange("p c i -> p (c i)").bitcast(I32))
+
+        nc.sync.dma_start(list2[:], offs2)
+        load_rows(nc.sync, t2s, tab2_scales, TAB2_ROW)
+        load_w2(0)
+        nc.sync.dma_start(list1[:], offs)
+        load_rows(nc.sync, t1s, tab_scales, 0)
+        load_w2(1)
+        load_rows(nc.sync, t3s, tab3_scales, 0)
+        load_w2(2)
+        nc.sync.dma_start(list3[:], offs3)
+        nc.sync.dma_start(t3w[:].bitcast(I32), tab3_words[0].bitcast(I32))
+        load_w2(3)
+        load_words(t2w[:], tab2_words[0])
+        load_words(t1w[0][:], tab_words[0])
+        nc.sync.dma_start(
+            g1rows[0:4, :].rearrange("t (x i) -> t x i", i=8), g1.rearrange("(x t i) -> t x i", t=4, i=8)
+        )
+        load_words(t1w[1][:], tab_words[1])
+        nc.sync.dma_start(w1w[:].bitcast(I32), w1_words.rearrange("a p c -> p a c").bitcast(I32))
+        nc.sync.dma_start(g2c[:], g2.rearrange("(b p t) -> p b t", b=2, t=4))
+        nc.sync.dma_start(w5raw[:], w5.rearrange("(p j) n -> p j n", j=4))
+        nc.sync.dma_start(w4w[:].bitcast(I32), w4_words.rearrange("a p c i -> p a (c i)").bitcast(I32))
+        load_rows(nc.sync, w4s, w4_scales, W4_ROW)
+        for b in range(2):
+            rows = w3[512 * b : 512 * (b + 1), :].rearrange("(q t i) n -> t q i n", t=4, i=8)
+            for t in range(4):
+                nc.sync.dma_start(w3raw[b][:, t, :], rows[t])
+
+        for quad in range(4):
+            nc.gpsimd.dma_start(
+                w1s[32 * quad : 32 * quad + 4, :, :].bitcast(I32),
+                w1_scales[:, 4 * quad : 4 * quad + 4, :].rearrange("a r c -> r a c").bitcast(I32),
+            )
+
+        def gather(dtype, window, offsets, name):
+            picked = held([P, S], dtype, name)
+            nc.vector.tensor_copy(picked[:], window.indirect(offsets[:]))
+            return picked
+
+        def quantise(grouped, name):
+            codes = held([P, 512], U32, name + "_codes")
+            plane = held([P, 512], U8, name + "_plane")
+            nc.vector.quantize_mx(out=codes[:].bitcast(FP8X4), scales=plane[:], in_=grouped[:])
+            return codes, plane
+
+        w2g = [held([P, 2048], BF16, f"w2g{b}") for b in range(2)]
+
+        def cast_w2(c):
+            b, half = divmod(c, 2)
+            dst = w2g[b][:].rearrange("p (t m j) -> p m j t", t=4, j=4)[:, 64 * half : 64 * (half + 1)]
+            nc.scalar.copy(dst, w2raw[c][:].rearrange("p j (m t) -> p m j t", t=4))
+
+        def weave(grouped, raw, lo, hi):
+            dst = grouped[:, 4 * lo : 4 * hi].rearrange("p (c i j) -> p c j i", i=4, j=4)
+            src = raw[:, :, lo:hi].rearrange("p j (c i) -> p c j i", i=4)
+            return dst, src
+
+        def hidden(b, pair, products, gain, grouped):
+            th = ring.tile([P, 2, 512], F32, name="th")
+            for u in range(2):
+                cols = slice(128 * (2 * pair + u), 128 * (2 * pair + u + 1))
+                bank = psum.tile([P, 4, P], F32, name="bank", tag="bank")
+                for t in range(4):
+                    products(bank[:, t, :], b, t, cols)
+                nc.scalar.activation(
+                    th[:, u, :].rearrange("p (s t) -> p s t", t=4), bank[:].rearrange("p t s -> p s t"),
+                    ACT.Tanh, bias=zero[:],
+                )
+            nc.vector.tensor_tensor(
+                grouped[:, 1024 * pair : 1024 * (pair + 1)].rearrange("p (s t) -> p s t", t=4),
+                th[:].rearrange("p u (s t) -> p (u s) t", t=4),
+                gain.unsqueeze(1).to_broadcast([P, 256, 4]),
+                ALU.mult,
+            )
+
+        v2s = gather(U8, t2s[:], list2, "v2s")
+        cast_w2(0)
+        cast_w2(1)
+        v1s_both = gather(U8, t1s[:], list1, "v1s_both")
+        nc.gpsimd.dma_start(v1s_second[0:100, :].bitcast(I32), v1s_both[4:104, :].bitcast(I32))
+        v1s = [v1s_both, v1s_second]
+        w2q = [quantise(w2g[0], "w2q0")]
+        cast_w2(2)
+        cast_w2(3)
+        v3w = gather(U16, t3w[:], list3, "v3w")
+        v3s = gather(U8, t3s[:], list3, "v3s")
+        w2q.append(quantise(w2g[1], "w2q1"))
+        v2w = gather(U32, t2w[:], list2, "v2w")
+
+        def products2(acc, b, t, cols):
+            codes, plane = w2q[b]
+            m = slice(128 * t, 128 * (t + 1))
+            nc.tensor.matmul_mx(
+                out=acc, lhsT=codes[:, m].bitcast(FP8X4), lhsT_scale=plane[:, m],
+                rhs=v2w[:, cols].bitcast(FP8X4), rhs_scale=v2s[TAB2_ROW:P, cols], start=True, stop=True,
+            )
+
+        h2g = [held([P, 2048], BF16, f"h2g{b}") for b in range(2)]
+        h1g = [held([P, 2048], BF16, f"h1g{b}") for b in range(2)]
+        v1w = [gather(U32, t1w[0][:], list1, "v1w0")]
+        w1ws = held([P, 4, 4, 256], U8, "w1ws")
+        w1ss = staged([P, 4, 4, P], U8, "w1ss", "t1w0")
+        nc.vector.tensor_copy(
+            w1ss[:].bitcast(I32).rearrange("p x t (q w) -> p x t q w", w=2),
+            w1s[:].bitcast(I32).rearrange("p a (b q t w) -> p (a b) t q w", b=2, t=4, w=2),
+        )
+        nc.vector.tensor_copy(
+            w1ws[:].bitcast(I32).rearrange("p x t (q w) -> p x t q w", w=4),
+            w1w[:].bitcast(I32).rearrange("p a (b q t w) -> p (a b) t q w", b=2, t=4, w=4),
+        )
+        v1w.append(gather(U32, t1w[1][:], list1, "v1w1"))
+        hidden(0, 0, products2, g2c[:, 0, :], h2g[0])
+        hidden(0, 1, products2, g2c[:, 0, :], h2g[0])
+        h2q = [quantise(h2g[0], "h2q0")]
+        hidden(1, 0, products2, g2c[:, 1, :], h2g[1])
+        hidden(1, 1, products2, g2c[:, 1, :], h2g[1])
+
+        gbank = psum.tile([P, 2, P], F32, name="gbank", tag="bank")
+        for b in range(2):
+            nc.tensor.transpose(gbank[:, b, :], g1rows[:, P * b : P * (b + 1)], ident[:])
+        nc.scalar.copy(g1c[:], gbank[:, :, 0:4])
+        h2q.append(quantise(h2g[1], "h2q1"))
+
+        w5g = held([P, 2048], BF16, "w5g")
+        for half in range(2):
+            dst, src = weave(w5g, w5raw, 256 * half, 256 * (half + 1))
+            nc.scalar.activation(dst, src, ACT.Copy, scale=-1.0)
+        w5q = quantise(w5g, "w5q")
+
+        def products1(acc, b, t, cols):
+            for a in range(2):
+                nc.tensor.matmul_mx(
+                    out=acc, lhsT=w1ws[:, 2 * a + b, t, :].bitcast(FP4X4), lhsT_scale=w1ss[:, 2 * a + b, t, :],
+                    rhs=v1w[a][:, cols].bitcast(FP8X4), rhs_scale=v1s[a][:, cols], start=(a == 0), stop=(a == 1),
+                )
+
+        def arena(acc, m):
+            nc.tensor.matmul_mx(
+                out=acc, lhsT=w5q[0][:, m].bitcast(FP8X4), lhsT_scale=w5q[1][:, m],
+                rhs=v3w[:].bitcast(FP4X4), rhs_scale=v3s[:], start=True, stop=False,
+            )
+
+        hidden(0, 0, products1, g1c[:, 0, :], h1g[0])
+        hidden(0, 1, products1, g1c[:, 0, :], h1g[0])
+        h1q = [quantise(h1g[0], "h1q0")]
+        hidden(1, 0, products1, g1c[:, 1, :], h1g[1])
+        hidden(1, 1, products1, g1c[:, 1, :], h1g[1])
+
+        w3g = [held([P, 2048], BF16, f"w3g{b}") for b in range(2)]
+        for half in range(2):
+            dst, src = weave(w3g[0], w3raw[0], 256 * half, 256 * (half + 1))
+            nc.scalar.copy(dst, src)
+        w3q = [quantise(w3g[0], "w3q0")]
+        h1q.append(quantise(h1g[1], "h1q1"))
+        dst, src = weave(w3g[1], w3raw[1], 0, 256)
+        nc.scalar.copy(dst, src)
+        dst, src = weave(w3g[1], w3raw[1], 256, 512)
+        nc.vector.tensor_copy(dst, src)
+        w3q.append(quantise(w3g[1], "w3q1"))
+
+        y2 = [held([P, S], F32, f"y2_{n}") for n in range(4)]
+        y2banks = []
+        for n in range(4):
+            m = slice(128 * n, 128 * (n + 1))
+            acc = psum.tile([P, S], F32, name="acc", tag="bank")
+            arena(acc[:], m)
+            for a in range(2):
+                nc.tensor.matmul_mx(
+                    out=acc[:], lhsT=w4w[:, a, m].bitcast(FP8X4), lhsT_scale=w4s[W4_ROW + 4 * a : P, m],
+                    rhs=h2q[a][0][:].bitcast(FP8X4), rhs_scale=h2q[a][1][:], start=False, stop=(a == 1),
+                )
+            y2banks.append(acc)
+        for n in range(4):
+            nc.scalar.copy(y2[n][:], y2banks[n][:])
+
+        y1banks = []
+        for n in range(4):
+            m = slice(128 * n, 128 * (n + 1))
+            acc = psum.tile([P, S], F32, name="acc", tag="bank")
+            arena(acc[:], m)
+            y1banks.append(acc)
+        for b in range(2):
+            for n in range(4):
+                m = slice(128 * n, 128 * (n + 1))
+                nc.tensor.matmul_mx(
+                    out=y1banks[n][:], lhsT=w3q[b][0][:, m].bitcast(FP8X4), lhsT_scale=w3q[b][1][:, m],
+                    rhs=h1q[b][0][:].bitcast(FP8X4), rhs_scale=h1q[b][1][:], start=False, stop=(b == 1),
+                )
+        for n in range(4):
+            res = held([P, S], F32, f"res{n}")
+            nc.vector.tensor_tensor(res[:], y1banks[n][:], y2[n][:], ALU.max)
+            nc.sync.dma_start(out[128 * n : 128 * (n + 1), :], res[:])

@@ -23,6 +23,8 @@ H = 1024
 T1, T2, T3 = 2048, 2048, 1024
 TAB2_ROW = 4
 W4_ROW = 8
+PASS1_ROW = 16
+G1_ROW = 4
 
 
 def tile_list_volleyball_rally_commentary_kernel(
@@ -32,7 +34,7 @@ def tile_list_volleyball_rally_commentary_kernel(
     nc = tc.nc
     with ExitStack() as ctx:
         keep = ctx.enter_context(tc.tile_pool(name="keep", bufs=1))
-        ring = ctx.enter_context(tc.tile_pool(name="ring", bufs=5))
+        ring = ctx.enter_context(tc.tile_pool(name="ring", bufs=4))
         psum = ctx.enter_context(tc.psum_pool(name="psum", bufs=8))
 
         def held(shape, dtype, name):
@@ -44,7 +46,7 @@ def tile_list_volleyball_rally_commentary_kernel(
         list1 = held([P, S // 16], U16, "list1")
         list2 = held([P, S // 16], U16, "list2")
         list3 = held([P, S // 16], U16, "list3")
-        t1w = [staged([P, T1], U32, "t1w0", "t1w0"), held([P, T1], U32, "t1w1")]
+        t1w = [staged([P, T1], U32, f"t1w{a}", f"t1w{a}") for a in range(2)]
         t2w = held([P, T2], U32, "t2w")
         t3w = held([P, T3], U16, "t3w")
         t1s = held([P, T1], U8, "t1s")
@@ -54,76 +56,62 @@ def tile_list_volleyball_rally_commentary_kernel(
         w1w = held([P, 2, 2 * H], U8, "w1w")
         w1s = held([P, 2, H], U8, "w1s")
         w4w = held([P, 2, N], U32, "w4w")
-        w4s = held([P, N], U8, "w4s")
-        w2raw = [held([P, 4, 256], F32, f"w2raw{c}") for c in range(4)]
+        w4s = held([P, 2, N], U8, "w4s")
+        w2raw = [held([P, 4, 512], F32, f"w2raw{b}") for b in range(2)]
         w5raw = held([P, 4, N], F32, "w5raw")
-        w3raw = [held([P, 4, N], F32, f"w3raw{b}") for b in range(2)]
+        w3raw = [staged([P, 4, N], F32, f"w3raw{b}", f"w3raw{b}") for b in range(2)]
+        g2rows = held([P, 512], F32, "g2rows")
         g1rows = held([P, 2 * P], F32, "g1rows")
-        g1c = held([P, 2, 4], F32, "g1c")
-        g2c = held([P, 2, 4], F32, "g2c")
         ident = held([P, P], F32, "ident")
-        zero_in = held([P, 1], F32, "zero_in")
-        zero = held([P, 1], F32, "zero")
 
-        nc.vector.memset(zero_in[:], 0.0)
-        nc.scalar.activation(zero[:], zero_in[:], ACT.Tanh)
-        nc.gpsimd.memset(t2s[:].bitcast(I32), 0)
+        nc.vector.memset(t2s[:].bitcast(I32), 0)
         nc.vector.memset(t1s[:].bitcast(I32), 0)
-        nc.gpsimd.memset(t3s[:].bitcast(I32), 0)
-        nc.gpsimd.memset(g1rows[:], 0.0)
-        make_identity(nc, ident[:])
-        nc.vector.memset(w1s[:].bitcast(I32), 0)
-        nc.vector.memset(w4s[:].bitcast(I32), 0)
-        nc.vector.memset(v1s_second[:].bitcast(I32), 0)
 
         def load_rows(queue, plane, scales, row0):
-            rows = 4 * scales.shape[0]
             for quad in range(4):
                 queue.dma_start(
-                    plane[32 * quad + row0 : 32 * quad + row0 + rows, :].bitcast(I32),
-                    scales[:, 4 * quad : 4 * quad + 4, :].bitcast(I32),
+                    plane[32 * quad + row0 : 32 * quad + row0 + 4, :].bitcast(I32),
+                    scales[0, 4 * quad : 4 * quad + 4, :].bitcast(I32),
                 )
 
-        w2v = w2.rearrange("(p j) c -> p j c", j=4)
-
-        def load_w2(c):
-            nc.sync.dma_start(w2raw[c][:], w2v[:, :, 256 * c : 256 * (c + 1)])
+        def load_rows_two_passes(plane, scales, row0):
+            for quad in range(4):
+                nc.sync.dma_start(
+                    plane[32 * quad + row0 : 32 * quad + row0 + 4, :, :].bitcast(I32),
+                    scales[:, 4 * quad : 4 * quad + 4, :].rearrange("a r c -> r a c").bitcast(I32),
+                )
 
         def load_words(dst, words):
             nc.sync.dma_start(dst.bitcast(I32), words.rearrange("p c i -> p (c i)").bitcast(I32))
 
-        nc.sync.dma_start(list2[:], offs2)
-        load_rows(nc.sync, t2s, tab2_scales, TAB2_ROW)
-        load_w2(0)
-        nc.sync.dma_start(list1[:], offs)
-        load_rows(nc.sync, t1s, tab_scales, 0)
-        load_w2(1)
-        load_rows(nc.sync, t3s, tab3_scales, 0)
-        load_w2(2)
-        nc.sync.dma_start(list3[:], offs3)
-        nc.sync.dma_start(t3w[:].bitcast(I32), tab3_words[0].bitcast(I32))
-        load_w2(3)
-        load_words(t2w[:], tab2_words[0])
-        load_words(t1w[0][:], tab_words[0])
-        nc.sync.dma_start(
-            g1rows[0:4, :].rearrange("t (x i) -> t x i", i=8), g1.rearrange("(x t i) -> t x i", t=4, i=8)
-        )
-        load_words(t1w[1][:], tab_words[1])
-        nc.sync.dma_start(w1w[:].bitcast(I32), w1_words.rearrange("a p c -> p a c").bitcast(I32))
-        nc.sync.dma_start(g2c[:], g2.rearrange("(b p t) -> p b t", b=2, t=4))
-        nc.sync.dma_start(w5raw[:], w5.rearrange("(p j) n -> p j n", j=4))
-        nc.sync.dma_start(w4w[:].bitcast(I32), w4_words.rearrange("a p c i -> p a (c i)").bitcast(I32))
-        load_rows(nc.sync, w4s, w4_scales, W4_ROW)
-        for b in range(2):
-            rows = w3[512 * b : 512 * (b + 1), :].rearrange("(q t i) n -> t q i n", t=4, i=8)
-            for t in range(4):
-                nc.sync.dma_start(w3raw[b][:, t, :], rows[t])
+        w2v = w2.rearrange("(p j) c -> p j c", j=4)
 
-        for quad in range(4):
-            nc.gpsimd.dma_start(
-                w1s[32 * quad : 32 * quad + 4, :, :].bitcast(I32),
-                w1_scales[:, 4 * quad : 4 * quad + 4, :].rearrange("a r c -> r a c").bitcast(I32),
+        nc.gpsimd.memset(g2rows[:], 0.0)
+        nc.gpsimd.memset(g1rows[:], 0.0)
+        make_identity(nc, ident[:])
+        nc.gpsimd.memset(t3s[:].bitcast(I32), 0)
+        nc.gpsimd.memset(v1s_second[:].bitcast(I32), 0)
+        nc.gpsimd.memset(w1s[:].bitcast(I32), 0)
+        nc.gpsimd.memset(w4s[:].bitcast(I32), 0)
+
+        nc.sync.dma_start(list2[:], offs2)
+        nc.sync.dma_start(w2raw[0][:], w2v[:, :, 0:512])
+        load_rows(nc.sync, t2s, tab2_scales, TAB2_ROW)
+        nc.sync.dma_start(list1[:], offs)
+        load_words(t2w[:], tab2_words[0])
+        nc.sync.dma_start(g2rows[0:2, :], g2.rearrange("(b c) -> b c", b=2))
+        nc.sync.dma_start(
+            g1rows[G1_ROW : G1_ROW + 4, :].rearrange("t (x i) -> t x i", i=8),
+            g1.rearrange("(x t i) -> t x i", t=4, i=8),
+        )
+        for r in range(4):
+            nc.sync.dma_start(
+                t1s[r:P:PASS1_ROW, :].bitcast(I32),
+                tab_scales.rearrange("a (q r) c -> r q a c", r=4)[r].bitcast(I32),
             )
+        load_words(t1w[0][:], tab_words[0])
+        nc.sync.dma_start(w2raw[1][:], w2v[:, :, 512:1024])
+        nc.sync.dma_start(w1w[:].bitcast(I32), w1_words.rearrange("a p c -> p a c").bitcast(I32))
 
         def gather(dtype, window, offsets, name):
             picked = held([P, S], dtype, name)
@@ -138,10 +126,16 @@ def tile_list_volleyball_rally_commentary_kernel(
 
         w2g = [held([P, 2048], BF16, f"w2g{b}") for b in range(2)]
 
-        def cast_w2(c):
-            b, half = divmod(c, 2)
+        def sort_w2(b, half):
             dst = w2g[b][:].rearrange("p (t m j) -> p m j t", t=4, j=4)[:, 64 * half : 64 * (half + 1)]
-            nc.scalar.copy(dst, w2raw[c][:].rearrange("p j (m t) -> p m j t", t=4))
+            src = w2raw[b][:, :, 256 * half : 256 * (half + 1)].rearrange("p j (m t) -> p m j t", t=4)
+            return dst, src
+
+        def pool_cast(grouped, raw, lo, hi, sign):
+            nc.gpsimd.tensor_scalar(
+                grouped[:, 4 * lo : 4 * hi].rearrange("p (c j) -> p c j", j=4),
+                raw[:, :, lo:hi].rearrange("p j c -> p c j"), sign, 0.0, ALU.mult, ALU.add,
+            )
 
         def weave(grouped, raw, lo, hi):
             dst = grouped[:, 4 * lo : 4 * hi].rearrange("p (c i j) -> p c j i", i=4, j=4)
@@ -156,8 +150,7 @@ def tile_list_volleyball_rally_commentary_kernel(
                 for t in range(4):
                     products(bank[:, t, :], b, t, cols)
                 nc.scalar.activation(
-                    th[:, u, :].rearrange("p (s t) -> p s t", t=4), bank[:].rearrange("p t s -> p s t"),
-                    ACT.Tanh, bias=zero[:],
+                    th[:, u, :].rearrange("p (s t) -> p s t", t=4), bank[:].rearrange("p t s -> p s t"), ACT.Tanh
                 )
             nc.vector.tensor_tensor(
                 grouped[:, 1024 * pair : 1024 * (pair + 1)].rearrange("p (s t) -> p s t", t=4),
@@ -167,18 +160,36 @@ def tile_list_volleyball_rally_commentary_kernel(
             )
 
         v2s = gather(U8, t2s[:], list2, "v2s")
-        cast_w2(0)
-        cast_w2(1)
-        v1s_both = gather(U8, t1s[:], list1, "v1s_both")
-        nc.gpsimd.dma_start(v1s_second[0:100, :].bitcast(I32), v1s_both[4:104, :].bitcast(I32))
-        v1s = [v1s_both, v1s_second]
+        nc.scalar.copy(*sort_w2(0, 0))
+        nc.vector.tensor_copy(*sort_w2(0, 1))
         w2q = [quantise(w2g[0], "w2q0")]
-        cast_w2(2)
-        cast_w2(3)
-        v3w = gather(U16, t3w[:], list3, "v3w")
-        v3s = gather(U8, t3s[:], list3, "v3s")
-        w2q.append(quantise(w2g[1], "w2q1"))
         v2w = gather(U32, t2w[:], list2, "v2w")
+        v1s_both = gather(U8, t1s[:], list1, "v1s_both")
+        nc.sync.dma_start(
+            v1s_second[0 : P - PASS1_ROW, :].bitcast(I32), v1s_both[PASS1_ROW:P, :].bitcast(I32)
+        )
+        load_rows_two_passes(w1s, w1_scales, 0)
+        load_words(t1w[1][:], tab_words[1])
+        nc.sync.dma_start(list3[:], offs3)
+        nc.sync.dma_start(t3w[:].bitcast(I32), tab3_words[0].bitcast(I32))
+        load_rows(nc.sync, t3s, tab3_scales, 0)
+        nc.sync.dma_start(w5raw[:], w5.rearrange("(p j) n -> p j n", j=4))
+        nc.sync.dma_start(w4w[:].bitcast(I32), w4_words.rearrange("a p c i -> p a (c i)").bitcast(I32))
+        load_rows_two_passes(w4s, w4_scales, W4_ROW)
+        for b in range(2):
+            rows = w3[512 * b : 512 * (b + 1), :].rearrange("(q t i) n -> t q i n", t=4, i=8)
+            for t in range(4):
+                nc.sync.dma_start(w3raw[b][:, t, :], rows[t])
+
+        v1s = [v1s_both, v1s_second]
+
+        gains = psum.tile([P, 4, P], F32, name="gains", tag="bank")
+        for t in range(4):
+            nc.tensor.matmul(gains[:, t, :], g2rows[:, t:512:4], ident[:], is_transpose=True, start=(t == 0), stop=False)
+        for b in range(2):
+            nc.tensor.matmul(
+                gains[:, b, :], g1rows[:, P * b : P * (b + 1)], ident[:], is_transpose=True, start=False, stop=(b == 1)
+            )
 
         def products2(acc, b, t, cols):
             codes, plane = w2q[b]
@@ -188,37 +199,32 @@ def tile_list_volleyball_rally_commentary_kernel(
                 rhs=v2w[:, cols].bitcast(FP8X4), rhs_scale=v2s[TAB2_ROW:P, cols], start=True, stop=True,
             )
 
-        h2g = [held([P, 2048], BF16, f"h2g{b}") for b in range(2)]
-        h1g = [held([P, 2048], BF16, f"h1g{b}") for b in range(2)]
         v1w = [gather(U32, t1w[0][:], list1, "v1w0")]
+        h2g = [staged([P, 2048], BF16, "h2g0", "t1w0")]
+        hidden(0, 0, products2, gains[:, :, 0], h2g[0])
+        hidden(0, 1, products2, gains[:, :, 0], h2g[0])
+        nc.scalar.copy(*sort_w2(1, 0))
+        nc.vector.tensor_copy(*sort_w2(1, 1))
+        w2q.append(quantise(w2g[1], "w2q1"))
         w1ws = held([P, 4, 4, 256], U8, "w1ws")
-        w1ss = staged([P, 4, 4, P], U8, "w1ss", "t1w0")
-        nc.vector.tensor_copy(
-            w1ss[:].bitcast(I32).rearrange("p x t (q w) -> p x t q w", w=2),
-            w1s[:].bitcast(I32).rearrange("p a (b q t w) -> p (a b) t q w", b=2, t=4, w=2),
-        )
-        nc.vector.tensor_copy(
+        w1ss = held([P, 4, 4, P], U8, "w1ss")
+        nc.gpsimd.tensor_copy(
             w1ws[:].bitcast(I32).rearrange("p x t (q w) -> p x t q w", w=4),
             w1w[:].bitcast(I32).rearrange("p a (b q t w) -> p (a b) t q w", b=2, t=4, w=4),
         )
+        nc.gpsimd.tensor_copy(
+            w1ss[:].bitcast(I32).rearrange("p x t (q w) -> p x t q w", w=2),
+            w1s[:].bitcast(I32).rearrange("p a (b q t w) -> p (a b) t q w", b=2, t=4, w=2),
+        )
         v1w.append(gather(U32, t1w[1][:], list1, "v1w1"))
-        hidden(0, 0, products2, g2c[:, 0, :], h2g[0])
-        hidden(0, 1, products2, g2c[:, 0, :], h2g[0])
+        h2g.append(staged([P, 2048], BF16, "h2g1", "t1w1"))
+        hidden(1, 0, products2, gains[:, :, 1], h2g[1])
         h2q = [quantise(h2g[0], "h2q0")]
-        hidden(1, 0, products2, g2c[:, 1, :], h2g[1])
-        hidden(1, 1, products2, g2c[:, 1, :], h2g[1])
-
-        gbank = psum.tile([P, 2, P], F32, name="gbank", tag="bank")
-        for b in range(2):
-            nc.tensor.transpose(gbank[:, b, :], g1rows[:, P * b : P * (b + 1)], ident[:])
-        nc.scalar.copy(g1c[:], gbank[:, :, 0:4])
+        hidden(1, 1, products2, gains[:, :, 1], h2g[1])
         h2q.append(quantise(h2g[1], "h2q1"))
 
-        w5g = held([P, 2048], BF16, "w5g")
-        for half in range(2):
-            dst, src = weave(w5g, w5raw, 256 * half, 256 * (half + 1))
-            nc.scalar.activation(dst, src, ACT.Copy, scale=-1.0)
-        w5q = quantise(w5g, "w5q")
+        v3w = gather(U16, t3w[:], list3, "v3w")
+        v3s = gather(U8, t3s[:], list3, "v3s")
 
         def products1(acc, b, t, cols):
             for a in range(2):
@@ -227,44 +233,44 @@ def tile_list_volleyball_rally_commentary_kernel(
                     rhs=v1w[a][:, cols].bitcast(FP8X4), rhs_scale=v1s[a][:, cols], start=(a == 0), stop=(a == 1),
                 )
 
+        w5g = staged([P, 2048], BF16, "w5g", "w5g")
+        for half in range(2):
+            pool_cast(w5g, w5raw, 256 * half, 256 * (half + 1), -1.0)
+        w5q = quantise(w5g, "w5q")
+        h1g = [staged([P, 2048], BF16, "h1g0", "w5g"), held([P, 2048], BF16, "h1g1")]
+        hidden(0, 0, products1, gains[:, 0, G1_ROW : G1_ROW + 4], h1g[0])
+        hidden(0, 1, products1, gains[:, 0, G1_ROW : G1_ROW + 4], h1g[0])
+        hidden(1, 0, products1, gains[:, 1, G1_ROW : G1_ROW + 4], h1g[1])
+        h1q = [quantise(h1g[0], "h1q0")]
+        hidden(1, 1, products1, gains[:, 1, G1_ROW : G1_ROW + 4], h1g[1])
+
+        h1q.append(quantise(h1g[1], "h1q1"))
+
         def arena(acc, m):
             nc.tensor.matmul_mx(
                 out=acc, lhsT=w5q[0][:, m].bitcast(FP8X4), lhsT_scale=w5q[1][:, m],
                 rhs=v3w[:].bitcast(FP4X4), rhs_scale=v3s[:], start=True, stop=False,
             )
 
-        hidden(0, 0, products1, g1c[:, 0, :], h1g[0])
-        hidden(0, 1, products1, g1c[:, 0, :], h1g[0])
-        h1q = [quantise(h1g[0], "h1q0")]
-        hidden(1, 0, products1, g1c[:, 1, :], h1g[1])
-        hidden(1, 1, products1, g1c[:, 1, :], h1g[1])
-
         w3g = [held([P, 2048], BF16, f"w3g{b}") for b in range(2)]
-        for half in range(2):
-            dst, src = weave(w3g[0], w3raw[0], 256 * half, 256 * (half + 1))
-            nc.scalar.copy(dst, src)
+        pool_cast(w3g[0], w3raw[0], 0, 256, 1.0)
+        nc.scalar.copy(*weave(w3g[0], w3raw[0], 256, 512))
         w3q = [quantise(w3g[0], "w3q0")]
-        h1q.append(quantise(h1g[1], "h1q1"))
-        dst, src = weave(w3g[1], w3raw[1], 0, 256)
-        nc.scalar.copy(dst, src)
-        dst, src = weave(w3g[1], w3raw[1], 256, 512)
-        nc.vector.tensor_copy(dst, src)
+        for half in range(2):
+            pool_cast(w3g[1], w3raw[1], 256 * half, 256 * (half + 1), 1.0)
         w3q.append(quantise(w3g[1], "w3q1"))
 
-        y2 = [held([P, S], F32, f"y2_{n}") for n in range(4)]
-        y2banks = []
+        y2 = staged([P, 4, S], F32, "y2", "w3raw0")
         for n in range(4):
             m = slice(128 * n, 128 * (n + 1))
             acc = psum.tile([P, S], F32, name="acc", tag="bank")
             arena(acc[:], m)
             for a in range(2):
                 nc.tensor.matmul_mx(
-                    out=acc[:], lhsT=w4w[:, a, m].bitcast(FP8X4), lhsT_scale=w4s[W4_ROW + 4 * a : P, m],
+                    out=acc[:], lhsT=w4w[:, a, m].bitcast(FP8X4), lhsT_scale=w4s[W4_ROW:P, a, m],
                     rhs=h2q[a][0][:].bitcast(FP8X4), rhs_scale=h2q[a][1][:], start=False, stop=(a == 1),
                 )
-            y2banks.append(acc)
-        for n in range(4):
-            nc.scalar.copy(y2[n][:], y2banks[n][:])
+            nc.scalar.copy(y2[:, n, :], acc[:])
 
         y1banks = []
         for n in range(4):
@@ -281,5 +287,5 @@ def tile_list_volleyball_rally_commentary_kernel(
                 )
         for n in range(4):
             res = held([P, S], F32, f"res{n}")
-            nc.vector.tensor_tensor(res[:], y1banks[n][:], y2[n][:], ALU.max)
+            nc.vector.tensor_tensor(res[:], y1banks[n][:], y2[:, n, :], ALU.max)
             nc.sync.dma_start(out[128 * n : 128 * (n + 1), :], res[:])

@@ -58,7 +58,7 @@ def tile_list_volleyball_rally_commentary_kernel(
         w4w = held([P, 2, N], U32, "w4w")
         w4s = held([P, 2, N], U8, "w4s")
         w2raw = [held([P, 4, 512], F32, f"w2raw{b}") for b in range(2)]
-        w5raw = held([P, 4, N], F32, "w5raw")
+        w5raw = staged([P, 4, N], F32, "w5raw", "w5raw")
         w3raw = [staged([P, 4, N], F32, f"w3raw{b}", f"w3raw{b}") for b in range(2)]
         g2rows = held([P, 512], F32, "g2rows")
         g1rows = held([P, 2 * P], F32, "g1rows")
@@ -131,19 +131,14 @@ def tile_list_volleyball_rally_commentary_kernel(
             src = w2raw[b][:, :, 256 * half : 256 * (half + 1)].rearrange("p j (m t) -> p m j t", t=4)
             return dst, src
 
-        def pool_cast(grouped, raw, lo, hi, sign):
-            nc.gpsimd.tensor_scalar(
-                grouped[:, 4 * lo : 4 * hi].rearrange("p (c j) -> p c j", j=4),
-                raw[:, :, lo:hi].rearrange("p j c -> p c j"), sign, 0.0, ALU.mult, ALU.add,
-            )
-
         def weave(grouped, raw, lo, hi):
             dst = grouped[:, 4 * lo : 4 * hi].rearrange("p (c i j) -> p c j i", i=4, j=4)
             src = raw[:, :, lo:hi].rearrange("p j (c i) -> p c j i", i=4)
             return dst, src
 
-        def hidden(b, pair, products, gain, grouped):
-            th = ring.tile([P, 2, 512], F32, name="th")
+        def hidden(b, pair, products, gain, grouped, th=None):
+            if th is None:
+                th = ring.tile([P, 2, 512], F32, name="th")
             for u in range(2):
                 cols = slice(128 * (2 * pair + u), 128 * (2 * pair + u + 1))
                 bank = psum.tile([P, 4, P], F32, name="bank", tag="bank")
@@ -154,7 +149,7 @@ def tile_list_volleyball_rally_commentary_kernel(
                 )
             nc.vector.tensor_tensor(
                 grouped[:, 1024 * pair : 1024 * (pair + 1)].rearrange("p (s t) -> p s t", t=4),
-                th[:].rearrange("p u (s t) -> p (u s) t", t=4),
+                th[:, :, :].rearrange("p u (s t) -> p (u s) t", t=4),
                 gain.unsqueeze(1).to_broadcast([P, 256, 4]),
                 ALU.mult,
             )
@@ -204,15 +199,15 @@ def tile_list_volleyball_rally_commentary_kernel(
         hidden(0, 0, products2, gains[:, :, 0], h2g[0])
         hidden(0, 1, products2, gains[:, :, 0], h2g[0])
         nc.scalar.copy(*sort_w2(1, 0))
-        nc.vector.tensor_copy(*sort_w2(1, 1))
+        nc.scalar.copy(*sort_w2(1, 1))
         w2q.append(quantise(w2g[1], "w2q1"))
         w1ws = held([P, 4, 4, 256], U8, "w1ws")
         w1ss = held([P, 4, 4, P], U8, "w1ss")
-        nc.gpsimd.tensor_copy(
+        nc.vector.tensor_copy(
             w1ws[:].bitcast(I32).rearrange("p x t (q w) -> p x t q w", w=4),
             w1w[:].bitcast(I32).rearrange("p a (b q t w) -> p (a b) t q w", b=2, t=4, w=4),
         )
-        nc.gpsimd.tensor_copy(
+        nc.vector.tensor_copy(
             w1ss[:].bitcast(I32).rearrange("p x t (q w) -> p x t q w", w=2),
             w1s[:].bitcast(I32).rearrange("p a (b q t w) -> p (a b) t q w", b=2, t=4, w=2),
         )
@@ -235,14 +230,15 @@ def tile_list_volleyball_rally_commentary_kernel(
 
         w5g = staged([P, 2048], BF16, "w5g", "w5g")
         for half in range(2):
-            pool_cast(w5g, w5raw, 256 * half, 256 * (half + 1), -1.0)
+            nc.scalar.activation(*weave(w5g, w5raw, 256 * half, 256 * (half + 1)), ACT.Copy, scale=-1.0)
         w5q = quantise(w5g, "w5q")
         h1g = [staged([P, 2048], BF16, "h1g0", "w5g"), held([P, 2048], BF16, "h1g1")]
-        hidden(0, 0, products1, gains[:, 0, G1_ROW : G1_ROW + 4], h1g[0])
-        hidden(0, 1, products1, gains[:, 0, G1_ROW : G1_ROW + 4], h1g[0])
-        hidden(1, 0, products1, gains[:, 1, G1_ROW : G1_ROW + 4], h1g[1])
+        th1 = staged([P, 4, 2, 512], F32, "th1", "w5raw")
+        hidden(0, 0, products1, gains[:, 0, G1_ROW : G1_ROW + 4], h1g[0], th1[:, 0])
+        hidden(0, 1, products1, gains[:, 0, G1_ROW : G1_ROW + 4], h1g[0], th1[:, 1])
+        hidden(1, 0, products1, gains[:, 1, G1_ROW : G1_ROW + 4], h1g[1], th1[:, 2])
         h1q = [quantise(h1g[0], "h1q0")]
-        hidden(1, 1, products1, gains[:, 1, G1_ROW : G1_ROW + 4], h1g[1])
+        hidden(1, 1, products1, gains[:, 1, G1_ROW : G1_ROW + 4], h1g[1], th1[:, 3])
 
         h1q.append(quantise(h1g[1], "h1q1"))
 
@@ -253,11 +249,10 @@ def tile_list_volleyball_rally_commentary_kernel(
             )
 
         w3g = [held([P, 2048], BF16, f"w3g{b}") for b in range(2)]
-        pool_cast(w3g[0], w3raw[0], 0, 256, 1.0)
-        nc.scalar.copy(*weave(w3g[0], w3raw[0], 256, 512))
-        w3q = [quantise(w3g[0], "w3q0")]
         for half in range(2):
-            pool_cast(w3g[1], w3raw[1], 256 * half, 256 * (half + 1), 1.0)
+            nc.scalar.copy(*weave(w3g[0], w3raw[0], 256 * half, 256 * (half + 1)))
+        w3q = [quantise(w3g[0], "w3q0")]
+        nc.vector.tensor_copy(*weave(w3g[1], w3raw[1], 0, 512))
         w3q.append(quantise(w3g[1], "w3q1"))
 
         y2 = staged([P, 4, S], F32, "y2", "w3raw0")

@@ -24,7 +24,6 @@ T1, T2, T3 = 2048, 2048, 1024
 TAB2_ROW = 4
 W4_ROW = 8
 PASS1_ROW = 16
-G1_ROW = 4
 
 
 def tile_list_volleyball_rally_commentary_kernel(
@@ -34,6 +33,7 @@ def tile_list_volleyball_rally_commentary_kernel(
     nc = tc.nc
     with ExitStack() as ctx:
         keep = ctx.enter_context(tc.tile_pool(name="keep", bufs=1))
+        second_window = ctx.enter_context(tc.tile_pool(name="second_window", bufs=1))
         ring = ctx.enter_context(tc.tile_pool(name="ring", bufs=4))
         psum = ctx.enter_context(tc.psum_pool(name="psum", bufs=8))
 
@@ -46,8 +46,11 @@ def tile_list_volleyball_rally_commentary_kernel(
         list1 = held([P, S // 16], U16, "list1")
         list2 = held([P, S // 16], U16, "list2")
         list3 = held([P, S // 16], U16, "list3")
-        t1w = [staged([P, T1], U32, f"t1w{a}", f"t1w{a}") for a in range(2)]
-        t2w = held([P, T2], U32, "t2w")
+        def after_tab(shape, dtype, name, offset):
+            return second_window.tile(shape, dtype, name=name, offset=offset, align_bytes=64)
+
+        t1w = [staged([P, T1], U32, "t1w0", "t1w0"), after_tab([P, T1], U32, "t1w1", 0)]
+        t2w = staged([P, T2], U32, "t2w", "t2w")
         t3w = held([P, T3], U16, "t3w")
         t1s = held([P, T1], U8, "t1s")
         t2s = held([P, T2], U8, "t2s")
@@ -61,24 +64,28 @@ def tile_list_volleyball_rally_commentary_kernel(
         w5raw = staged([P, 4, N], F32, "w5raw", "w5raw")
         w3raw = [staged([P, 4, N], F32, f"w3raw{b}", f"w3raw{b}") for b in range(2)]
         g2rows = held([P, 512], F32, "g2rows")
-        g1rows = held([P, 2 * P], F32, "g1rows")
+        g1rows = held([P, 512], F32, "g1rows")
         ident = held([P, P], F32, "ident")
 
-        nc.vector.memset(t2s[:].bitcast(I32), 0)
+        nc.gpsimd.memset(t2s[:].bitcast(I32), 0)
         nc.vector.memset(t1s[:].bitcast(I32), 0)
+        nc.gpsimd.memset(g2rows[:], 0.0)
+        make_identity(nc, ident[:])
+        nc.gpsimd.memset(v1s_second[:].bitcast(I32), 0)
+        nc.gpsimd.memset(t3s[:].bitcast(I32), 0)
+        nc.gpsimd.memset(g1rows[:], 0.0)
+        nc.vector.memset(w1s[:].bitcast(I32), 0)
+        nc.vector.memset(w4s[:].bitcast(I32), 0)
 
-        def load_rows(queue, plane, scales, row0):
-            for quad in range(4):
-                queue.dma_start(
-                    plane[32 * quad + row0 : 32 * quad + row0 + 4, :].bitcast(I32),
-                    scales[0, 4 * quad : 4 * quad + 4, :].bitcast(I32),
-                )
+        def load_rows(plane, scales, row0):
+            for r in range(4):
+                nc.sync.dma_start(plane[row0 + r : P : 32, :].bitcast(I32), scales[0, r:16:4, :].bitcast(I32))
 
         def load_rows_two_passes(plane, scales, row0):
-            for quad in range(4):
+            for r in range(4):
                 nc.sync.dma_start(
-                    plane[32 * quad + row0 : 32 * quad + row0 + 4, :, :].bitcast(I32),
-                    scales[:, 4 * quad : 4 * quad + 4, :].rearrange("a r c -> r a c").bitcast(I32),
+                    plane[row0 + r : P : 32, :, :].bitcast(I32),
+                    scales[:, r:16:4, :].rearrange("a q c -> q a c").bitcast(I32),
                 )
 
         def load_words(dst, words):
@@ -86,31 +93,22 @@ def tile_list_volleyball_rally_commentary_kernel(
 
         w2v = w2.rearrange("(p j) c -> p j c", j=4)
 
-        nc.gpsimd.memset(g2rows[:], 0.0)
-        nc.gpsimd.memset(g1rows[:], 0.0)
-        make_identity(nc, ident[:])
-        nc.gpsimd.memset(t3s[:].bitcast(I32), 0)
-        nc.gpsimd.memset(v1s_second[:].bitcast(I32), 0)
-        nc.gpsimd.memset(w1s[:].bitcast(I32), 0)
-        nc.gpsimd.memset(w4s[:].bitcast(I32), 0)
-
         nc.sync.dma_start(list2[:], offs2)
+        nc.sync.dma_start(list3[:], offs3)
+        nc.sync.dma_start(t3w[:].bitcast(I32), tab3_words[0].bitcast(I32))
+        load_rows(t2s, tab2_scales, TAB2_ROW)
         nc.sync.dma_start(w2raw[0][:], w2v[:, :, 0:512])
-        load_rows(nc.sync, t2s, tab2_scales, TAB2_ROW)
+        nc.sync.dma_start(w2raw[1][:], w2v[:, :, 512:1024])
         nc.sync.dma_start(list1[:], offs)
-        load_words(t2w[:], tab2_words[0])
-        nc.sync.dma_start(g2rows[0:2, :], g2.rearrange("(b c) -> b c", b=2))
-        nc.sync.dma_start(
-            g1rows[G1_ROW : G1_ROW + 4, :].rearrange("t (x i) -> t x i", i=8),
-            g1.rearrange("(x t i) -> t x i", t=4, i=8),
-        )
         for r in range(4):
             nc.sync.dma_start(
                 t1s[r:P:PASS1_ROW, :].bitcast(I32),
                 tab_scales.rearrange("a (q r) c -> r q a c", r=4)[r].bitcast(I32),
             )
+        nc.sync.dma_start(g2rows[0:2, :], g2.rearrange("(b c) -> b c", b=2))
+        load_words(t2w[:], tab2_words[0])
+        load_rows(t3s, tab3_scales, 0)
         load_words(t1w[0][:], tab_words[0])
-        nc.sync.dma_start(w2raw[1][:], w2v[:, :, 512:1024])
         nc.sync.dma_start(w1w[:].bitcast(I32), w1_words.rearrange("a p c -> p a c").bitcast(I32))
 
         def gather(dtype, window, offsets, name):
@@ -124,11 +122,11 @@ def tile_list_volleyball_rally_commentary_kernel(
             nc.vector.quantize_mx(out=codes[:].bitcast(FP8X4), scales=plane[:], in_=grouped[:])
             return codes, plane
 
-        w2g = [held([P, 2048], BF16, f"w2g{b}") for b in range(2)]
+        w2g = [staged([P, 2048], BF16, f"w2g{b}", f"w2g{b}") for b in range(2)]
 
         def sort_w2(b, half):
-            dst = w2g[b][:].rearrange("p (t m j) -> p m j t", t=4, j=4)[:, 64 * half : 64 * (half + 1)]
-            src = w2raw[b][:, :, 256 * half : 256 * (half + 1)].rearrange("p j (m t) -> p m j t", t=4)
+            dst = w2g[b][:, 1024 * half : 1024 * (half + 1)].rearrange("p (t m j) -> p m j t", t=2, j=4)
+            src = w2raw[b][:].rearrange("p j (m t) -> p m j t", t=4)[:, :, :, 2 * half : 2 * (half + 1)]
             return dst, src
 
         def weave(grouped, raw, lo, hi):
@@ -136,7 +134,7 @@ def tile_list_volleyball_rally_commentary_kernel(
             src = raw[:, :, lo:hi].rearrange("p j (c i) -> p c j i", i=4)
             return dst, src
 
-        def hidden(b, pair, products, gain, grouped, th=None):
+        def hidden(b, pair, products, gain, half, th=None):
             if th is None:
                 th = ring.tile([P, 2, 512], F32, name="th")
             for u in range(2):
@@ -148,27 +146,32 @@ def tile_list_volleyball_rally_commentary_kernel(
                     th[:, u, :].rearrange("p (s t) -> p s t", t=4), bank[:].rearrange("p t s -> p s t"), ACT.Tanh
                 )
             nc.vector.tensor_tensor(
-                grouped[:, 1024 * pair : 1024 * (pair + 1)].rearrange("p (s t) -> p s t", t=4),
+                half.rearrange("p (s t) -> p s t", t=4),
                 th[:, :, :].rearrange("p u (s t) -> p (u s) t", t=4),
                 gain.unsqueeze(1).to_broadcast([P, 256, 4]),
                 ALU.mult,
             )
 
+        v3w = gather(U16, t3w[:], list3, "v3w")
         v2s = gather(U8, t2s[:], list2, "v2s")
         nc.scalar.copy(*sort_w2(0, 0))
         nc.vector.tensor_copy(*sort_w2(0, 1))
         w2q = [quantise(w2g[0], "w2q0")]
-        v2w = gather(U32, t2w[:], list2, "v2w")
+        for half in range(2):
+            nc.scalar.copy(*sort_w2(1, half))
         v1s_both = gather(U8, t1s[:], list1, "v1s_both")
+        v2w = gather(U32, t2w[:], list2, "v2w")
+        w2q.append((staged([P, 512], U32, "w2q1_codes", "t2w"), held([P, 512], U8, "w2q1_plane")))
+        nc.vector.quantize_mx(out=w2q[1][0][:].bitcast(FP8X4), scales=w2q[1][1][:], in_=w2g[1][:])
+        v3s = gather(U8, t3s[:], list3, "v3s")
         nc.sync.dma_start(
             v1s_second[0 : P - PASS1_ROW, :].bitcast(I32), v1s_both[PASS1_ROW:P, :].bitcast(I32)
         )
+        v1s = [v1s_both, v1s_second]
         load_rows_two_passes(w1s, w1_scales, 0)
-        load_words(t1w[1][:], tab_words[1])
-        nc.sync.dma_start(list3[:], offs3)
-        nc.sync.dma_start(t3w[:].bitcast(I32), tab3_words[0].bitcast(I32))
-        load_rows(nc.sync, t3s, tab3_scales, 0)
         nc.sync.dma_start(w5raw[:], w5.rearrange("(p j) n -> p j n", j=4))
+        nc.sync.dma_start(g1rows[0:2, :], g1.rearrange("(b c) -> b c", b=2))
+        load_words(t1w[1][:], tab_words[1])
         nc.sync.dma_start(w4w[:].bitcast(I32), w4_words.rearrange("a p c i -> p a (c i)").bitcast(I32))
         load_rows_two_passes(w4s, w4_scales, W4_ROW)
         for b in range(2):
@@ -176,15 +179,9 @@ def tile_list_volleyball_rally_commentary_kernel(
             for t in range(4):
                 nc.sync.dma_start(w3raw[b][:, t, :], rows[t])
 
-        v1s = [v1s_both, v1s_second]
-
-        gains = psum.tile([P, 4, P], F32, name="gains", tag="bank")
+        gains2 = psum.tile([P, 4, P], F32, name="gains2", tag="bank")
         for t in range(4):
-            nc.tensor.matmul(gains[:, t, :], g2rows[:, t:512:4], ident[:], is_transpose=True, start=(t == 0), stop=False)
-        for b in range(2):
-            nc.tensor.matmul(
-                gains[:, b, :], g1rows[:, P * b : P * (b + 1)], ident[:], is_transpose=True, start=False, stop=(b == 1)
-            )
+            nc.tensor.transpose(gains2[:, t, :], g2rows[:, t:512:4], ident[:])
 
         def products2(acc, b, t, cols):
             codes, plane = w2q[b]
@@ -196,30 +193,43 @@ def tile_list_volleyball_rally_commentary_kernel(
 
         v1w = [gather(U32, t1w[0][:], list1, "v1w0")]
         h2g = [staged([P, 2048], BF16, "h2g0", "t1w0")]
-        hidden(0, 0, products2, gains[:, :, 0], h2g[0])
-        hidden(0, 1, products2, gains[:, :, 0], h2g[0])
-        nc.scalar.copy(*sort_w2(1, 0))
-        nc.scalar.copy(*sort_w2(1, 1))
-        w2q.append(quantise(w2g[1], "w2q1"))
+        hidden(0, 0, products2, gains2[:, :, 0], h2g[0][:, 0:1024])
+        hidden(0, 1, products2, gains2[:, :, 0], h2g[0][:, 1024:2048])
+        h2q = []
         w1ws = held([P, 4, 4, 256], U8, "w1ws")
-        w1ss = held([P, 4, 4, P], U8, "w1ss")
         nc.vector.tensor_copy(
             w1ws[:].bitcast(I32).rearrange("p x t (q w) -> p x t q w", w=4),
             w1w[:].bitcast(I32).rearrange("p a (b q t w) -> p (a b) t q w", b=2, t=4, w=4),
         )
+        h2q.append(quantise(h2g[0], "h2q0"))
+        w1ss = held([P, 4, 4, P], U8, "w1ss")
         nc.vector.tensor_copy(
             w1ss[:].bitcast(I32).rearrange("p x t (q w) -> p x t q w", w=2),
             w1s[:].bitcast(I32).rearrange("p a (b q t w) -> p (a b) t q w", b=2, t=4, w=2),
         )
+        h2g1 = [held([P, 1024], BF16, "h2g1_first")]
+        h2q.append((held([P, 512], U32, "h2q1_codes"), held([P, 512], U8, "h2q1_plane")))
+        hidden(1, 0, products2, gains2[:, :, 1], h2g1[0][:])
         v1w.append(gather(U32, t1w[1][:], list1, "v1w1"))
-        h2g.append(staged([P, 2048], BF16, "h2g1", "t1w1"))
-        hidden(1, 0, products2, gains[:, :, 1], h2g[1])
-        h2q = [quantise(h2g[0], "h2q0")]
-        hidden(1, 1, products2, gains[:, :, 1], h2g[1])
-        h2q.append(quantise(h2g[1], "h2q1"))
+        h2g1.append(after_tab([P, 1024], BF16, "h2g1_second", 0))
+        hidden(1, 1, products2, gains2[:, :, 1], h2g1[1][:])
+        w5g = staged([P, 2048], BF16, "w5g", "w5g")
+        for half in range(2):
+            nc.scalar.activation(*weave(w5g, w5raw, 256 * half, 256 * (half + 1)), ACT.Copy, scale=-1.0)
+        w5q = (after_tab([P, 512], U32, "w5q_codes", 2048), held([P, 512], U8, "w5q_plane"))
+        nc.vector.quantize_mx(out=w5q[0][:].bitcast(FP8X4), scales=w5q[1][:], in_=w5g[:])
+        for half in range(2):
+            cols = slice(256 * half, 256 * (half + 1))
+            nc.vector.quantize_mx(out=h2q[1][0][:, cols].bitcast(FP8X4), scales=h2q[1][1][:, cols], in_=h2g1[half][:])
+        late = staged([P, 4, 2, 512], F32, "late", "w5raw")
 
-        v3w = gather(U16, t3w[:], list3, "v3w")
-        v3s = gather(U8, t3s[:], list3, "v3s")
+        g1sorted = held([P, 4, P], F32, "g1sorted")
+        nc.scalar.copy(
+            g1sorted[:].rearrange("p t (q i) -> p t q i", i=8), g1rows[:].rearrange("p (q t i) -> p t q i", t=4, i=8)
+        )
+        gains1 = psum.tile([P, 4, P], F32, name="gains1", tag="bank")
+        for t in range(4):
+            nc.tensor.transpose(gains1[:, t, :], g1sorted[:, t, :], ident[:])
 
         def products1(acc, b, t, cols):
             for a in range(2):
@@ -228,17 +238,19 @@ def tile_list_volleyball_rally_commentary_kernel(
                     rhs=v1w[a][:, cols].bitcast(FP8X4), rhs_scale=v1s[a][:, cols], start=(a == 0), stop=(a == 1),
                 )
 
-        w5g = staged([P, 2048], BF16, "w5g", "w5g")
-        for half in range(2):
-            nc.scalar.activation(*weave(w5g, w5raw, 256 * half, 256 * (half + 1)), ACT.Copy, scale=-1.0)
-        w5q = quantise(w5g, "w5q")
-        h1g = [staged([P, 2048], BF16, "h1g0", "w5g"), held([P, 2048], BF16, "h1g1")]
-        th1 = staged([P, 4, 2, 512], F32, "th1", "w5raw")
-        hidden(0, 0, products1, gains[:, 0, G1_ROW : G1_ROW + 4], h1g[0], th1[:, 0])
-        hidden(0, 1, products1, gains[:, 0, G1_ROW : G1_ROW + 4], h1g[0], th1[:, 1])
-        hidden(1, 0, products1, gains[:, 1, G1_ROW : G1_ROW + 4], h1g[1], th1[:, 2])
+        h1g = [staged([P, 2048], BF16, "h1g0", "w5g")]
+        hidden(0, 0, products1, gains1[:, :, 0], h1g[0][:, 0:1024], late[:, 0])
+        hidden(0, 1, products1, gains1[:, :, 0], h1g[0][:, 1024:2048], late[:, 1])
+        w3g = [held([P, 2048], BF16, f"w3g{b}") for b in range(2)]
+        nc.vector.tensor_copy(*weave(w3g[0], w3raw[0], 0, 512))
         h1q = [quantise(h1g[0], "h1q0")]
-        hidden(1, 1, products1, gains[:, 1, G1_ROW : G1_ROW + 4], h1g[1], th1[:, 3])
+        w3q = [quantise(w3g[0], "w3q0")]
+        h1g.append(staged([P, 2048], BF16, "h1g1", "w3raw0"))
+        hidden(1, 0, products1, gains1[:, :, 1], h1g[1][:, 0:1024], late[:, 2])
+        hidden(1, 1, products1, gains1[:, :, 1], h1g[1][:, 1024:2048], late[:, 3])
+        for half in range(2):
+            nc.scalar.copy(*weave(w3g[1], w3raw[1], 256 * half, 256 * (half + 1)))
+        w3q.append(quantise(w3g[1], "w3q1"))
 
         h1q.append(quantise(h1g[1], "h1q1"))
 
@@ -248,14 +260,8 @@ def tile_list_volleyball_rally_commentary_kernel(
                 rhs=v3w[:].bitcast(FP4X4), rhs_scale=v3s[:], start=True, stop=False,
             )
 
-        w3g = [held([P, 2048], BF16, f"w3g{b}") for b in range(2)]
-        for half in range(2):
-            nc.scalar.copy(*weave(w3g[0], w3raw[0], 256 * half, 256 * (half + 1)))
-        w3q = [quantise(w3g[0], "w3q0")]
-        nc.vector.tensor_copy(*weave(w3g[1], w3raw[1], 0, 512))
-        w3q.append(quantise(w3g[1], "w3q1"))
 
-        y2 = staged([P, 4, S], F32, "y2", "w3raw0")
+        y2 = staged([P, 4, S], F32, "y2", "w3raw1")
         for n in range(4):
             m = slice(128 * n, 128 * (n + 1))
             acc = psum.tile([P, S], F32, name="acc", tag="bank")

@@ -33,8 +33,8 @@ def tile_list_volleyball_rally_commentary_kernel(
     nc = tc.nc
     with ExitStack() as ctx:
         keep = ctx.enter_context(tc.tile_pool(name="keep", bufs=1))
-        second_window = ctx.enter_context(tc.tile_pool(name="second_window", bufs=1))
-        ring = ctx.enter_context(tc.tile_pool(name="ring", bufs=4))
+        line = ctx.enter_context(tc.tile_pool(name="line", bufs=36))
+        ring = ctx.enter_context(tc.tile_pool(name="ring", bufs=6))
         psum = ctx.enter_context(tc.psum_pool(name="psum", bufs=8))
 
         def held(shape, dtype, name):
@@ -43,18 +43,18 @@ def tile_list_volleyball_rally_commentary_kernel(
         def staged(shape, dtype, name, tag):
             return keep.tile(shape, dtype, name=name, tag=tag, align_bytes=64)
 
+        def lined(shape, dtype, name):
+            return line.tile(shape, dtype, name=name, tag="line", align_bytes=64)
+
         list1 = held([P, S // 16], U16, "list1")
         list2 = held([P, S // 16], U16, "list2")
         list3 = held([P, S // 16], U16, "list3")
-        def after_tab(shape, dtype, name, offset):
-            return second_window.tile(shape, dtype, name=name, offset=offset, align_bytes=64)
-
-        t1w = [staged([P, T1], U32, "t1w0", "t1w0"), after_tab([P, T1], U32, "t1w1", 0)]
-        t2w = staged([P, T2], U32, "t2w", "t2w")
+        t1w = [staged([P, T1], U32, "t1w0", "t1w0"), held([P, T1], U32, "t1w1")]
+        t2w = held([P, T2], U32, "t2w")
         t3w = held([P, T3], U16, "t3w")
         t1s = held([P, T1], U8, "t1s")
         t2s = held([P, T2], U8, "t2s")
-        t3s = held([P, T3], U8, "t3s")
+        t3s = staged([P, T3], U8, "t3s", "t3s")
         v1s_second = held([P, S], U8, "v1s_second")
         w1w = held([P, 2, 2 * H], U8, "w1w")
         w1s = held([P, 2, H], U8, "w1s")
@@ -91,6 +91,11 @@ def tile_list_volleyball_rally_commentary_kernel(
         def load_words(dst, words):
             nc.sync.dma_start(dst.bitcast(I32), words.rearrange("p c i -> p (c i)").bitcast(I32))
 
+        def load_w3(b):
+            rows = w3[512 * b : 512 * (b + 1), :].rearrange("(q t i) n -> t q i n", t=4, i=8)
+            for t in range(4):
+                nc.sync.dma_start(w3raw[b][:, t, :], rows[t])
+
         w2v = w2.rearrange("(p j) c -> p j c", j=4)
 
         nc.sync.dma_start(list2[:], offs2)
@@ -98,45 +103,46 @@ def tile_list_volleyball_rally_commentary_kernel(
         nc.sync.dma_start(t3w[:].bitcast(I32), tab3_words[0].bitcast(I32))
         load_rows(t2s, tab2_scales, TAB2_ROW)
         nc.sync.dma_start(w2raw[0][:], w2v[:, :, 0:512])
-        nc.sync.dma_start(w2raw[1][:], w2v[:, :, 512:1024])
+        nc.sync.dma_start(g2rows[0:2, :], g2.rearrange("(b c) -> b c", b=2))
+        nc.sync.dma_start(g1rows[2:4, :], g1.rearrange("(b c) -> b c", b=2))
+        load_rows(t3s, tab3_scales, 0)
+        load_words(t2w[:], tab2_words[0])
         nc.sync.dma_start(list1[:], offs)
         for r in range(4):
             nc.sync.dma_start(
                 t1s[r:P:PASS1_ROW, :].bitcast(I32),
                 tab_scales.rearrange("a (q r) c -> r q a c", r=4)[r].bitcast(I32),
             )
-        nc.sync.dma_start(g2rows[0:2, :], g2.rearrange("(b c) -> b c", b=2))
-        load_words(t2w[:], tab2_words[0])
-        load_rows(t3s, tab3_scales, 0)
+        nc.sync.dma_start(w2raw[1][:], w2v[:, :, 512:1024])
         load_words(t1w[0][:], tab_words[0])
-        nc.sync.dma_start(w1w[:].bitcast(I32), w1_words.rearrange("a p c -> p a c").bitcast(I32))
 
         def gather(dtype, window, offsets, name):
-            picked = held([P, S], dtype, name)
+            picked = lined([P, S], dtype, name)
             nc.vector.tensor_copy(picked[:], window.indirect(offsets[:]))
             return picked
 
-        def quantise(grouped, name):
-            codes = held([P, 512], U32, name + "_codes")
-            plane = held([P, 512], U8, name + "_plane")
-            nc.vector.quantize_mx(out=codes[:].bitcast(FP8X4), scales=plane[:], in_=grouped[:])
-            return codes, plane
+        def operand(name):
+            return lined([P, 512], U32, name + "_codes"), held([P, 512], U8, name + "_plane")
 
-        w2g = [staged([P, 2048], BF16, f"w2g{b}", f"w2g{b}") for b in range(2)]
+        def quantise(dst, half, grouped):
+            cols = slice(256 * half, 256 * (half + 1))
+            nc.vector.quantize_mx(out=dst[0][:, cols].bitcast(FP8X4), scales=dst[1][:, cols], in_=grouped)
 
-        def sort_w2(b, half):
-            dst = w2g[b][:, 1024 * half : 1024 * (half + 1)].rearrange("p (t m j) -> p m j t", t=2, j=4)
+        def quantise_whole(grouped, name):
+            dst = operand(name)
+            nc.vector.quantize_mx(out=dst[0][:].bitcast(FP8X4), scales=dst[1][:], in_=grouped[:])
+            return dst
+
+        def sort_w2(dst, b, half):
             src = w2raw[b][:].rearrange("p j (m t) -> p m j t", t=4)[:, :, :, 2 * half : 2 * (half + 1)]
-            return dst, src
+            return dst.rearrange("p (t m j) -> p m j t", t=2, j=4), src
 
-        def weave(grouped, raw, lo, hi):
-            dst = grouped[:, 4 * lo : 4 * hi].rearrange("p (c i j) -> p c j i", i=4, j=4)
-            src = raw[:, :, lo:hi].rearrange("p j (c i) -> p c j i", i=4)
-            return dst, src
+        def weave(dst, raw, half):
+            src = raw[:, :, 256 * half : 256 * (half + 1)].rearrange("p j (c i) -> p c j i", i=4)
+            return dst.rearrange("p (c i j) -> p c j i", i=4, j=4), src
 
-        def hidden(b, pair, products, gain, half, th=None):
-            if th is None:
-                th = ring.tile([P, 2, 512], F32, name="th")
+        def hidden(b, pair, products, gain, name):
+            th = ring.tile([P, 2, 512], F32, name="th", tag="th", align_bytes=64)
             for u in range(2):
                 cols = slice(128 * (2 * pair + u), 128 * (2 * pair + u + 1))
                 bank = psum.tile([P, 4, P], F32, name="bank", tag="bank")
@@ -145,43 +151,48 @@ def tile_list_volleyball_rally_commentary_kernel(
                 nc.scalar.activation(
                     th[:, u, :].rearrange("p (s t) -> p s t", t=4), bank[:].rearrange("p t s -> p s t"), ACT.Tanh
                 )
+            grouped = lined([P, 1024], BF16, name)
             nc.vector.tensor_tensor(
-                half.rearrange("p (s t) -> p s t", t=4),
-                th[:, :, :].rearrange("p u (s t) -> p (u s) t", t=4),
+                grouped[:].rearrange("p (s t) -> p s t", t=4),
+                th[:].rearrange("p u (s t) -> p (u s) t", t=4),
                 gain.unsqueeze(1).to_broadcast([P, 256, 4]),
                 ALU.mult,
             )
+            return grouped
 
         v3w = gather(U16, t3w[:], list3, "v3w")
         v2s = gather(U8, t2s[:], list2, "v2s")
-        nc.scalar.copy(*sort_w2(0, 0))
-        nc.vector.tensor_copy(*sort_w2(0, 1))
-        w2q = [quantise(w2g[0], "w2q0")]
-        for half in range(2):
-            nc.scalar.copy(*sort_w2(1, half))
-        v1s_both = gather(U8, t1s[:], list1, "v1s_both")
-        v2w = gather(U32, t2w[:], list2, "v2w")
-        w2q.append((staged([P, 512], U32, "w2q1_codes", "t2w"), held([P, 512], U8, "w2q1_plane")))
-        nc.vector.quantize_mx(out=w2q[1][0][:].bitcast(FP8X4), scales=w2q[1][1][:], in_=w2g[1][:])
+        w2g0 = [held([P, 1024], BF16, "w2g0_0"), lined([P, 1024], BF16, "w2g0_1")]
+        nc.scalar.copy(*sort_w2(w2g0[0][:], 0, 0))
+        nc.vector.tensor_copy(*sort_w2(w2g0[1][:], 0, 1))
+        w2q = [operand("w2q0")]
+        quantise(w2q[0], 1, w2g0[1][:])
+        quantise(w2q[0], 0, w2g0[0][:])
         v3s = gather(U8, t3s[:], list3, "v3s")
+        v2w = gather(U32, t2w[:], list2, "v2w")
+        v1s_both = gather(U8, t1s[:], list1, "v1s_both")
         nc.sync.dma_start(
             v1s_second[0 : P - PASS1_ROW, :].bitcast(I32), v1s_both[PASS1_ROW:P, :].bitcast(I32)
         )
         v1s = [v1s_both, v1s_second]
+        nc.sync.dma_start(w1w[:].bitcast(I32), w1_words.rearrange("a p c -> p a c").bitcast(I32))
         load_rows_two_passes(w1s, w1_scales, 0)
-        nc.sync.dma_start(w5raw[:], w5.rearrange("(p j) n -> p j n", j=4))
-        nc.sync.dma_start(g1rows[0:2, :], g1.rearrange("(b c) -> b c", b=2))
         load_words(t1w[1][:], tab_words[1])
+        nc.sync.dma_start(w5raw[:], w5.rearrange("(p j) n -> p j n", j=4))
         nc.sync.dma_start(w4w[:].bitcast(I32), w4_words.rearrange("a p c i -> p a (c i)").bitcast(I32))
         load_rows_two_passes(w4s, w4_scales, W4_ROW)
-        for b in range(2):
-            rows = w3[512 * b : 512 * (b + 1), :].rearrange("(q t i) n -> t q i n", t=4, i=8)
-            for t in range(4):
-                nc.sync.dma_start(w3raw[b][:, t, :], rows[t])
+        load_w3(0)
+        load_w3(1)
 
-        gains2 = psum.tile([P, 4, P], F32, name="gains2", tag="bank")
+        g1sorted = held([P, 4, P], F32, "g1sorted")
+        nc.scalar.copy(
+            g1sorted[:].rearrange("p t (q i) -> p t q i", i=8), g1rows[:].rearrange("p (q t i) -> p t q i", t=4, i=8)
+        )
+        gains = psum.tile([P, 4, P], F32, name="gains", tag="bank")
         for t in range(4):
-            nc.tensor.transpose(gains2[:, t, :], g2rows[:, t:512:4], ident[:])
+            nc.tensor.matmul(gains[:, t, :], g2rows[:, t:512:4], ident[:], is_transpose=True, start=(t == 0), stop=False)
+        for t in range(4):
+            nc.tensor.matmul(gains[:, t, :], g1sorted[:, t, :], ident[:], is_transpose=True, start=False, stop=(t == 3))
 
         def products2(acc, b, t, cols):
             codes, plane = w2q[b]
@@ -191,81 +202,82 @@ def tile_list_volleyball_rally_commentary_kernel(
                 rhs=v2w[:, cols].bitcast(FP8X4), rhs_scale=v2s[TAB2_ROW:P, cols], start=True, stop=True,
             )
 
+        def products1(acc, b, t, cols):
+            for a in range(2):
+                nc.tensor.matmul_mx(
+                    out=acc, lhsT=w1ws[a][:, b, t, :].bitcast(FP4X4), lhsT_scale=w1ss[:, 2 * a + b, t, :],
+                    rhs=v1w[a][:, cols].bitcast(FP8X4), rhs_scale=v1s[a][:, cols], start=(a == 0), stop=(a == 1),
+                )
+
+        def sort_w1(a):
+            dst = lined([P, 2, 4, 256], U8, f"w1ws{a}")
+            nc.vector.tensor_copy(
+                dst[:].bitcast(I32).rearrange("p b t (q w) -> p b t q w", w=4),
+                w1w[:, a, :].bitcast(I32).rearrange("p (b q t w) -> p b t q w", b=2, t=4, w=4),
+            )
+            return dst
+
+        first = hidden(0, 0, products2, gains[:, :, 0], "h2g0_0")
+        second = hidden(0, 1, products2, gains[:, :, 0], "h2g0_1")
+        w2g1 = held([P, 2048], BF16, "w2g1")
+        for half in range(2):
+            nc.scalar.copy(*sort_w2(w2g1[:, 1024 * half : 1024 * (half + 1)], 1, half))
         v1w = [gather(U32, t1w[0][:], list1, "v1w0")]
-        h2g = [staged([P, 2048], BF16, "h2g0", "t1w0")]
-        hidden(0, 0, products2, gains2[:, :, 0], h2g[0][:, 0:1024])
-        hidden(0, 1, products2, gains2[:, :, 0], h2g[0][:, 1024:2048])
-        h2q = []
-        w1ws = held([P, 4, 4, 256], U8, "w1ws")
-        nc.vector.tensor_copy(
-            w1ws[:].bitcast(I32).rearrange("p x t (q w) -> p x t q w", w=4),
-            w1w[:].bitcast(I32).rearrange("p a (b q t w) -> p (a b) t q w", b=2, t=4, w=4),
-        )
-        h2q.append(quantise(h2g[0], "h2q0"))
-        w1ss = held([P, 4, 4, P], U8, "w1ss")
+        w2q.append(quantise_whole(w2g1, "w2q1"))
+        h2q = [operand("h2q0")]
+        quantise(h2q[0], 0, first[:])
+        quantise(h2q[0], 1, second[:])
+        w1ws = [sort_w1(0), sort_w1(1)]
+        w1ss = lined([P, 4, 4, P], U8, "w1ss")
         nc.vector.tensor_copy(
             w1ss[:].bitcast(I32).rearrange("p x t (q w) -> p x t q w", w=2),
             w1s[:].bitcast(I32).rearrange("p a (b q t w) -> p (a b) t q w", b=2, t=4, w=2),
         )
-        h2g1 = [held([P, 1024], BF16, "h2g1_first")]
-        h2q.append((held([P, 512], U32, "h2q1_codes"), held([P, 512], U8, "h2q1_plane")))
-        hidden(1, 0, products2, gains2[:, :, 1], h2g1[0][:])
         v1w.append(gather(U32, t1w[1][:], list1, "v1w1"))
-        h2g1.append(after_tab([P, 1024], BF16, "h2g1_second", 0))
-        hidden(1, 1, products2, gains2[:, :, 1], h2g1[1][:])
-        w5g = staged([P, 2048], BF16, "w5g", "w5g")
+        first = hidden(1, 0, products2, gains[:, :, 1], "h2g1_0")
+        second = hidden(1, 1, products2, gains[:, :, 1], "h2g1_1")
+        w5g = [lined([P, 1024], BF16, "w5g_0")]
+        nc.vector.tensor_scalar(*weave(w5g[0][:], w5raw, 0), -1.0, None, ALU.mult)
+        h2q.append(operand("h2q1"))
+        quantise(h2q[1], 0, first[:])
+        quantise(h2q[1], 1, second[:])
+        first = hidden(0, 0, products1, gains[:, :, 2], "h1g0_0")
+        second = hidden(0, 1, products1, gains[:, :, 2], "h1g0_1")
+        w5g.append(ring.tile([P, 1024], BF16, name="w5g_1", tag="th", align_bytes=64))
+        nc.scalar.activation(*weave(w5g[1][:], w5raw, 1), ACT.Copy, scale=-1.0)
+        w5q = operand("w5q")
         for half in range(2):
-            nc.scalar.activation(*weave(w5g, w5raw, 256 * half, 256 * (half + 1)), ACT.Copy, scale=-1.0)
-        w5q = (after_tab([P, 512], U32, "w5q_codes", 2048), held([P, 512], U8, "w5q_plane"))
-        nc.vector.quantize_mx(out=w5q[0][:].bitcast(FP8X4), scales=w5q[1][:], in_=w5g[:])
+            quantise(w5q, half, w5g[half][:])
+        h1q = [operand("h1q0")]
+        quantise(h1q[0], 0, first[:])
+        quantise(h1q[0], 1, second[:])
+        first = hidden(1, 0, products1, gains[:, :, 3], "h1g1_0")
+        w3g0 = held([P, 2048], BF16, "w3g0")
+        w3g1 = [lined([P, 1024], BF16, "w3g1_0"), held([P, 1024], BF16, "w3g1_1")]
+        nc.vector.tensor_copy(*weave(w3g1[0][:], w3raw[1], 0))
+        second = hidden(1, 1, products1, gains[:, :, 3], "h1g1_1")
         for half in range(2):
-            cols = slice(256 * half, 256 * (half + 1))
-            nc.vector.quantize_mx(out=h2q[1][0][:, cols].bitcast(FP8X4), scales=h2q[1][1][:, cols], in_=h2g1[half][:])
-        late = staged([P, 4, 2, 512], F32, "late", "w5raw")
-
-        g1sorted = held([P, 4, P], F32, "g1sorted")
-        nc.scalar.copy(
-            g1sorted[:].rearrange("p t (q i) -> p t q i", i=8), g1rows[:].rearrange("p (q t i) -> p t q i", t=4, i=8)
-        )
-        gains1 = psum.tile([P, 4, P], F32, name="gains1", tag="bank")
-        for t in range(4):
-            nc.tensor.transpose(gains1[:, t, :], g1sorted[:, t, :], ident[:])
-
-        def products1(acc, b, t, cols):
-            for a in range(2):
-                nc.tensor.matmul_mx(
-                    out=acc, lhsT=w1ws[:, 2 * a + b, t, :].bitcast(FP4X4), lhsT_scale=w1ss[:, 2 * a + b, t, :],
-                    rhs=v1w[a][:, cols].bitcast(FP8X4), rhs_scale=v1s[a][:, cols], start=(a == 0), stop=(a == 1),
-                )
-
-        h1g = [staged([P, 2048], BF16, "h1g0", "w5g")]
-        hidden(0, 0, products1, gains1[:, :, 0], h1g[0][:, 0:1024], late[:, 0])
-        hidden(0, 1, products1, gains1[:, :, 0], h1g[0][:, 1024:2048], late[:, 1])
-        w3g = [held([P, 2048], BF16, f"w3g{b}") for b in range(2)]
-        nc.vector.tensor_copy(*weave(w3g[0], w3raw[0], 0, 512))
-        h1q = [quantise(h1g[0], "h1q0")]
-        w3q = [quantise(w3g[0], "w3q0")]
-        h1g.append(staged([P, 2048], BF16, "h1g1", "w3raw0"))
-        hidden(1, 0, products1, gains1[:, :, 1], h1g[1][:, 0:1024], late[:, 2])
-        hidden(1, 1, products1, gains1[:, :, 1], h1g[1][:, 1024:2048], late[:, 3])
+            nc.scalar.copy(*weave(w3g0[:, 1024 * half : 1024 * (half + 1)], w3raw[0], half))
+        nc.scalar.copy(*weave(w3g1[1][:], w3raw[1], 1))
+        w3q = [quantise_whole(w3g0, "w3q0")]
+        h1q.append(operand("h1q1"))
+        quantise(h1q[1], 0, first[:])
+        quantise(h1q[1], 1, second[:])
+        w3q.append(operand("w3q1"))
         for half in range(2):
-            nc.scalar.copy(*weave(w3g[1], w3raw[1], 256 * half, 256 * (half + 1)))
-        w3q.append(quantise(w3g[1], "w3q1"))
+            quantise(w3q[1], half, w3g1[half][:])
 
-        h1q.append(quantise(h1g[1], "h1q1"))
-
-        def arena(acc, m):
+        def arena(acc, m, start, stop):
             nc.tensor.matmul_mx(
                 out=acc, lhsT=w5q[0][:, m].bitcast(FP8X4), lhsT_scale=w5q[1][:, m],
-                rhs=v3w[:].bitcast(FP4X4), rhs_scale=v3s[:], start=True, stop=False,
+                rhs=v3w[:].bitcast(FP4X4), rhs_scale=v3s[:], start=start, stop=stop,
             )
-
 
         y2 = staged([P, 4, S], F32, "y2", "w3raw1")
         for n in range(4):
             m = slice(128 * n, 128 * (n + 1))
             acc = psum.tile([P, S], F32, name="acc", tag="bank")
-            arena(acc[:], m)
+            arena(acc[:], m, True, False)
             for a in range(2):
                 nc.tensor.matmul_mx(
                     out=acc[:], lhsT=w4w[:, a, m].bitcast(FP8X4), lhsT_scale=w4s[W4_ROW:P, a, m],
@@ -277,7 +289,7 @@ def tile_list_volleyball_rally_commentary_kernel(
         for n in range(4):
             m = slice(128 * n, 128 * (n + 1))
             acc = psum.tile([P, S], F32, name="acc", tag="bank")
-            arena(acc[:], m)
+            arena(acc[:], m, True, False)
             y1banks.append(acc)
         for b in range(2):
             for n in range(4):

@@ -188,11 +188,13 @@ def tile_list_volleyball_rally_commentary_kernel(
         nc.scalar.copy(
             g1sorted[:].rearrange("p t (q i) -> p t q i", i=8), g1rows[:].rearrange("p (q t i) -> p t q i", t=4, i=8)
         )
-        gains = psum.tile([P, 4, P], F32, name="gains", tag="bank")
+        turned = psum.tile([P, 4, P], F32, name="turned", tag="bank")
         for t in range(4):
-            nc.tensor.matmul(gains[:, t, :], g2rows[:, t:512:4], ident[:], is_transpose=True, start=(t == 0), stop=False)
+            nc.tensor.matmul(turned[:, t, :], g2rows[:, t:512:4], ident[:], is_transpose=True, start=(t == 0), stop=False)
         for t in range(4):
-            nc.tensor.matmul(gains[:, t, :], g1sorted[:, t, :], ident[:], is_transpose=True, start=False, stop=(t == 3))
+            nc.tensor.matmul(turned[:, t, :], g1sorted[:, t, :], ident[:], is_transpose=True, start=False, stop=(t == 3))
+        gains = held([P, 4, 4], F32, "gains")
+        nc.scalar.copy(gains[:], turned[:, :, 0:4].rearrange("p t r -> p r t"))
 
         def products2(acc, b, t, cols):
             codes, plane = w2q[b]
@@ -217,8 +219,8 @@ def tile_list_volleyball_rally_commentary_kernel(
             )
             return dst
 
-        first = hidden(0, 0, products2, gains[:, :, 0], "h2g0_0")
-        second = hidden(0, 1, products2, gains[:, :, 0], "h2g0_1")
+        first = hidden(0, 0, products2, gains[:, 0, :], "h2g0_0")
+        second = hidden(0, 1, products2, gains[:, 0, :], "h2g0_1")
         w2g1 = held([P, 2048], BF16, "w2g1")
         for half in range(2):
             nc.scalar.copy(*sort_w2(w2g1[:, 1024 * half : 1024 * (half + 1)], 1, half))
@@ -234,15 +236,15 @@ def tile_list_volleyball_rally_commentary_kernel(
             w1s[:].bitcast(I32).rearrange("p a (b q t w) -> p (a b) t q w", b=2, t=4, w=2),
         )
         v1w.append(gather(U32, t1w[1][:], list1, "v1w1"))
-        first = hidden(1, 0, products2, gains[:, :, 1], "h2g1_0")
-        second = hidden(1, 1, products2, gains[:, :, 1], "h2g1_1")
+        first = hidden(1, 0, products2, gains[:, 1, :], "h2g1_0")
+        second = hidden(1, 1, products2, gains[:, 1, :], "h2g1_1")
         w5g = [lined([P, 1024], BF16, "w5g_0")]
         nc.vector.tensor_scalar(*weave(w5g[0][:], w5raw, 0), -1.0, None, ALU.mult)
         h2q.append(operand("h2q1"))
         quantise(h2q[1], 0, first[:])
         quantise(h2q[1], 1, second[:])
-        first = hidden(0, 0, products1, gains[:, :, 2], "h1g0_0")
-        second = hidden(0, 1, products1, gains[:, :, 2], "h1g0_1")
+        first = hidden(0, 0, products1, gains[:, 2, :], "h1g0_0")
+        second = hidden(0, 1, products1, gains[:, 2, :], "h1g0_1")
         w5g.append(ring.tile([P, 1024], BF16, name="w5g_1", tag="th", align_bytes=64))
         nc.scalar.activation(*weave(w5g[1][:], w5raw, 1), ACT.Copy, scale=-1.0)
         w5q = operand("w5q")
@@ -251,11 +253,11 @@ def tile_list_volleyball_rally_commentary_kernel(
         h1q = [operand("h1q0")]
         quantise(h1q[0], 0, first[:])
         quantise(h1q[0], 1, second[:])
-        first = hidden(1, 0, products1, gains[:, :, 3], "h1g1_0")
+        first = hidden(1, 0, products1, gains[:, 3, :], "h1g1_0")
         w3g0 = held([P, 2048], BF16, "w3g0")
         w3g1 = [lined([P, 1024], BF16, "w3g1_0"), held([P, 1024], BF16, "w3g1_1")]
         nc.vector.tensor_copy(*weave(w3g1[0][:], w3raw[1], 0))
-        second = hidden(1, 1, products1, gains[:, :, 3], "h1g1_1")
+        second = hidden(1, 1, products1, gains[:, 3, :], "h1g1_1")
         for half in range(2):
             nc.scalar.copy(*weave(w3g0[:, 1024 * half : 1024 * (half + 1)], w3raw[0], half))
         nc.scalar.copy(*weave(w3g1[1][:], w3raw[1], 1))

@@ -63,17 +63,15 @@ def tile_list_volleyball_rally_commentary_kernel(
         w2raw = [held([P, 4, 512], F32, f"w2raw{b}") for b in range(2)]
         w5raw = staged([P, 4, N], F32, "w5raw", "w5raw")
         w3raw = [staged([P, 4, N], F32, f"w3raw{b}", f"w3raw{b}") for b in range(2)]
-        g2rows = held([P, 512], F32, "g2rows")
-        g1rows = held([P, 512], F32, "g1rows")
+        grows = held([P, 512], F32, "grows")
         ident = held([P, P], F32, "ident")
 
         nc.gpsimd.memset(t2s[:].bitcast(I32), 0)
         nc.vector.memset(t1s[:].bitcast(I32), 0)
-        nc.gpsimd.memset(g2rows[:], 0.0)
+        nc.gpsimd.memset(grows[:], 0.0)
         make_identity(nc, ident[:])
         nc.gpsimd.memset(v1s_second[:].bitcast(I32), 0)
         nc.gpsimd.memset(t3s[:].bitcast(I32), 0)
-        nc.gpsimd.memset(g1rows[:], 0.0)
         nc.vector.memset(w1s[:].bitcast(I32), 0)
         nc.vector.memset(w4s[:].bitcast(I32), 0)
 
@@ -92,9 +90,7 @@ def tile_list_volleyball_rally_commentary_kernel(
             nc.sync.dma_start(dst.bitcast(I32), words.rearrange("p c i -> p (c i)").bitcast(I32))
 
         def load_w3(b):
-            rows = w3[512 * b : 512 * (b + 1), :].rearrange("(q t i) n -> t q i n", t=4, i=8)
-            for t in range(4):
-                nc.sync.dma_start(w3raw[b][:, t, :], rows[t])
+            nc.sync.dma_start(w3raw[b][:], w3[512 * b : 512 * (b + 1), :].rearrange("(p j) n -> p j n", j=4))
 
         w2v = w2.rearrange("(p j) c -> p j c", j=4)
 
@@ -103,8 +99,8 @@ def tile_list_volleyball_rally_commentary_kernel(
         nc.sync.dma_start(t3w[:].bitcast(I32), tab3_words[0].bitcast(I32))
         load_rows(t2s, tab2_scales, TAB2_ROW)
         nc.sync.dma_start(w2raw[0][:], w2v[:, :, 0:512])
-        nc.sync.dma_start(g2rows[0:2, :], g2.rearrange("(b c) -> b c", b=2))
-        nc.sync.dma_start(g1rows[2:4, :], g1.rearrange("(b c) -> b c", b=2))
+        nc.sync.dma_start(grows[0:2, :], g2.rearrange("(b c) -> b c", b=2))
+        nc.sync.dma_start(grows[2:4, :], g1.rearrange("(b c) -> b c", b=2))
         load_rows(t3s, tab3_scales, 0)
         load_words(t2w[:], tab2_words[0])
         nc.sync.dma_start(list1[:], offs)
@@ -184,15 +180,9 @@ def tile_list_volleyball_rally_commentary_kernel(
         load_w3(0)
         load_w3(1)
 
-        g1sorted = held([P, 4, P], F32, "g1sorted")
-        nc.scalar.copy(
-            g1sorted[:].rearrange("p t (q i) -> p t q i", i=8), g1rows[:].rearrange("p (q t i) -> p t q i", t=4, i=8)
-        )
         turned = psum.tile([P, 4, P], F32, name="turned", tag="bank")
         for t in range(4):
-            nc.tensor.matmul(turned[:, t, :], g2rows[:, t:512:4], ident[:], is_transpose=True, start=(t == 0), stop=False)
-        for t in range(4):
-            nc.tensor.matmul(turned[:, t, :], g1sorted[:, t, :], ident[:], is_transpose=True, start=False, stop=(t == 3))
+            nc.tensor.transpose(turned[:, t, :], grows[:, t:512:4], ident[:])
         gains = held([P, 4, 4], F32, "gains")
         nc.scalar.copy(gains[:], turned[:, :, 0:4].rearrange("p t r -> p r t"))
 
@@ -214,8 +204,8 @@ def tile_list_volleyball_rally_commentary_kernel(
         def sort_w1(a):
             dst = lined([P, 2, 4, 256], U8, f"w1ws{a}")
             nc.vector.tensor_copy(
-                dst[:].bitcast(I32).rearrange("p b t (q w) -> p b t q w", w=4),
-                w1w[:, a, :].bitcast(I32).rearrange("p (b q t w) -> p b t q w", b=2, t=4, w=4),
+                dst[:].bitcast(U16),
+                w1w[:, a, :].bitcast(U16).rearrange("p (b m t) -> p b t m", b=2, t=4),
             )
             return dst
 
@@ -232,8 +222,7 @@ def tile_list_volleyball_rally_commentary_kernel(
         w1ws = [sort_w1(0), sort_w1(1)]
         w1ss = lined([P, 4, 4, P], U8, "w1ss")
         nc.vector.tensor_copy(
-            w1ss[:].bitcast(I32).rearrange("p x t (q w) -> p x t q w", w=2),
-            w1s[:].bitcast(I32).rearrange("p a (b q t w) -> p (a b) t q w", b=2, t=4, w=2),
+            w1ss[:], w1s[:].rearrange("p a (b m t) -> p (a b) t m", b=2, t=4)
         )
         v1w.append(gather(U32, t1w[1][:], list1, "v1w1"))
         first = hidden(1, 0, products2, gains[:, 1, :], "h2g1_0")

@@ -33,7 +33,7 @@ def tile_list_volleyball_rally_commentary_kernel(
     nc = tc.nc
     with ExitStack() as ctx:
         keep = ctx.enter_context(tc.tile_pool(name="keep", bufs=1))
-        line = ctx.enter_context(tc.tile_pool(name="line", bufs=36))
+        line = ctx.enter_context(tc.tile_pool(name="line", bufs=38))
         ring = ctx.enter_context(tc.tile_pool(name="ring", bufs=6))
         psum = ctx.enter_context(tc.psum_pool(name="psum", bufs=8))
 
@@ -109,6 +109,7 @@ def tile_list_volleyball_rally_commentary_kernel(
                 t1s[r:P:PASS1_ROW, :].bitcast(I32),
                 tab_scales.rearrange("a (q r) c -> r q a c", r=4)[r].bitcast(I32),
             )
+        nc.sync.dma_start(w1w[:].bitcast(I32), w1_words.rearrange("a p c -> p a c").bitcast(I32))
         nc.sync.dma_start(w2raw[1][:], w2v[:, :, 512:1024])
         load_words(t1w[0][:], tab_words[0])
 
@@ -138,20 +139,17 @@ def tile_list_volleyball_rally_commentary_kernel(
             return dst.rearrange("p (c i j) -> p c j i", i=4, j=4), src
 
         def hidden(b, pair, products, gain, name):
-            th = ring.tile([P, 2, 512], F32, name="th", tag="th", align_bytes=64)
+            th = ring.tile([P, 2, 256, 2], F32, name="th", tag="th", align_bytes=64)
             for u in range(2):
-                cols = slice(128 * (2 * pair + u), 128 * (2 * pair + u + 1))
-                bank = psum.tile([P, 4, P], F32, name="bank", tag="bank")
-                for t in range(4):
-                    products(bank[:, t, :], b, t, cols)
-                nc.scalar.activation(
-                    th[:, u, :].rearrange("p (s t) -> p s t", t=4), bank[:].rearrange("p t s -> p s t"), ACT.Tanh
-                )
+                bank = psum.tile([P, 2, 256], F32, name="bank", tag="bank")
+                for e in range(2):
+                    products(bank[:, e, :], b, 2 * u + e, 256 * pair)
+                nc.scalar.activation(th[:, u], bank[:].rearrange("p e s -> p s e"), ACT.Tanh)
             grouped = lined([P, 1024], BF16, name)
             nc.vector.tensor_tensor(
-                grouped[:].rearrange("p (s t) -> p s t", t=4),
-                th[:].rearrange("p u (s t) -> p (u s) t", t=4),
-                gain.unsqueeze(1).to_broadcast([P, 256, 4]),
+                grouped[:].rearrange("p (s u e) -> p s u e", u=2, e=2),
+                th[:].rearrange("p u s e -> p s u e"),
+                gain.rearrange("p (u e) -> p u e", e=2).unsqueeze(1).to_broadcast([P, 256, 2, 2]),
                 ALU.mult,
             )
             return grouped
@@ -171,7 +169,6 @@ def tile_list_volleyball_rally_commentary_kernel(
             v1s_second[0 : P - PASS1_ROW, :].bitcast(I32), v1s_both[PASS1_ROW:P, :].bitcast(I32)
         )
         v1s = [v1s_both, v1s_second]
-        nc.sync.dma_start(w1w[:].bitcast(I32), w1_words.rearrange("a p c -> p a c").bitcast(I32))
         load_rows_two_passes(w1s, w1_scales, 0)
         load_words(t1w[1][:], tab_words[1])
         nc.sync.dma_start(w5raw[:], w5.rearrange("(p j) n -> p j n", j=4))
@@ -186,7 +183,8 @@ def tile_list_volleyball_rally_commentary_kernel(
         gains = held([P, 4, 4], F32, "gains")
         nc.scalar.copy(gains[:], turned[:, :, 0:4].rearrange("p t r -> p r t"))
 
-        def products2(acc, b, t, cols):
+        def products2(acc, b, t, first):
+            cols = slice(first, first + 256)
             codes, plane = w2q[b]
             m = slice(128 * t, 128 * (t + 1))
             nc.tensor.matmul_mx(
@@ -194,12 +192,15 @@ def tile_list_volleyball_rally_commentary_kernel(
                 rhs=v2w[:, cols].bitcast(FP8X4), rhs_scale=v2s[TAB2_ROW:P, cols], start=True, stop=True,
             )
 
-        def products1(acc, b, t, cols):
-            for a in range(2):
-                nc.tensor.matmul_mx(
-                    out=acc, lhsT=w1ws[a][:, b, t, :].bitcast(FP4X4), lhsT_scale=w1ss[:, 2 * a + b, t, :],
-                    rhs=v1w[a][:, cols].bitcast(FP8X4), rhs_scale=v1s[a][:, cols], start=(a == 0), stop=(a == 1),
-                )
+        def products1(acc, b, t, first):
+            for lo in (0, 128):
+                cols = slice(first + lo, first + lo + 128)
+                for a in (1, 0):
+                    nc.tensor.matmul_mx(
+                        out=acc[:, lo : lo + 128],
+                        lhsT=w1ws[a][:, b, t, :].bitcast(FP4X4), lhsT_scale=w1ss[:, 2 * a + b, t, :],
+                        rhs=v1w[a][:, cols].bitcast(FP8X4), rhs_scale=v1s[a][:, cols], start=(a == 1), stop=(a == 0),
+                    )
 
         def sort_w1(a):
             dst = lined([P, 2, 4, 256], U8, f"w1ws{a}")
@@ -209,17 +210,17 @@ def tile_list_volleyball_rally_commentary_kernel(
             )
             return dst
 
+        w1ws = [sort_w1(0), sort_w1(1)]
         first = hidden(0, 0, products2, gains[:, 0, :], "h2g0_0")
         second = hidden(0, 1, products2, gains[:, 0, :], "h2g0_1")
         w2g1 = held([P, 2048], BF16, "w2g1")
         for half in range(2):
             nc.scalar.copy(*sort_w2(w2g1[:, 1024 * half : 1024 * (half + 1)], 1, half))
-        v1w = [gather(U32, t1w[0][:], list1, "v1w0")]
-        w2q.append(quantise_whole(w2g1, "w2q1"))
         h2q = [operand("h2q0")]
         quantise(h2q[0], 0, first[:])
         quantise(h2q[0], 1, second[:])
-        w1ws = [sort_w1(0), sort_w1(1)]
+        v1w = [gather(U32, t1w[0][:], list1, "v1w0")]
+        w2q.append(quantise_whole(w2g1, "w2q1"))
         w1ss = lined([P, 4, 4, P], U8, "w1ss")
         nc.vector.tensor_copy(
             w1ss[:], w1s[:].rearrange("p a (b m t) -> p (a b) t m", b=2, t=4)
@@ -242,21 +243,23 @@ def tile_list_volleyball_rally_commentary_kernel(
         h1q = [operand("h1q0")]
         quantise(h1q[0], 0, first[:])
         quantise(h1q[0], 1, second[:])
+        w3g = [[lined([P, 1024], BF16, "w3g0_0"), held([P, 1024], BF16, "w3g0_1")]]
+        nc.vector.tensor_copy(*weave(w3g[0][0][:], w3raw[0], 0))
         first = hidden(1, 0, products1, gains[:, 3, :], "h1g1_0")
-        w3g0 = held([P, 2048], BF16, "w3g0")
-        w3g1 = [lined([P, 1024], BF16, "w3g1_0"), held([P, 1024], BF16, "w3g1_1")]
-        nc.vector.tensor_copy(*weave(w3g1[0][:], w3raw[1], 0))
+        w3g.append([lined([P, 1024], BF16, "w3g1_0"), held([P, 1024], BF16, "w3g1_1")])
+        nc.vector.tensor_copy(*weave(w3g[1][0][:], w3raw[1], 0))
         second = hidden(1, 1, products1, gains[:, 3, :], "h1g1_1")
+        for b in range(2):
+            nc.scalar.copy(*weave(w3g[b][1][:], w3raw[b], 1))
+        w3q = [operand("w3q0")]
         for half in range(2):
-            nc.scalar.copy(*weave(w3g0[:, 1024 * half : 1024 * (half + 1)], w3raw[0], half))
-        nc.scalar.copy(*weave(w3g1[1][:], w3raw[1], 1))
-        w3q = [quantise_whole(w3g0, "w3q0")]
+            quantise(w3q[0], half, w3g[0][half][:])
         h1q.append(operand("h1q1"))
         quantise(h1q[1], 0, first[:])
         quantise(h1q[1], 1, second[:])
         w3q.append(operand("w3q1"))
         for half in range(2):
-            quantise(w3q[1], half, w3g1[half][:])
+            quantise(w3q[1], half, w3g[1][half][:])
 
         def arena(acc, m, start, stop):
             nc.tensor.matmul_mx(

@@ -33,8 +33,8 @@ def tile_list_volleyball_rally_commentary_kernel(
     nc = tc.nc
     with ExitStack() as ctx:
         keep = ctx.enter_context(tc.tile_pool(name="keep", bufs=1))
-        line = ctx.enter_context(tc.tile_pool(name="line", bufs=38))
-        ring = ctx.enter_context(tc.tile_pool(name="ring", bufs=6))
+        line = ctx.enter_context(tc.tile_pool(name="line", bufs=32))
+        ring = ctx.enter_context(tc.tile_pool(name="ring", bufs=5))
         psum = ctx.enter_context(tc.psum_pool(name="psum", bufs=8))
 
         def held(shape, dtype, name):
@@ -49,229 +49,247 @@ def tile_list_volleyball_rally_commentary_kernel(
         list1 = held([P, S // 16], U16, "list1")
         list2 = held([P, S // 16], U16, "list2")
         list3 = held([P, S // 16], U16, "list3")
-        t1w = [staged([P, T1], U32, "t1w0", "t1w0"), held([P, T1], U32, "t1w1")]
-        t2w = held([P, T2], U32, "t2w")
+        t1w = [held([P, T1], U32, f"t1w{a}") for a in range(2)]
+        t2w = staged([P, T2], U32, "t2w", "shared")
         t3w = held([P, T3], U16, "t3w")
         t1s = held([P, T1], U8, "t1s")
         t2s = held([P, T2], U8, "t2s")
-        t3s = staged([P, T3], U8, "t3s", "t3s")
+        t3s = held([P, T3], U8, "t3s")
         v1s_second = held([P, S], U8, "v1s_second")
         w1w = held([P, 2, 2 * H], U8, "w1w")
-        w1s = held([P, 2, H], U8, "w1s")
+        w1s = held([P, H], U8, "w1s")
+        w1ss_second = held([P, H], U8, "w1ss_second")
         w4w = held([P, 2, N], U32, "w4w")
         w4s = held([P, 2, N], U8, "w4s")
-        w2raw = [held([P, 4, 512], F32, f"w2raw{b}") for b in range(2)]
-        w5raw = staged([P, 4, N], F32, "w5raw", "w5raw")
+        w2raw = [staged([P, 4, 512], F32, f"w2raw{b}", f"w2raw{b}") for b in range(2)]
+        w5raw = held([P, 4, N], F32, "w5raw")
         w3raw = [staged([P, 4, N], F32, f"w3raw{b}", f"w3raw{b}") for b in range(2)]
         grows = held([P, 512], F32, "grows")
         ident = held([P, P], F32, "ident")
 
-        nc.gpsimd.memset(t2s[:].bitcast(I32), 0)
-        nc.vector.memset(t1s[:].bitcast(I32), 0)
+        nc.gpsimd.memset(t1s[:].bitcast(I32), 0)
+        nc.vector.memset(w1s[:].bitcast(I32), 0)
+        nc.vector.memset(t3s[:].bitcast(I32), 0)
+        nc.vector.memset(t2s[:].bitcast(I32), 0)
         nc.gpsimd.memset(grows[:], 0.0)
         make_identity(nc, ident[:])
         nc.gpsimd.memset(v1s_second[:].bitcast(I32), 0)
-        nc.gpsimd.memset(t3s[:].bitcast(I32), 0)
-        nc.vector.memset(w1s[:].bitcast(I32), 0)
+        nc.gpsimd.memset(w1ss_second[:].bitcast(I32), 0)
         nc.vector.memset(w4s[:].bitcast(I32), 0)
 
         def load_rows(plane, scales, row0):
             for r in range(4):
                 nc.sync.dma_start(plane[row0 + r : P : 32, :].bitcast(I32), scales[0, r:16:4, :].bitcast(I32))
 
-        def load_rows_two_passes(plane, scales, row0):
+        def load_rows_side_by_side(plane, scales, row0):
             for r in range(4):
                 nc.sync.dma_start(
                     plane[row0 + r : P : 32, :, :].bitcast(I32),
                     scales[:, r:16:4, :].rearrange("a q c -> q a c").bitcast(I32),
                 )
 
+        def load_rows_stacked(plane, scales):
+            for r in range(4):
+                nc.sync.dma_start(
+                    plane[r:P:PASS1_ROW, :].bitcast(I32), scales.rearrange("a (q r) c -> r q a c", r=4)[r].bitcast(I32)
+                )
+
+        def lift_second_pass(dst, both):
+            nc.sync.dma_start(dst[0 : P - PASS1_ROW, :].bitcast(I32), both[PASS1_ROW:P, :].bitcast(I32))
+
         def load_words(dst, words):
             nc.sync.dma_start(dst.bitcast(I32), words.rearrange("p c i -> p (c i)").bitcast(I32))
 
-        def load_w3(b):
-            nc.sync.dma_start(w3raw[b][:], w3[512 * b : 512 * (b + 1), :].rearrange("(p j) n -> p j n", j=4))
-
-        w2v = w2.rearrange("(p j) c -> p j c", j=4)
-
-        nc.sync.dma_start(list2[:], offs2)
-        nc.sync.dma_start(list3[:], offs3)
-        nc.sync.dma_start(t3w[:].bitcast(I32), tab3_words[0].bitcast(I32))
-        load_rows(t2s, tab2_scales, TAB2_ROW)
-        nc.sync.dma_start(w2raw[0][:], w2v[:, :, 0:512])
-        nc.sync.dma_start(grows[0:2, :], g2.rearrange("(b c) -> b c", b=2))
-        nc.sync.dma_start(grows[2:4, :], g1.rearrange("(b c) -> b c", b=2))
-        load_rows(t3s, tab3_scales, 0)
-        load_words(t2w[:], tab2_words[0])
-        nc.sync.dma_start(list1[:], offs)
-        for r in range(4):
-            nc.sync.dma_start(
-                t1s[r:P:PASS1_ROW, :].bitcast(I32),
-                tab_scales.rearrange("a (q r) c -> r q a c", r=4)[r].bitcast(I32),
-            )
-        nc.sync.dma_start(w1w[:].bitcast(I32), w1_words.rearrange("a p c -> p a c").bitcast(I32))
-        nc.sync.dma_start(w2raw[1][:], w2v[:, :, 512:1024])
-        load_words(t1w[0][:], tab_words[0])
+        def load_floats(dst, rows):
+            nc.sync.dma_start(dst[:], rows.rearrange("(p j) n -> p j n", j=4))
 
         def gather(dtype, window, offsets, name):
             picked = lined([P, S], dtype, name)
             nc.vector.tensor_copy(picked[:], window.indirect(offsets[:]))
             return picked
 
-        def operand(name):
-            return lined([P, 512], U32, name + "_codes"), held([P, 512], U8, name + "_plane")
+        def halves(tile):
+            return tile[:, 0:1024], tile[:, 1024:2048]
 
-        def quantise(dst, half, grouped):
-            cols = slice(256 * half, 256 * (half + 1))
-            nc.vector.quantize_mx(out=dst[0][:, cols].bitcast(FP8X4), scales=dst[1][:, cols], in_=grouped)
+        def quantise(grouped, name):
+            words = grouped.shape[1] // 4
+            codes, plane = lined([P, words], U32, name + "_codes"), held([P, words], U8, name + "_plane")
+            nc.vector.quantize_mx(out=codes[:].bitcast(FP8X4), scales=plane[:], in_=grouped)
+            return codes, plane
 
-        def quantise_whole(grouped, name):
-            dst = operand(name)
-            nc.vector.quantize_mx(out=dst[0][:].bitcast(FP8X4), scales=dst[1][:], in_=grouped[:])
-            return dst
+        def window(operand, lo, hi):
+            return operand[0][:, lo:hi].bitcast(FP8X4), operand[1][:, lo:hi]
 
-        def sort_w2(dst, b, half):
+        def sort_w2(grouped, b, half):
             src = w2raw[b][:].rearrange("p j (m t) -> p m j t", t=4)[:, :, :, 2 * half : 2 * (half + 1)]
-            return dst.rearrange("p (t m j) -> p m j t", t=2, j=4), src
+            return grouped[:].rearrange("p (t m j) -> p m j t", t=2, j=4), src
 
-        def weave(dst, raw, half):
+        def weave(grouped, raw, half):
             src = raw[:, :, 256 * half : 256 * (half + 1)].rearrange("p j (c i) -> p c j i", i=4)
-            return dst.rearrange("p (c i j) -> p c j i", i=4, j=4), src
+            return grouped[:].rearrange("p (c i j) -> p c j i", i=4, j=4), src
 
-        def hidden(b, pair, products, gain, name):
-            th = ring.tile([P, 2, 256, 2], F32, name="th", tag="th", align_bytes=64)
-            for u in range(2):
-                bank = psum.tile([P, 2, 256], F32, name="bank", tag="bank")
-                for e in range(2):
-                    products(bank[:, e, :], b, 2 * u + e, 256 * pair)
-                nc.scalar.activation(th[:, u], bank[:].rearrange("p e s -> p s e"), ACT.Tanh)
-            grouped = lined([P, 1024], BF16, name)
+        def scalar_half(name):
+            return ring.tile([P, 1024], BF16, name=name, tag="th", align_bytes=64)
+
+        def column_tile(parts, k):
+            return window(parts[k // 2], 128 * (k % 2), 128 * (k % 2 + 1))
+
+        def first_stage(products, blocks):
+            th = ring.tile([P, 4, 512], F32, name="th", tag="th", align_bytes=64)
+            for u, (b, first) in enumerate(blocks):
+                bank = psum.tile([P, 4, P], F32, name="bank", tag="bank")
+                for t in range(4):
+                    products(bank[:, t, :], b, t, slice(first, first + P))
+                nc.scalar.activation(
+                    th[:, u, :].rearrange("p (s t) -> p s t", t=4), bank[:].rearrange("p t s -> p s t"), ACT.Tanh
+                )
+            return th
+
+        def gain_on_vector(grouped, th, lo, hi, row):
             nc.vector.tensor_tensor(
-                grouped[:].rearrange("p (s u e) -> p s u e", u=2, e=2),
-                th[:].rearrange("p u s e -> p s u e"),
-                gain.rearrange("p (u e) -> p u e", e=2).unsqueeze(1).to_broadcast([P, 256, 2, 2]),
+                grouped.rearrange("p (s t) -> p s t", t=4),
+                th[:, lo:hi, :].rearrange("p u (s t) -> p (u s) t", t=4),
+                turned[:, :, row].unsqueeze(1).to_broadcast([P, P * (hi - lo), 4]),
                 ALU.mult,
             )
-            return grouped
+
+        def gain_on_pool(grouped, th, u, row):
+            nc.gpsimd.tensor_tensor(
+                grouped.rearrange("p (x c) -> p x c", c=64),
+                th[:, u, :].rearrange("p (x c) -> p x c", c=64),
+                spread[:, row, :].unsqueeze(1).to_broadcast([P, 8, 64]),
+                ALU.mult,
+            )
+
+        def blocks(b):
+            return [(b, first) for first in range(0, S, P)]
+
+        def gains(name, tag, th, row):
+            first, shared = lined([P, 1024], BF16, name), staged([P, 1024], BF16, name + "_shared", tag)
+            gain_on_vector(first[:], th, 0, 2, row)
+            gain_on_pool(shared[:, 0:512], th, 2, row)
+            gain_on_vector(shared[:, 512:1024], th, 3, 4, row)
+            return first, shared
+
+        nc.sync.dma_start(list3[:], offs3)
+        nc.sync.dma_start(list1[:], offs)
+        nc.sync.dma_start(t3w[:].bitcast(I32), tab3_words[0].bitcast(I32))
+        load_rows_stacked(t1s, tab_scales)
+        load_words(t1w[0][:], tab_words[0])
+        load_rows_stacked(w1s, w1_scales)
+        nc.sync.dma_start(w1w[:].bitcast(I32), w1_words.rearrange("a p c -> p a c").bitcast(I32))
+        nc.sync.dma_start(list2[:], offs2)
+        load_rows(t2s, tab2_scales, TAB2_ROW)
 
         v3w = gather(U16, t3w[:], list3, "v3w")
-        v2s = gather(U8, t2s[:], list2, "v2s")
-        w2g0 = [held([P, 1024], BF16, "w2g0_0"), lined([P, 1024], BF16, "w2g0_1")]
-        nc.scalar.copy(*sort_w2(w2g0[0][:], 0, 0))
-        nc.vector.tensor_copy(*sort_w2(w2g0[1][:], 0, 1))
-        w2q = [operand("w2q0")]
-        quantise(w2q[0], 1, w2g0[1][:])
-        quantise(w2q[0], 0, w2g0[0][:])
-        v3s = gather(U8, t3s[:], list3, "v3s")
-        v2w = gather(U32, t2w[:], list2, "v2w")
         v1s_both = gather(U8, t1s[:], list1, "v1s_both")
-        nc.sync.dma_start(
-            v1s_second[0 : P - PASS1_ROW, :].bitcast(I32), v1s_both[PASS1_ROW:P, :].bitcast(I32)
+        v1w = [gather(U32, t1w[0][:], list1, "v1w0")]
+        w1ss_both = lined([P, H], U8, "w1ss_both")
+        nc.vector.tensor_copy(
+            w1ss_both[:].rearrange("p (b t m) -> p b t m", b=2, t=4), w1s[:].rearrange("p (b m t) -> p b t m", b=2, t=4)
         )
-        v1s = [v1s_both, v1s_second]
-        load_rows_two_passes(w1s, w1_scales, 0)
+        w1ws = held([P, 4, 4, 256], U8, "w1ws")
+        nc.vector.tensor_copy(
+            w1ws[:].bitcast(U16), w1w[:].bitcast(U16).rearrange("p a (b m t) -> p (a b) t m", b=2, t=4)
+        )
+        v2s = gather(U8, t2s[:], list2, "v2s")
         load_words(t1w[1][:], tab_words[1])
-        nc.sync.dma_start(w5raw[:], w5.rearrange("(p j) n -> p j n", j=4))
+        lift_second_pass(v1s_second, v1s_both)
+        lift_second_pass(w1ss_second, w1ss_both)
+        v1s = [v1s_both, v1s_second]
+        w1ss = [w1ss_both, w1ss_second]
+        nc.sync.dma_start(grows[0:2, :], g1.rearrange("(b c) -> b c", b=2))
+        nc.sync.dma_start(grows[2:4, :], g2.rearrange("(b c) -> b c", b=2))
+        load_floats(w2raw[0], w2[:, 0:512])
+        load_rows(t3s, tab3_scales, 0)
+        load_words(t2w[:], tab2_words[0])
+        load_floats(w2raw[1], w2[:, 512:1024])
+        load_floats(w5raw, w5)
         nc.sync.dma_start(w4w[:].bitcast(I32), w4_words.rearrange("a p c i -> p a (c i)").bitcast(I32))
-        load_rows_two_passes(w4s, w4_scales, W4_ROW)
-        load_w3(0)
-        load_w3(1)
+        load_rows_side_by_side(w4s, w4_scales, W4_ROW)
+        for b in range(2):
+            load_floats(w3raw[b], w3[512 * b : 512 * (b + 1), :])
 
         turned = psum.tile([P, 4, P], F32, name="turned", tag="bank")
         for t in range(4):
             nc.tensor.transpose(turned[:, t, :], grows[:, t:512:4], ident[:])
-        gains = held([P, 4, 4], F32, "gains")
-        nc.scalar.copy(gains[:], turned[:, :, 0:4].rearrange("p t r -> p r t"))
+        spread = held([P, 4, 64], F32, "spread")
+        nc.scalar.copy(
+            spread[:].rearrange("p r (s t) -> p r s t", t=4),
+            turned[:, :, 0:4].rearrange("p t r -> p r t").unsqueeze(2).to_broadcast([P, 4, 16, 4]),
+        )
 
-        def products2(acc, b, t, first):
-            cols = slice(first, first + 256)
-            codes, plane = w2q[b]
-            m = slice(128 * t, 128 * (t + 1))
+        def products1(acc, b, t, cols):
+            m = slice(512 * b + 128 * t, 512 * b + 128 * (t + 1))
+            for a in (1, 0):
+                nc.tensor.matmul_mx(
+                    out=acc, lhsT=w1ws[:, 2 * a + b, t, :].bitcast(FP4X4), lhsT_scale=w1ss[a][:, m],
+                    rhs=v1w[a][:, cols].bitcast(FP8X4), rhs_scale=v1s[a][:, cols], start=(a == 1), stop=(a == 0),
+                )
+
+        def products2(acc, b, t, cols):
+            codes, plane = column_tile(w2q[b], t)
             nc.tensor.matmul_mx(
-                out=acc, lhsT=codes[:, m].bitcast(FP8X4), lhsT_scale=plane[:, m],
+                out=acc, lhsT=codes, lhsT_scale=plane,
                 rhs=v2w[:, cols].bitcast(FP8X4), rhs_scale=v2s[TAB2_ROW:P, cols], start=True, stop=True,
             )
 
-        def products1(acc, b, t, first):
-            for lo in (0, 128):
-                cols = slice(first + lo, first + lo + 128)
-                for a in (1, 0):
-                    nc.tensor.matmul_mx(
-                        out=acc[:, lo : lo + 128],
-                        lhsT=w1ws[a][:, b, t, :].bitcast(FP4X4), lhsT_scale=w1ss[:, 2 * a + b, t, :],
-                        rhs=v1w[a][:, cols].bitcast(FP8X4), rhs_scale=v1s[a][:, cols], start=(a == 1), stop=(a == 0),
-                    )
+        def cast_on_vector(name, view, *source):
+            grouped = lined([P, 1024], BF16, name)
+            nc.vector.tensor_copy(*view(grouped, *source))
+            return grouped
 
-        def sort_w1(a):
-            dst = lined([P, 2, 4, 256], U8, f"w1ws{a}")
-            nc.vector.tensor_copy(
-                dst[:].bitcast(U16),
-                w1w[:, a, :].bitcast(U16).rearrange("p (b m t) -> p b t m", b=2, t=4),
-            )
-            return dst
+        def cast_on_scalar(name, view, *source):
+            grouped = scalar_half(name)
+            nc.scalar.copy(*view(grouped, *source))
+            return grouped
 
-        w1ws = [sort_w1(0), sort_w1(1)]
-        first = hidden(0, 0, products2, gains[:, 0, :], "h2g0_0")
-        second = hidden(0, 1, products2, gains[:, 0, :], "h2g0_1")
-        w2g1 = held([P, 2048], BF16, "w2g1")
-        for half in range(2):
-            nc.scalar.copy(*sort_w2(w2g1[:, 1024 * half : 1024 * (half + 1)], 1, half))
-        h2q = [operand("h2q0")]
-        quantise(h2q[0], 0, first[:])
-        quantise(h2q[0], 1, second[:])
-        v1w = [gather(U32, t1w[0][:], list1, "v1w0")]
-        w2q.append(quantise_whole(w2g1, "w2q1"))
-        w1ss = lined([P, 4, 4, P], U8, "w1ss")
-        nc.vector.tensor_copy(
-            w1ss[:], w1s[:].rearrange("p a (b m t) -> p (a b) t m", b=2, t=4)
-        )
+        def quantise_both(parts, name):
+            codes, plane = lined([P, 512], U32, name + "_codes"), held([P, 512], U8, name + "_plane")
+            for half in range(2):
+                cols = slice(256 * half, 256 * (half + 1))
+                nc.vector.quantize_mx(out=codes[:, cols].bitcast(FP8X4), scales=plane[:, cols], in_=parts[half][:])
+            return codes, plane
+
         v1w.append(gather(U32, t1w[1][:], list1, "v1w1"))
-        first = hidden(1, 0, products2, gains[:, 1, :], "h2g1_0")
-        second = hidden(1, 1, products2, gains[:, 1, :], "h2g1_1")
-        w5g = [lined([P, 1024], BF16, "w5g_0")]
-        nc.vector.tensor_scalar(*weave(w5g[0][:], w5raw, 0), -1.0, None, ALU.mult)
-        h2q.append(operand("h2q1"))
-        quantise(h2q[1], 0, first[:])
-        quantise(h2q[1], 1, second[:])
-        first = hidden(0, 0, products1, gains[:, 2, :], "h1g0_0")
-        second = hidden(0, 1, products1, gains[:, 2, :], "h1g0_1")
-        w5g.append(ring.tile([P, 1024], BF16, name="w5g_1", tag="th", align_bytes=64))
-        nc.scalar.activation(*weave(w5g[1][:], w5raw, 1), ACT.Copy, scale=-1.0)
-        w5q = operand("w5q")
+        w2g = [cast_on_scalar("w2g0_0", sort_w2, 0, 0), cast_on_vector("w2g0_1", sort_w2, 0, 1)]
+        th = first_stage(products1, blocks(0))
+        v3s = gather(U8, t3s[:], list3, "v3s")
+        w2q = [[quantise(w2g[half][:], f"w2q0_{half}") for half in range(2)]]
+        v2w = gather(U32, t2w[:], list2, "v2w")
+        parts = gains("h1g0", "shared", th, 0)
+        th = first_stage(products1, blocks(1))
+        w2g = [cast_on_scalar("w2g1_0", sort_w2, 1, 0), cast_on_vector("w2g1_1", sort_w2, 1, 1)]
+        h1q = [quantise_both(parts, "h1q0")]
+        parts = gains("h1g1", "shared", th, 1)
+        w2q.append([quantise(w2g[half][:], f"w2q1_{half}") for half in range(2)])
+        th = first_stage(products2, blocks(0))
+        w5g = [lined([P, 1024], BF16, f"w5g_{half}") for half in range(2)]
         for half in range(2):
-            quantise(w5q, half, w5g[half][:])
-        h1q = [operand("h1q0")]
-        quantise(h1q[0], 0, first[:])
-        quantise(h1q[0], 1, second[:])
-        w3g = [[lined([P, 1024], BF16, "w3g0_0"), held([P, 1024], BF16, "w3g0_1")]]
-        nc.vector.tensor_copy(*weave(w3g[0][0][:], w3raw[0], 0))
-        first = hidden(1, 0, products1, gains[:, 3, :], "h1g1_0")
-        w3g.append([lined([P, 1024], BF16, "w3g1_0"), held([P, 1024], BF16, "w3g1_1")])
-        nc.vector.tensor_copy(*weave(w3g[1][0][:], w3raw[1], 0))
-        second = hidden(1, 1, products1, gains[:, 3, :], "h1g1_1")
-        for b in range(2):
-            nc.scalar.copy(*weave(w3g[b][1][:], w3raw[b], 1))
-        w3q = [operand("w3q0")]
-        for half in range(2):
-            quantise(w3q[0], half, w3g[0][half][:])
-        h1q.append(operand("h1q1"))
-        quantise(h1q[1], 0, first[:])
-        quantise(h1q[1], 1, second[:])
-        w3q.append(operand("w3q1"))
-        for half in range(2):
-            quantise(w3q[1], half, w3g[1][half][:])
+            nc.vector.tensor_scalar(*weave(w5g[half], w5raw, half), -1.0, None, ALU.mult)
+        w5q = [quantise(w5g[half][:], f"w5q_{half}") for half in range(2)]
+        h1q.append(quantise_both(parts, "h1q1"))
+        parts = gains("h2g0", "shared", th, 2)
+        th = first_stage(products2, blocks(1))
+        h2q = [quantise_both(parts, "h2q0")]
+        parts = gains("h2g1", "shared", th, 3)
+        w3g = [[cast_on_scalar(f"w3g0_{half}", weave, w3raw[0], half) for half in range(2)]]
+        w3g.append([cast_on_vector("w3g1_0", weave, w3raw[1], 0), cast_on_scalar("w3g1_1", weave, w3raw[1], 1)])
+        h2q.append(quantise_both(parts, "h2q1"))
+        w3q = [[quantise(w3g[b][half][:], f"w3q{b}_{half}") for half in range(2)] for b in range(2)]
 
-        def arena(acc, m, start, stop):
+        def arena(acc, n, cols, start):
+            codes, plane = column_tile(w5q, n)
             nc.tensor.matmul_mx(
-                out=acc, lhsT=w5q[0][:, m].bitcast(FP8X4), lhsT_scale=w5q[1][:, m],
-                rhs=v3w[:].bitcast(FP4X4), rhs_scale=v3s[:], start=start, stop=stop,
+                out=acc, lhsT=codes, lhsT_scale=plane,
+                rhs=v3w[:, cols].bitcast(FP4X4), rhs_scale=v3s[:, cols], start=start, stop=False,
             )
 
         y2 = staged([P, 4, S], F32, "y2", "w3raw1")
         for n in range(4):
             m = slice(128 * n, 128 * (n + 1))
-            acc = psum.tile([P, S], F32, name="acc", tag="bank")
-            arena(acc[:], m, True, False)
+            acc = psum.tile([P, S], F32, name="y2bank", tag="bank")
+            arena(acc[:], n, slice(0, S), True)
             for a in range(2):
                 nc.tensor.matmul_mx(
                     out=acc[:], lhsT=w4w[:, a, m].bitcast(FP8X4), lhsT_scale=w4s[W4_ROW:P, a, m],
@@ -279,20 +297,15 @@ def tile_list_volleyball_rally_commentary_kernel(
                 )
             nc.scalar.copy(y2[:, n, :], acc[:])
 
-        y1banks = []
+        res = staged([P, 4, S], F32, "res", "w2raw0")
         for n in range(4):
-            m = slice(128 * n, 128 * (n + 1))
-            acc = psum.tile([P, S], F32, name="acc", tag="bank")
-            arena(acc[:], m, True, False)
-            y1banks.append(acc)
-        for b in range(2):
-            for n in range(4):
-                m = slice(128 * n, 128 * (n + 1))
+            acc = psum.tile([P, S], F32, name="y1bank", tag="bank")
+            arena(acc[:], n, slice(0, S), True)
+            for b in range(2):
+                codes, plane = column_tile(w3q[b], n)
                 nc.tensor.matmul_mx(
-                    out=y1banks[n][:], lhsT=w3q[b][0][:, m].bitcast(FP8X4), lhsT_scale=w3q[b][1][:, m],
+                    out=acc[:], lhsT=codes, lhsT_scale=plane,
                     rhs=h1q[b][0][:].bitcast(FP8X4), rhs_scale=h1q[b][1][:], start=False, stop=(b == 1),
                 )
-        for n in range(4):
-            res = held([P, S], F32, f"res{n}")
-            nc.vector.tensor_tensor(res[:], y1banks[n][:], y2[:, n, :], ALU.max)
-            nc.sync.dma_start(out[128 * n : 128 * (n + 1), :], res[:])
+            nc.vector.tensor_tensor(res[:, n, :], acc[:], y2[:, n, :], ALU.max)
+            nc.sync.dma_start(out[128 * n : 128 * (n + 1), :], res[:, n, :])

@@ -273,10 +273,13 @@ def tile_list_volleyball_rally_commentary_kernel(
         th = first_stage(products2, blocks(1))
         h2q = [quantise_both(parts, "h2q0")]
         parts = gains("h2g1", "shared", th, 3)
+        h2q.append(quantise_both(parts, "h2q1"))
         w3g = [[cast_on_scalar(f"w3g0_{half}", weave, w3raw[0], half) for half in range(2)]]
         w3g.append([cast_on_vector("w3g1_0", weave, w3raw[1], 0), cast_on_scalar("w3g1_1", weave, w3raw[1], 1)])
-        h2q.append(quantise_both(parts, "h2q1"))
-        w3q = [[quantise(w3g[b][half][:], f"w3q{b}_{half}") for half in range(2)] for b in range(2)]
+        w3q = [[], []]
+        for half in range(2):
+            for b in range(2):
+                w3q[b].append(quantise(w3g[b][half][:], f"w3q{b}_{half}"))
 
         def arena(acc, n, cols, start):
             codes, plane = column_tile(w5q, n)

@@ -24,6 +24,9 @@ T1, T2, T3 = 2048, 2048, 1024
 TAB2_ROW = 4
 W4_ROW = 8
 PASS1_ROW = 16
+HALF = 1024
+VECTOR_BUFS = 26
+SCALAR_BUFS = 8
 
 
 def tile_list_volleyball_rally_commentary_kernel(
@@ -33,49 +36,28 @@ def tile_list_volleyball_rally_commentary_kernel(
     nc = tc.nc
     with ExitStack() as ctx:
         keep = ctx.enter_context(tc.tile_pool(name="keep", bufs=1))
-        line = ctx.enter_context(tc.tile_pool(name="line", bufs=32))
-        ring = ctx.enter_context(tc.tile_pool(name="ring", bufs=5))
+        vector_line = ctx.enter_context(tc.tile_pool(name="vector_line", bufs=VECTOR_BUFS))
+        scalar_line = ctx.enter_context(tc.tile_pool(name="scalar_line", bufs=SCALAR_BUFS))
         psum = ctx.enter_context(tc.psum_pool(name="psum", bufs=8))
 
-        def held(shape, dtype, name):
-            return keep.tile(shape, dtype, name=name, align_bytes=64)
+        def held(shape, dtype, name, tag=None):
+            return keep.tile(shape, dtype, name=name, tag=tag or name, align_bytes=64)
 
-        def staged(shape, dtype, name, tag):
-            return keep.tile(shape, dtype, name=name, tag=tag, align_bytes=64)
+        def for_vector(shape, dtype, name):
+            return vector_line.tile(shape, dtype, name=name, tag="line", align_bytes=64)
 
-        def lined(shape, dtype, name):
-            return line.tile(shape, dtype, name=name, tag="line", align_bytes=64)
+        def for_scalar(shape, dtype, name):
+            return scalar_line.tile(shape, dtype, name=name, tag="line", align_bytes=64)
 
-        list1 = held([P, S // 16], U16, "list1")
-        list2 = held([P, S // 16], U16, "list2")
-        list3 = held([P, S // 16], U16, "list3")
-        t1w = [held([P, T1], U32, f"t1w{a}") for a in range(2)]
-        t2w = staged([P, T2], U32, "t2w", "shared")
-        t3w = held([P, T3], U16, "t3w")
-        t1s = held([P, T1], U8, "t1s")
-        t2s = held([P, T2], U8, "t2s")
-        t3s = held([P, T3], U8, "t3s")
-        v1s_second = held([P, S], U8, "v1s_second")
-        w1w = held([P, 2, 2 * H], U8, "w1w")
-        w1s = held([P, H], U8, "w1s")
-        w1ss_second = held([P, H], U8, "w1ss_second")
-        w4w = held([P, 2, N], U32, "w4w")
-        w4s = held([P, 2, N], U8, "w4s")
-        w2raw = [staged([P, 4, 512], F32, f"w2raw{b}", f"w2raw{b}") for b in range(2)]
-        w5raw = held([P, 4, N], F32, "w5raw")
-        w3raw = [staged([P, 4, N], F32, f"w3raw{b}", f"w3raw{b}") for b in range(2)]
-        grows = held([P, 512], F32, "grows")
-        ident = held([P, P], F32, "ident")
+        def load_list(offsets, name):
+            dst = held([P, S // 16], U16, name)
+            nc.sync.dma_start(dst[:], offsets)
+            return dst
 
-        nc.gpsimd.memset(t1s[:].bitcast(I32), 0)
-        nc.vector.memset(w1s[:].bitcast(I32), 0)
-        nc.vector.memset(t3s[:].bitcast(I32), 0)
-        nc.vector.memset(t2s[:].bitcast(I32), 0)
-        nc.gpsimd.memset(grows[:], 0.0)
-        make_identity(nc, ident[:])
-        nc.gpsimd.memset(v1s_second[:].bitcast(I32), 0)
-        nc.gpsimd.memset(w1ss_second[:].bitcast(I32), 0)
-        nc.vector.memset(w4s[:].bitcast(I32), 0)
+        def cleared(shape, dtype, name, tag=None):
+            dst = held(shape, dtype, name, tag)
+            nc.vector.memset(dst[:].bitcast(I32), 0)
+            return dst
 
         def load_rows(plane, scales, row0):
             for r in range(4):
@@ -97,53 +79,74 @@ def tile_list_volleyball_rally_commentary_kernel(
         def lift_second_pass(dst, both):
             nc.sync.dma_start(dst[0 : P - PASS1_ROW, :].bitcast(I32), both[PASS1_ROW:P, :].bitcast(I32))
 
-        def load_words(dst, words):
-            nc.sync.dma_start(dst.bitcast(I32), words.rearrange("p c i -> p (c i)").bitcast(I32))
+        def load_words(words, name):
+            dst = held([P, words.shape[1]], U32, name)
+            nc.sync.dma_start(dst[:].bitcast(I32), words.rearrange("p c i -> p (c i)").bitcast(I32))
+            return dst
 
-        def load_floats(dst, rows):
+        def load_floats(rows, name):
+            dst = held([P, 4, 512], F32, name)
             nc.sync.dma_start(dst[:], rows.rearrange("(p j) n -> p j n", j=4))
+            return dst
 
         def gather(dtype, window, offsets, name):
-            picked = lined([P, S], dtype, name)
-            nc.vector.tensor_copy(picked[:], window.indirect(offsets[:]))
+            picked = for_vector([P, S], dtype, name)
+            nc.vector.tensor_copy(picked[:], window[:].indirect(offsets[:]))
             return picked
-
-        def halves(tile):
-            return tile[:, 0:1024], tile[:, 1024:2048]
 
         def quantise(grouped, name):
             words = grouped.shape[1] // 4
-            codes, plane = lined([P, words], U32, name + "_codes"), held([P, words], U8, name + "_plane")
-            nc.vector.quantize_mx(out=codes[:].bitcast(FP8X4), scales=plane[:], in_=grouped)
+            codes, plane = for_vector([P, words], U32, name + "_codes"), held([P, words], U8, name + "_plane")
+            nc.vector.quantize_mx(out=codes[:].bitcast(FP8X4), scales=plane[:], in_=grouped[:])
             return codes, plane
 
-        def window(operand, lo, hi):
-            return operand[0][:, lo:hi].bitcast(FP8X4), operand[1][:, lo:hi]
+        def column_tile(parts, k):
+            codes, plane = parts[k // 2]
+            cols = slice(128 * (k % 2), 128 * (k % 2 + 1))
+            return codes[:, cols].bitcast(FP8X4), plane[:, cols]
 
-        def sort_w2(grouped, b, half):
-            src = w2raw[b][:].rearrange("p j (m t) -> p m j t", t=4)[:, :, :, 2 * half : 2 * (half + 1)]
+        def sort_w2(grouped, raw, half):
+            src = raw[:].rearrange("p j (m t) -> p m j t", t=4)[:, :, :, 2 * half : 2 * (half + 1)]
             return grouped[:].rearrange("p (t m j) -> p m j t", t=2, j=4), src
 
         def weave(grouped, raw, half):
             src = raw[:, :, 256 * half : 256 * (half + 1)].rearrange("p j (c i) -> p c j i", i=4)
             return grouped[:].rearrange("p (c i j) -> p c j i", i=4, j=4), src
 
-        def scalar_half(name):
-            return ring.tile([P, 1024], BF16, name=name, tag="th", align_bytes=64)
+        def cast_on_vector(name, view, raw, half):
+            grouped = for_vector([P, HALF], BF16, name)
+            nc.vector.tensor_copy(*view(grouped, raw, half))
+            return grouped
 
-        def column_tile(parts, k):
-            return window(parts[k // 2], 128 * (k % 2), 128 * (k % 2 + 1))
+        def cast_on_scalar(name, view, raw, half):
+            grouped = for_scalar([P, HALF], BF16, name)
+            nc.scalar.copy(*view(grouped, raw, half))
+            return grouped
 
-        def first_stage(products, blocks):
-            th = ring.tile([P, 4, 512], F32, name="th", tag="th", align_bytes=64)
-            for u, (b, first) in enumerate(blocks):
+        def negate_on_vector(name, raw, half):
+            grouped = for_vector([P, HALF], BF16, name)
+            nc.vector.tensor_scalar(*weave(grouped, raw, half), -1.0, None, ALU.mult)
+            return grouped
+
+        def negate_on_scalar(name, raw, half):
+            grouped = for_scalar([P, HALF], BF16, name)
+            nc.scalar.activation(*weave(grouped, raw, half), ACT.Copy, scale=-1.0)
+            return grouped
+
+        def hidden():
+            return for_scalar([P, 4, 512], F32, "th")
+
+        def activate(th, u, bank):
+            nc.scalar.activation(
+                th[:, u, :].rearrange("p (s t) -> p s t", t=4), bank[:].rearrange("p t s -> p s t"), ACT.Tanh
+            )
+
+        def receiving_tanh(th, b, blocks):
+            for u in blocks:
                 bank = psum.tile([P, 4, P], F32, name="bank", tag="bank")
                 for t in range(4):
-                    products(bank[:, t, :], b, t, slice(first, first + P))
-                nc.scalar.activation(
-                    th[:, u, :].rearrange("p (s t) -> p s t", t=4), bank[:].rearrange("p t s -> p s t"), ACT.Tanh
-                )
-            return th
+                    products2(bank[:, t, :], b, t, slice(P * u, P * (u + 1)))
+                activate(th, u, bank)
 
         def gain_on_vector(grouped, th, lo, hi, row):
             nc.vector.tensor_tensor(
@@ -161,71 +164,20 @@ def tile_list_volleyball_rally_commentary_kernel(
                 ALU.mult,
             )
 
-        def blocks(b):
-            return [(b, first) for first in range(0, S, P)]
+        def gains(name, th, row):
+            wide, narrow = for_vector([P, 3 * 512], BF16, name), held([P, 512], BF16, name + "_pool", "baton")
+            gain_on_vector(wide[:], th, 0, 3, row)
+            gain_on_pool(narrow[:], th, 3, row)
+            return wide, narrow
 
-        def gains(name, tag, th, row):
-            first, shared = lined([P, 1024], BF16, name), staged([P, 1024], BF16, name + "_shared", tag)
-            gain_on_vector(first[:], th, 0, 2, row)
-            gain_on_pool(shared[:, 0:512], th, 2, row)
-            gain_on_vector(shared[:, 512:1024], th, 3, 4, row)
-            return first, shared
+        def quantise_wide(parts, name):
+            codes, plane = for_vector([P, 512], U32, name + "_codes"), held([P, 512], U8, name + "_plane")
+            nc.vector.quantize_mx(out=codes[:, 0:384].bitcast(FP8X4), scales=plane[:, 0:384], in_=parts[0][:])
+            return codes, plane
 
-        nc.sync.dma_start(list3[:], offs3)
-        nc.sync.dma_start(list1[:], offs)
-        nc.sync.dma_start(t3w[:].bitcast(I32), tab3_words[0].bitcast(I32))
-        load_rows_stacked(t1s, tab_scales)
-        load_words(t1w[0][:], tab_words[0])
-        load_rows_stacked(w1s, w1_scales)
-        nc.sync.dma_start(w1w[:].bitcast(I32), w1_words.rearrange("a p c -> p a c").bitcast(I32))
-        nc.sync.dma_start(list2[:], offs2)
-        load_rows(t2s, tab2_scales, TAB2_ROW)
-
-        v3w = gather(U16, t3w[:], list3, "v3w")
-        v1s_both = gather(U8, t1s[:], list1, "v1s_both")
-        v1w = [gather(U32, t1w[0][:], list1, "v1w0")]
-        w1ss_both = lined([P, H], U8, "w1ss_both")
-        nc.vector.tensor_copy(
-            w1ss_both[:].rearrange("p (b t m) -> p b t m", b=2, t=4), w1s[:].rearrange("p (b m t) -> p b t m", b=2, t=4)
-        )
-        w1ws = held([P, 4, 4, 256], U8, "w1ws")
-        nc.vector.tensor_copy(
-            w1ws[:].bitcast(U16), w1w[:].bitcast(U16).rearrange("p a (b m t) -> p (a b) t m", b=2, t=4)
-        )
-        v2s = gather(U8, t2s[:], list2, "v2s")
-        load_words(t1w[1][:], tab_words[1])
-        lift_second_pass(v1s_second, v1s_both)
-        lift_second_pass(w1ss_second, w1ss_both)
-        v1s = [v1s_both, v1s_second]
-        w1ss = [w1ss_both, w1ss_second]
-        nc.sync.dma_start(grows[0:2, :], g1.rearrange("(b c) -> b c", b=2))
-        nc.sync.dma_start(grows[2:4, :], g2.rearrange("(b c) -> b c", b=2))
-        load_floats(w2raw[0], w2[:, 0:512])
-        load_rows(t3s, tab3_scales, 0)
-        load_words(t2w[:], tab2_words[0])
-        load_floats(w2raw[1], w2[:, 512:1024])
-        load_floats(w5raw, w5)
-        nc.sync.dma_start(w4w[:].bitcast(I32), w4_words.rearrange("a p c i -> p a (c i)").bitcast(I32))
-        load_rows_side_by_side(w4s, w4_scales, W4_ROW)
-        for b in range(2):
-            load_floats(w3raw[b], w3[512 * b : 512 * (b + 1), :])
-
-        turned = psum.tile([P, 4, P], F32, name="turned", tag="bank")
-        for t in range(4):
-            nc.tensor.transpose(turned[:, t, :], grows[:, t:512:4], ident[:])
-        spread = held([P, 4, 64], F32, "spread")
-        nc.scalar.copy(
-            spread[:].rearrange("p r (s t) -> p r s t", t=4),
-            turned[:, :, 0:4].rearrange("p t r -> p r t").unsqueeze(2).to_broadcast([P, 4, 16, 4]),
-        )
-
-        def products1(acc, b, t, cols):
-            m = slice(512 * b + 128 * t, 512 * b + 128 * (t + 1))
-            for a in (1, 0):
-                nc.tensor.matmul_mx(
-                    out=acc, lhsT=w1ws[:, 2 * a + b, t, :].bitcast(FP4X4), lhsT_scale=w1ss[a][:, m],
-                    rhs=v1w[a][:, cols].bitcast(FP8X4), rhs_scale=v1s[a][:, cols], start=(a == 1), stop=(a == 0),
-                )
+        def quantise_narrow(parts, operand):
+            codes, plane = operand
+            nc.vector.quantize_mx(out=codes[:, 384:512].bitcast(FP8X4), scales=plane[:, 384:512], in_=parts[1][:])
 
         def products2(acc, b, t, cols):
             codes, plane = column_tile(w2q[b], t)
@@ -234,81 +186,181 @@ def tile_list_volleyball_rally_commentary_kernel(
                 rhs=v2w[:, cols].bitcast(FP8X4), rhs_scale=v2s[TAB2_ROW:P, cols], start=True, stop=True,
             )
 
-        def cast_on_vector(name, view, *source):
-            grouped = lined([P, 1024], BF16, name)
-            nc.vector.tensor_copy(*view(grouped, *source))
-            return grouped
+        def open_banks(count):
+            banks = []
+            for k in range(count):
+                b, first = k // 4, P * (k % 4)
+                banks.append(psum.tile([P, 4, P], F32, name="bank", tag="bank"))
+                serving_products(banks[k], b, first, 0)
+            return banks
 
-        def cast_on_scalar(name, view, *source):
-            grouped = scalar_half(name)
-            nc.scalar.copy(*view(grouped, *source))
-            return grouped
+        def serving_products(bank, b, first, a):
+            cols = slice(first, first + P)
+            for t in range(4):
+                m = slice(512 * b + 128 * t, 512 * b + 128 * (t + 1))
+                nc.tensor.matmul_mx(
+                    out=bank[:, t, :], lhsT=w1ws[a][:, b, t, :].bitcast(FP4X4), lhsT_scale=w1ss[a][:, m],
+                    rhs=v1w[a][:, cols].bitcast(FP8X4), rhs_scale=v1s[a][:, cols],
+                    start=(a == 0 and t == 0), stop=(a == 1 and t == 3),
+                )
 
-        def quantise_both(parts, name):
-            codes, plane = lined([P, 512], U32, name + "_codes"), held([P, 512], U8, name + "_plane")
-            for half in range(2):
-                cols = slice(256 * half, 256 * (half + 1))
-                nc.vector.quantize_mx(out=codes[:, cols].bitcast(FP8X4), scales=plane[:, cols], in_=parts[half][:])
-            return codes, plane
+        def serving_tanh(th, b, blocks):
+            for u in blocks:
+                k = 4 * b + u
+                if k == len(opened):
+                    opened.append(psum.tile([P, 4, P], F32, name="bank", tag="bank"))
+                    serving_products(opened[k], b, P * u, 0)
+                serving_products(opened[k], b, P * u, 1)
+                activate(th, u, opened[k])
 
-        v1w.append(gather(U32, t1w[1][:], list1, "v1w1"))
-        w2g = [cast_on_scalar("w2g0_0", sort_w2, 0, 0), cast_on_vector("w2g0_1", sort_w2, 0, 1)]
-        th = first_stage(products1, blocks(0))
-        v3s = gather(U8, t3s[:], list3, "v3s")
-        w2q = [[quantise(w2g[half][:], f"w2q0_{half}") for half in range(2)]]
-        v2w = gather(U32, t2w[:], list2, "v2w")
-        parts = gains("h1g0", "shared", th, 0)
-        th = first_stage(products1, blocks(1))
-        w2g = [cast_on_scalar("w2g1_0", sort_w2, 1, 0), cast_on_vector("w2g1_1", sort_w2, 1, 1)]
-        h1q = [quantise_both(parts, "h1q0")]
-        parts = gains("h1g1", "shared", th, 1)
-        w2q.append([quantise(w2g[half][:], f"w2q1_{half}") for half in range(2)])
-        th = first_stage(products2, blocks(0))
-        w5g = [lined([P, 1024], BF16, f"w5g_{half}") for half in range(2)]
-        for half in range(2):
-            nc.vector.tensor_scalar(*weave(w5g[half], w5raw, half), -1.0, None, ALU.mult)
-        w5q = [quantise(w5g[half][:], f"w5q_{half}") for half in range(2)]
-        h1q.append(quantise_both(parts, "h1q1"))
-        parts = gains("h2g0", "shared", th, 2)
-        th = first_stage(products2, blocks(1))
-        h2q = [quantise_both(parts, "h2q0")]
-        parts = gains("h2g1", "shared", th, 3)
-        h2q.append(quantise_both(parts, "h2q1"))
-        w3g = [[cast_on_scalar(f"w3g0_{half}", weave, w3raw[0], half) for half in range(2)]]
-        w3g.append([cast_on_vector("w3g1_0", weave, w3raw[1], 0), cast_on_scalar("w3g1_1", weave, w3raw[1], 1)])
-        w3q = [[], []]
-        for half in range(2):
-            for b in range(2):
-                w3q[b].append(quantise(w3g[b][half][:], f"w3q{b}_{half}"))
+        def sort_w1_scales(a):
+            ordered = for_vector([P, H], U8, f"w1ss{a}")
+            nc.vector.tensor_copy(
+                ordered[:].rearrange("p (b t m) -> p b t m", b=2, t=4),
+                w1s[:, a, :].rearrange("p (b m t) -> p b t m", b=2, t=4),
+            )
+            return ordered
 
-        def arena(acc, n, cols, start):
+        def sort_w1_words(a):
+            ordered = for_scalar([P, 2, 4, 256], U8, f"w1ws{a}")
+            nc.scalar.copy(
+                ordered[:].bitcast(U16), w1w[:, a, :].bitcast(U16).rearrange("p (b m t) -> p b t m", b=2, t=4)
+            )
+            return ordered
+
+        def arena(acc, n):
             codes, plane = column_tile(w5q, n)
             nc.tensor.matmul_mx(
-                out=acc, lhsT=codes, lhsT_scale=plane,
-                rhs=v3w[:, cols].bitcast(FP4X4), rhs_scale=v3s[:, cols], start=start, stop=False,
+                out=acc[:], lhsT=codes, lhsT_scale=plane,
+                rhs=v3w[:].bitcast(FP4X4), rhs_scale=v3s[:], start=True, stop=False,
             )
 
-        y2 = staged([P, 4, S], F32, "y2", "w3raw1")
-        for n in range(4):
+        def receiving(n):
             m = slice(128 * n, 128 * (n + 1))
             acc = psum.tile([P, S], F32, name="y2bank", tag="bank")
-            arena(acc[:], n, slice(0, S), True)
+            arena(acc, n)
             for a in range(2):
                 nc.tensor.matmul_mx(
                     out=acc[:], lhsT=w4w[:, a, m].bitcast(FP8X4), lhsT_scale=w4s[W4_ROW:P, a, m],
                     rhs=h2q[a][0][:].bitcast(FP8X4), rhs_scale=h2q[a][1][:], start=False, stop=(a == 1),
                 )
-            nc.scalar.copy(y2[:, n, :], acc[:])
+            y2 = for_scalar([P, S], F32, f"y2_{n}")
+            nc.scalar.copy(y2[:], acc[:])
+            return y2
 
-        res = staged([P, 4, S], F32, "res", "w2raw0")
+        def serving_pass(acc, n, b):
+            codes, plane = column_tile(w3q[b], n)
+            nc.tensor.matmul_mx(
+                out=acc[:], lhsT=codes, lhsT_scale=plane,
+                rhs=h1q[b][0][:].bitcast(FP8X4), rhs_scale=h1q[b][1][:], start=False, stop=(b == 1),
+            )
+
+        def finish(acc, n):
+            res = for_vector([P, S], F32, f"res{n}")
+            nc.vector.tensor_tensor(res[:], acc[:], y2[n][:], ALU.max)
+            nc.sync.dma_start(out[128 * n : 128 * (n + 1), :], res[:])
+
+        t3s = cleared([P, T3], U8, "t3s")
+        grows = held([P, 512], F32, "grows")
+        nc.vector.memset(grows[:], 0.0)
+        t2s = cleared([P, T2], U8, "t2s")
+        t1s = cleared([P, T1], U8, "t1s")
+        w1s = cleared([P, H], U8, "w1s", "baton")
+        w4s = cleared([P, 2, N], U8, "w4s")
+        v1s_second = cleared([P, S], U8, "v1s_second")
+        w1ss_second = cleared([P, H], U8, "w1ss_second")
+        nc.gpsimd.dma_start(grows[0:2, :], g1.rearrange("(b c) -> b c", b=2))
+        nc.gpsimd.dma_start(grows[2:4, :], g2.rearrange("(b c) -> b c", b=2))
+        ident = held([P, P], F32, "ident")
+        make_identity(nc, ident[:])
+
+        list3 = load_list(offs3, "list3")
+        t3w = held([P, T3], U16, "t3w")
+        nc.sync.dma_start(t3w[:].bitcast(I32), tab3_words[0].bitcast(I32))
+        load_rows(t3s, tab3_scales, 0)
+        w2raw = [load_floats(w2[:, 0:512], "w2raw0")]
+        list2 = load_list(offs2, "list2")
+        load_rows(t2s, tab2_scales, TAB2_ROW)
+        t2w = load_words(tab2_words[0], "t2w")
+        list1 = load_list(offs, "list1")
+        load_rows_stacked(t1s, tab_scales)
+        w2raw.append(load_floats(w2[:, 512:1024], "w2raw1"))
+        load_rows_stacked(w1s, w1_scales)
+        w1w = held([P, 2, 2 * H], U8, "w1w")
+        nc.sync.dma_start(w1w[:].bitcast(I32), w1_words.rearrange("a p c -> p a c").bitcast(I32))
+        t1w = [load_words(tab_words[a], f"t1w{a}") for a in range(2)]
+
+        v3w = gather(U16, t3w, list3, "v3w")
+        v3s = gather(U8, t3s, list3, "v3s")
+        w2g = [cast_on_vector("w2g0_0", sort_w2, w2raw[0], 0), cast_on_scalar("w2g0_1", sort_w2, w2raw[0], 1)]
+        turned = psum.tile([P, 4, P], F32, name="turned", tag="bank")
+        for t in range(4):
+            nc.tensor.transpose(turned[:, t, :], grows[:, t:512:4], ident[:])
+        spread = for_scalar([P, 4, 64], F32, "spread")
+        nc.scalar.copy(
+            spread[:].rearrange("p r (s t) -> p r s t", t=4),
+            turned[:, :, 0:4].rearrange("p t r -> p r t").unsqueeze(2).to_broadcast([P, 4, 16, 4]),
+        )
+        v2s = gather(U8, t2s, list2, "v2s")
+        w2q = [[quantise(w2g[half], f"w2q0_{half}") for half in range(2)]]
+        v2w = gather(U32, t2w, list2, "v2w")
+        v1s_both = gather(U8, t1s, list1, "v1s_both")
+        lift_second_pass(v1s_second, v1s_both)
+        th = hidden()
+        receiving_tanh(th, 0, range(4))
+        w2g = [cast_on_vector(f"w2g1_{half}", sort_w2, w2raw[1], half) for half in range(2)]
+        w2q.append([quantise(w2g[half], f"w2q1_{half}") for half in range(2)])
+        w1ss_both = for_vector([P, H], U8, "w1ss_both")
+        nc.vector.tensor_copy(
+            w1ss_both[:].rearrange("p (b t m) -> p b t m", b=2, t=4), w1s[:].rearrange("p (b m t) -> p b t m", b=2, t=4)
+        )
+        lift_second_pass(w1ss_second, w1ss_both)
+        v1s = [v1s_both, v1s_second]
+        w1ss = [w1ss_both, w1ss_second]
+        w5raw = load_floats(w5, "w5raw")
+        load_rows_side_by_side(w4s, w4_scales, W4_ROW)
+        w4w = held([P, 2, N], U32, "w4w")
+        nc.sync.dma_start(w4w[:].bitcast(I32), w4_words.rearrange("a p c i -> p a (c i)").bitcast(I32))
+        w3raw = [load_floats(w3[512 * b : 512 * (b + 1), :], f"w3raw{b}") for b in range(2)]
+
+        parts = gains("h2g0", th, 2)
+        w1ws = [sort_w1_words(0)]
+        th = hidden()
+        receiving_tanh(th, 1, range(4))
+        w1ws.append(sort_w1_words(1))
+        v1w = [gather(U32, t1w[0], list1, "v1w0")]
+        h2q = [quantise_wide(parts, "h2q0")]
+        opened = open_banks(3)
+        v1w.append(gather(U32, t1w[1], list1, "v1w1"))
+        quantise_narrow(parts, h2q[0])
+        parts = gains("h2g1", th, 3)
+        th = hidden()
+        serving_tanh(th, 0, range(4))
+        w5g = [negate_on_vector("w5g_0", w5raw, 0), negate_on_scalar("w5g_1", w5raw, 1)]
+        h2q.append(quantise_wide(parts, "h2q1"))
+        quantise_narrow(parts, h2q[1])
+        parts = gains("h1g0", th, 0)
+        th = hidden()
+        serving_tanh(th, 1, range(4))
+        w5q = [quantise(w5g[half], f"w5q_{half}") for half in range(2)]
+        h1q = [quantise_wide(parts, "h1q0")]
+        quantise_narrow(parts, h1q[0])
+        w3g = [[cast_on_scalar(f"w3g0_{half}", weave, w3raw[0], half) for half in range(2)]]
+        parts = gains("h1g1", th, 1)
+        y2 = [receiving(0)]
+        w3g.append([cast_on_vector("w3g1_0", weave, w3raw[1], 0), cast_on_scalar("w3g1_1", weave, w3raw[1], 1)])
+        y2.extend(receiving(n) for n in range(1, 4))
+        h1q.append(quantise_wide(parts, "h1q1"))
+        quantise_narrow(parts, h1q[1])
+        acc1 = []
         for n in range(4):
-            acc = psum.tile([P, S], F32, name="y1bank", tag="bank")
-            arena(acc[:], n, slice(0, S), True)
-            for b in range(2):
-                codes, plane = column_tile(w3q[b], n)
-                nc.tensor.matmul_mx(
-                    out=acc[:], lhsT=codes, lhsT_scale=plane,
-                    rhs=h1q[b][0][:].bitcast(FP8X4), rhs_scale=h1q[b][1][:], start=False, stop=(b == 1),
-                )
-            nc.vector.tensor_tensor(res[:, n, :], acc[:], y2[:, n, :], ALU.max)
-            nc.sync.dma_start(out[128 * n : 128 * (n + 1), :], res[:, n, :])
+            acc1.append(psum.tile([P, S], F32, name="y1bank", tag="bank"))
+            arena(acc1[n], n)
+        w3q = [[quantise(w3g[b][0], f"w3q{b}_0")] for b in range(2)]
+        w3q[0].append(quantise(w3g[0][1], "w3q0_1"))
+        for n in range(4):
+            if n == 1:
+                w3q[1].append(quantise(w3g[1][1], "w3q1_1"))
+            serving_pass(acc1[n], n, 0)
+            serving_pass(acc1[n], n, 1)
+            finish(acc1[n], n)

@@ -191,27 +191,30 @@ def tile_list_volleyball_rally_commentary_kernel(
             for k in range(count):
                 b, first = k // 4, P * (k % 4)
                 banks.append(psum.tile([P, 4, P], F32, name="bank", tag="bank"))
-                serving_products(banks[k], b, first, 0)
+                serving_products(banks[k], b, first, 0, True)
             return banks
 
-        def serving_products(bank, b, first, a):
+        def serving_products(bank, b, first, a, opens):
             cols = slice(first, first + P)
             for t in range(4):
                 m = slice(512 * b + 128 * t, 512 * b + 128 * (t + 1))
                 nc.tensor.matmul_mx(
                     out=bank[:, t, :], lhsT=w1ws[a][:, b, t, :].bitcast(FP4X4), lhsT_scale=w1ss[a][:, m],
                     rhs=v1w[a][:, cols].bitcast(FP8X4), rhs_scale=v1s[a][:, cols],
-                    start=(a == 0 and t == 0), stop=(a == 1 and t == 3),
+                    start=(opens and t == 0), stop=(not opens and t == 3),
                 )
 
         def serving_tanh(th, b, blocks):
             for u in blocks:
                 k = 4 * b + u
-                if k == len(opened):
-                    opened.append(psum.tile([P, 4, P], F32, name="bank", tag="bank"))
-                    serving_products(opened[k], b, P * u, 0)
-                serving_products(opened[k], b, P * u, 1)
-                activate(th, u, opened[k])
+                if k < len(opened):
+                    bank = opened[k]
+                    serving_products(bank, b, P * u, 1, False)
+                else:
+                    bank = psum.tile([P, 4, P], F32, name="bank", tag="bank")
+                    serving_products(bank, b, P * u, 1, True)
+                    serving_products(bank, b, P * u, 0, False)
+                activate(th, u, bank)
 
         def sort_w1_scales(a):
             ordered = for_vector([P, H], U8, f"w1ss{a}")
@@ -260,6 +263,8 @@ def tile_list_volleyball_rally_commentary_kernel(
             nc.vector.tensor_tensor(res[:], acc[:], y2[n][:], ALU.max)
             nc.sync.dma_start(out[128 * n : 128 * (n + 1), :], res[:])
 
+        ident = held([P, P], F32, "ident")
+        make_identity(nc, ident[:])
         t3s = cleared([P, T3], U8, "t3s")
         grows = held([P, 512], F32, "grows")
         nc.vector.memset(grows[:], 0.0)
@@ -271,8 +276,6 @@ def tile_list_volleyball_rally_commentary_kernel(
         w1ss_second = cleared([P, H], U8, "w1ss_second")
         nc.gpsimd.dma_start(grows[0:2, :], g1.rearrange("(b c) -> b c", b=2))
         nc.gpsimd.dma_start(grows[2:4, :], g2.rearrange("(b c) -> b c", b=2))
-        ident = held([P, P], F32, "ident")
-        make_identity(nc, ident[:])
 
         list3 = load_list(offs3, "list3")
         t3w = held([P, T3], U16, "t3w")

@@ -25,7 +25,7 @@ TAB2_ROW = 4
 W4_ROW = 8
 PASS1_ROW = 16
 HALF = 1024
-VECTOR_BUFS = 26
+VECTOR_BUFS = 25
 SCALAR_BUFS = 8
 
 
@@ -79,8 +79,8 @@ def tile_list_volleyball_rally_commentary_kernel(
         def lift_second_pass(dst, both):
             nc.sync.dma_start(dst[0 : P - PASS1_ROW, :].bitcast(I32), both[PASS1_ROW:P, :].bitcast(I32))
 
-        def load_words(words, name):
-            dst = held([P, words.shape[1]], U32, name)
+        def load_words(words, name, tag=None):
+            dst = held([P, words.shape[1]], U32, name, tag)
             nc.sync.dma_start(dst[:].bitcast(I32), words.rearrange("p c i -> p (c i)").bitcast(I32))
             return dst
 
@@ -94,43 +94,46 @@ def tile_list_volleyball_rally_commentary_kernel(
             nc.vector.tensor_copy(picked[:], window[:].indirect(offsets[:]))
             return picked
 
+        def gather_in_halves(dtype, window, offsets, name):
+            picked = for_vector([P, S], dtype, name)
+            for half in range(2):
+                nc.vector.tensor_copy(
+                    picked[:, 256 * half : 256 * (half + 1)], window[:].indirect(offsets[:, 16 * half : 16 * (half + 1)])
+                )
+            return picked
+
         def quantise(grouped, name):
             words = grouped.shape[1] // 4
             codes, plane = for_vector([P, words], U32, name + "_codes"), held([P, words], U8, name + "_plane")
             nc.vector.quantize_mx(out=codes[:].bitcast(FP8X4), scales=plane[:], in_=grouped[:])
-            return codes, plane
+            return [(codes[:, c : c + P].bitcast(FP8X4), plane[:, c : c + P]) for c in range(0, words, P)]
 
-        def column_tile(parts, k):
-            codes, plane = parts[k // 2]
-            cols = slice(128 * (k % 2), 128 * (k % 2 + 1))
-            return codes[:, cols].bitcast(FP8X4), plane[:, cols]
+        def sort_w2(grouped, raw, lo, hi):
+            src = raw[:].rearrange("p j (m t) -> p m j t", t=4)[:, :, :, lo:hi]
+            return grouped[:].rearrange("p (t m j) -> p m j t", t=hi - lo, j=4), src
 
-        def sort_w2(grouped, raw, half):
-            src = raw[:].rearrange("p j (m t) -> p m j t", t=4)[:, :, :, 2 * half : 2 * (half + 1)]
-            return grouped[:].rearrange("p (t m j) -> p m j t", t=2, j=4), src
-
-        def weave(grouped, raw, half):
-            src = raw[:, :, 256 * half : 256 * (half + 1)].rearrange("p j (c i) -> p c j i", i=4)
+        def weave(grouped, raw, lo, hi):
+            src = raw[:, :, P * lo : P * hi].rearrange("p j (c i) -> p c j i", i=4)
             return grouped[:].rearrange("p (c i j) -> p c j i", i=4, j=4), src
 
-        def cast_on_vector(name, view, raw, half):
-            grouped = for_vector([P, HALF], BF16, name)
-            nc.vector.tensor_copy(*view(grouped, raw, half))
+        def cast_on_vector(name, view, raw, lo, hi):
+            grouped = for_vector([P, 512 * (hi - lo)], BF16, name)
+            nc.vector.tensor_copy(*view(grouped, raw, lo, hi))
             return grouped
 
-        def cast_on_scalar(name, view, raw, half):
-            grouped = for_scalar([P, HALF], BF16, name)
-            nc.scalar.copy(*view(grouped, raw, half))
+        def cast_on_scalar(name, view, raw, lo, hi):
+            grouped = for_scalar([P, 512 * (hi - lo)], BF16, name)
+            nc.scalar.copy(*view(grouped, raw, lo, hi))
             return grouped
 
-        def negate_on_vector(name, raw, half):
-            grouped = for_vector([P, HALF], BF16, name)
-            nc.vector.tensor_scalar(*weave(grouped, raw, half), -1.0, None, ALU.mult)
+        def negate_on_vector(name, raw, lo, hi):
+            grouped = for_vector([P, 512 * (hi - lo)], BF16, name)
+            nc.vector.tensor_scalar(*weave(grouped, raw, lo, hi), -1.0, None, ALU.mult)
             return grouped
 
-        def negate_on_scalar(name, raw, half):
-            grouped = for_scalar([P, HALF], BF16, name)
-            nc.scalar.activation(*weave(grouped, raw, half), ACT.Copy, scale=-1.0)
+        def negate_on_scalar(name, raw, lo, hi):
+            grouped = for_scalar([P, 512 * (hi - lo)], BF16, name)
+            nc.scalar.activation(*weave(grouped, raw, lo, hi), ACT.Copy, scale=-1.0)
             return grouped
 
         def hidden():
@@ -180,7 +183,7 @@ def tile_list_volleyball_rally_commentary_kernel(
             nc.vector.quantize_mx(out=codes[:, 384:512].bitcast(FP8X4), scales=plane[:, 384:512], in_=parts[1][:])
 
         def products2(acc, b, t, cols):
-            codes, plane = column_tile(w2q[b], t)
+            codes, plane = w2q[b][t]
             nc.tensor.matmul_mx(
                 out=acc, lhsT=codes, lhsT_scale=plane,
                 rhs=v2w[:, cols].bitcast(FP8X4), rhs_scale=v2s[TAB2_ROW:P, cols], start=True, stop=True,
@@ -199,7 +202,7 @@ def tile_list_volleyball_rally_commentary_kernel(
             for t in range(4):
                 m = slice(512 * b + 128 * t, 512 * b + 128 * (t + 1))
                 nc.tensor.matmul_mx(
-                    out=bank[:, t, :], lhsT=w1ws[a][:, b, t, :].bitcast(FP4X4), lhsT_scale=w1ss[a][:, m],
+                    out=bank[:, t, :], lhsT=w1ws[a][b][:, t, :].bitcast(FP4X4), lhsT_scale=w1ss[a][:, m],
                     rhs=v1w[a][:, cols].bitcast(FP8X4), rhs_scale=v1s[a][:, cols],
                     start=(opens and t == 0), stop=(not opens and t == 3),
                 )
@@ -224,15 +227,16 @@ def tile_list_volleyball_rally_commentary_kernel(
             )
             return ordered
 
-        def sort_w1_words(a):
-            ordered = for_scalar([P, 2, 4, 256], U8, f"w1ws{a}")
+        def sort_w1_words(a, blocks):
+            ordered = for_scalar([P, len(blocks), 4, 256], U8, f"w1ws{a}")
+            lo, hi = 512 * blocks[0], 512 * (blocks[-1] + 1)
             nc.scalar.copy(
-                ordered[:].bitcast(U16), w1w[:, a, :].bitcast(U16).rearrange("p (b m t) -> p b t m", b=2, t=4)
+                ordered[:].bitcast(U16), w1w[a].bitcast(U16)[:, lo:hi].rearrange("p (b m t) -> p b t m", m=128, t=4)
             )
-            return ordered
+            return [ordered[:, k, :, :] for k in range(len(blocks))]
 
         def arena(acc, n):
-            codes, plane = column_tile(w5q, n)
+            codes, plane = w5q[n]
             nc.tensor.matmul_mx(
                 out=acc[:], lhsT=codes, lhsT_scale=plane,
                 rhs=v3w[:].bitcast(FP4X4), rhs_scale=v3s[:], start=True, stop=False,
@@ -252,25 +256,27 @@ def tile_list_volleyball_rally_commentary_kernel(
             return y2
 
         def serving_pass(acc, n, b):
-            codes, plane = column_tile(w3q[b], n)
+            codes, plane = w3q[b][n]
             nc.tensor.matmul_mx(
                 out=acc[:], lhsT=codes, lhsT_scale=plane,
                 rhs=h1q[b][0][:].bitcast(FP8X4), rhs_scale=h1q[b][1][:], start=False, stop=(b == 1),
             )
 
-        def finish(acc, n):
-            res = for_vector([P, S], F32, f"res{n}")
-            nc.vector.tensor_tensor(res[:], acc[:], y2[n][:], ALU.max)
-            nc.sync.dma_start(out[128 * n : 128 * (n + 1), :], res[:])
+        def finish(acc, n, pieces):
+            for lo, hi in pieces:
+                res = for_vector([P, hi - lo], F32, f"res{n}")
+                nc.vector.tensor_tensor(res[:], acc[:, lo:hi], y2[n][:, lo:hi], ALU.max)
+                nc.sync.dma_start(out[128 * n : 128 * (n + 1), lo:hi], res[:])
 
+        t3s = held([P, T3], U8, "t3s")
+        nc.gpsimd.memset(t3s[:].bitcast(I32), 0)
         ident = held([P, P], F32, "ident")
         make_identity(nc, ident[:])
-        t3s = cleared([P, T3], U8, "t3s")
         grows = held([P, 512], F32, "grows")
         nc.vector.memset(grows[:], 0.0)
         t2s = cleared([P, T2], U8, "t2s")
         t1s = cleared([P, T1], U8, "t1s")
-        w1s = cleared([P, H], U8, "w1s", "baton")
+        w1s = cleared([P, H], U8, "w1s")
         w4s = cleared([P, 2, N], U8, "w4s")
         v1s_second = cleared([P, S], U8, "v1s_second")
         w1ss_second = cleared([P, H], U8, "w1ss_second")
@@ -289,13 +295,14 @@ def tile_list_volleyball_rally_commentary_kernel(
         load_rows_stacked(t1s, tab_scales)
         w2raw.append(load_floats(w2[:, 512:1024], "w2raw1"))
         load_rows_stacked(w1s, w1_scales)
-        w1w = held([P, 2, 2 * H], U8, "w1w")
-        nc.sync.dma_start(w1w[:].bitcast(I32), w1_words.rearrange("a p c -> p a c").bitcast(I32))
+        w1w_both = held([P, 2, 2 * H], U8, "w1w")
+        nc.sync.dma_start(w1w_both[:].bitcast(I32), w1_words.rearrange("a p c -> p a c").bitcast(I32))
+        w1w = [w1w_both[:, a, :] for a in range(2)]
         t1w = [load_words(tab_words[a], f"t1w{a}") for a in range(2)]
 
         v3w = gather(U16, t3w, list3, "v3w")
         v3s = gather(U8, t3s, list3, "v3s")
-        w2g = [cast_on_vector("w2g0_0", sort_w2, w2raw[0], 0), cast_on_scalar("w2g0_1", sort_w2, w2raw[0], 1)]
+        w2g = [cast_on_vector("w2g0_0", sort_w2, w2raw[0], 0, 2), cast_on_scalar("w2g0_1", sort_w2, w2raw[0], 2, 4)]
         turned = psum.tile([P, 4, P], F32, name="turned", tag="bank")
         for t in range(4):
             nc.tensor.transpose(turned[:, t, :], grows[:, t:512:4], ident[:])
@@ -305,18 +312,19 @@ def tile_list_volleyball_rally_commentary_kernel(
             turned[:, :, 0:4].rearrange("p t r -> p r t").unsqueeze(2).to_broadcast([P, 4, 16, 4]),
         )
         v2s = gather(U8, t2s, list2, "v2s")
-        w2q = [[quantise(w2g[half], f"w2q0_{half}") for half in range(2)]]
+        w2q = [quantise(w2g[0], "w2q0_0") + quantise(w2g[1], "w2q0_1")]
         v2w = gather(U32, t2w, list2, "v2w")
         v1s_both = gather(U8, t1s, list1, "v1s_both")
         lift_second_pass(v1s_second, v1s_both)
         th = hidden()
         receiving_tanh(th, 0, range(4))
-        w2g = [cast_on_vector(f"w2g1_{half}", sort_w2, w2raw[1], half) for half in range(2)]
-        w2q.append([quantise(w2g[half], f"w2q1_{half}") for half in range(2)])
+        w2g = held([P, 2048], BF16, "w2g1", "baton")
+        nc.vector.tensor_copy(*sort_w2(w2g, w2raw[1], 0, 4))
         w1ss_both = for_vector([P, H], U8, "w1ss_both")
         nc.vector.tensor_copy(
             w1ss_both[:].rearrange("p (b t m) -> p b t m", b=2, t=4), w1s[:].rearrange("p (b m t) -> p b t m", b=2, t=4)
         )
+        w2q.append(quantise(w2g, "w2q1"))
         lift_second_pass(w1ss_second, w1ss_both)
         v1s = [v1s_both, v1s_second]
         w1ss = [w1ss_both, w1ss_second]
@@ -327,43 +335,41 @@ def tile_list_volleyball_rally_commentary_kernel(
         w3raw = [load_floats(w3[512 * b : 512 * (b + 1), :], f"w3raw{b}") for b in range(2)]
 
         parts = gains("h2g0", th, 2)
-        w1ws = [sort_w1_words(0)]
+        w1ws = [sort_w1_words(a, [0, 1]) for a in range(2)]
         th = hidden()
         receiving_tanh(th, 1, range(4))
-        w1ws.append(sort_w1_words(1))
         v1w = [gather(U32, t1w[0], list1, "v1w0")]
-        h2q = [quantise_wide(parts, "h2q0")]
         opened = open_banks(3)
-        v1w.append(gather(U32, t1w[1], list1, "v1w1"))
+        h2q = [quantise_wide(parts, "h2q0")]
+        v1w.append(gather_in_halves(U32, t1w[1], list1, "v1w1"))
         quantise_narrow(parts, h2q[0])
         parts = gains("h2g1", th, 3)
         th = hidden()
         serving_tanh(th, 0, range(4))
-        w5g = [negate_on_vector("w5g_0", w5raw, 0), negate_on_scalar("w5g_1", w5raw, 1)]
+        w5g = [negate_on_vector("w5g_0", w5raw, 0, 2), negate_on_scalar("w5g_1", w5raw, 2, 4)]
         h2q.append(quantise_wide(parts, "h2q1"))
         quantise_narrow(parts, h2q[1])
         parts = gains("h1g0", th, 0)
         th = hidden()
         serving_tanh(th, 1, range(4))
-        w5q = [quantise(w5g[half], f"w5q_{half}") for half in range(2)]
+        w5q = quantise(w5g[0], "w5q_0") + quantise(w5g[1], "w5q_1")
         h1q = [quantise_wide(parts, "h1q0")]
         quantise_narrow(parts, h1q[0])
-        w3g = [[cast_on_scalar(f"w3g0_{half}", weave, w3raw[0], half) for half in range(2)]]
+        w3g = [[cast_on_scalar(f"w3g0_{half}", weave, w3raw[0], 2 * half, 2 * half + 2) for half in range(2)]]
         parts = gains("h1g1", th, 1)
-        y2 = [receiving(0)]
-        w3g.append([cast_on_vector("w3g1_0", weave, w3raw[1], 0), cast_on_scalar("w3g1_1", weave, w3raw[1], 1)])
-        y2.extend(receiving(n) for n in range(1, 4))
+        w3q = [quantise(w3g[0][0], "w3q0_0")]
+        w3g.append([cast_on_vector("w3g1_0", weave, w3raw[1], 0, 2), cast_on_scalar("w3g1_1", weave, w3raw[1], 2, 4)])
+        y2 = [receiving(n) for n in range(4)]
         h1q.append(quantise_wide(parts, "h1q1"))
         quantise_narrow(parts, h1q[1])
+        w3q.append(quantise(w3g[1][0], "w3q1_0"))
+        for b in range(2):
+            w3q[b].extend(quantise(w3g[b][1], f"w3q{b}_1"))
         acc1 = []
         for n in range(4):
             acc1.append(psum.tile([P, S], F32, name="y1bank", tag="bank"))
             arena(acc1[n], n)
-        w3q = [[quantise(w3g[b][0], f"w3q{b}_0")] for b in range(2)]
-        w3q[0].append(quantise(w3g[0][1], "w3q0_1"))
         for n in range(4):
-            if n == 1:
-                w3q[1].append(quantise(w3g[1][1], "w3q1_1"))
             serving_pass(acc1[n], n, 0)
             serving_pass(acc1[n], n, 1)
-            finish(acc1[n], n)
+            finish(acc1[n], n, [(0, S)])

@@ -21,7 +21,6 @@ S = 512
 N = 512
 H = 1024
 T1, T2, T3 = 2048, 2048, 1024
-TAB2_ROW = 4
 W4_ROW = 8
 PASS1_ROW = 16
 HALF = 1024
@@ -59,10 +58,6 @@ def tile_list_volleyball_rally_commentary_kernel(
             nc.vector.memset(dst[:].bitcast(I32), 0)
             return dst
 
-        def load_rows(plane, scales, row0):
-            for r in range(4):
-                nc.sync.dma_start(plane[row0 + r : P : 32, :].bitcast(I32), scales[0, r:16:4, :].bitcast(I32))
-
         def load_rows_side_by_side(plane, scales, row0):
             for r in range(4):
                 nc.sync.dma_start(
@@ -75,6 +70,15 @@ def tile_list_volleyball_rally_commentary_kernel(
                 nc.sync.dma_start(
                     plane[r:P:PASS1_ROW, :].bitcast(I32), scales.rearrange("a (q r) c -> r q a c", r=4)[r].bitcast(I32)
                 )
+
+        def load_rows_apart(plane, scales):
+            rows = scales.rearrange("a q c -> (a q) c")
+            nc.sync.dma_start(plane[0 : P : P // rows.shape[0], :].bitcast(I32), rows.bitcast(I32))
+
+        def carry_rows(plane, picked, first, apart):
+            for r in range(4):
+                src = picked[first + apart * r : first + 16 * apart : 4 * apart, :]
+                nc.sync.dma_start(plane[r:P:32, :].bitcast(I32), src.bitcast(I32))
 
         def lift_second_pass(dst, both):
             nc.sync.dma_start(dst[0 : P - PASS1_ROW, :].bitcast(I32), both[PASS1_ROW:P, :].bitcast(I32))
@@ -186,7 +190,7 @@ def tile_list_volleyball_rally_commentary_kernel(
             codes, plane = w2q[b][t]
             nc.tensor.matmul_mx(
                 out=acc, lhsT=codes, lhsT_scale=plane,
-                rhs=v2w[:, cols].bitcast(FP8X4), rhs_scale=v2s[TAB2_ROW:P, cols], start=True, stop=True,
+                rhs=v2w[:, cols].bitcast(FP8X4), rhs_scale=v2s[:, cols], start=True, stop=True,
             )
 
         def open_banks(count):
@@ -268,40 +272,43 @@ def tile_list_volleyball_rally_commentary_kernel(
                 nc.vector.tensor_tensor(res[:], acc[:, lo:hi], y2[n][:, lo:hi], ALU.max)
                 nc.sync.dma_start(out[128 * n : 128 * (n + 1), lo:hi], res[:])
 
-        t3s = held([P, T3], U8, "t3s")
-        nc.gpsimd.memset(t3s[:].bitcast(I32), 0)
+        t2s = cleared([P, T2], U8, "t2s")
+        t3s = cleared([P, T3], U8, "t3s")
         ident = held([P, P], F32, "ident")
         make_identity(nc, ident[:])
         grows = held([P, 512], F32, "grows")
         nc.vector.memset(grows[:], 0.0)
-        t2s = cleared([P, T2], U8, "t2s")
         t1s = cleared([P, T1], U8, "t1s")
+        v2s = cleared([P, S], U8, "v2s")
         w1s = cleared([P, H], U8, "w1s")
+        v1s = [cleared([P, S], U8, f"v1s{a}") for a in range(2)]
+        v3s = cleared([P, S], U8, "v3s")
         w4s = cleared([P, 2, N], U8, "w4s")
-        v1s_second = cleared([P, S], U8, "v1s_second")
         w1ss_second = cleared([P, H], U8, "w1ss_second")
         nc.gpsimd.dma_start(grows[0:2, :], g1.rearrange("(b c) -> b c", b=2))
         nc.gpsimd.dma_start(grows[2:4, :], g2.rearrange("(b c) -> b c", b=2))
 
-        list3 = load_list(offs3, "list3")
         t3w = held([P, T3], U16, "t3w")
         nc.sync.dma_start(t3w[:].bitcast(I32), tab3_words[0].bitcast(I32))
-        load_rows(t3s, tab3_scales, 0)
-        w2raw = [load_floats(w2[:, 0:512], "w2raw0")]
         list2 = load_list(offs2, "list2")
-        load_rows(t2s, tab2_scales, TAB2_ROW)
+        list3 = load_list(offs3, "list3")
+        load_rows_apart(t2s, tab2_scales)
+        load_rows_apart(t3s, tab3_scales)
+        w2raw = [load_floats(w2[:, 0:512], "w2raw0")]
         t2w = load_words(tab2_words[0], "t2w")
         list1 = load_list(offs, "list1")
-        load_rows_stacked(t1s, tab_scales)
+        load_rows_apart(t1s, tab_scales)
+
+        v2s_apart = gather(U8, t2s, list2, "v2s_apart")
+        carry_rows(v2s, v2s_apart, 0, 8)
         w2raw.append(load_floats(w2[:, 512:1024], "w2raw1"))
         load_rows_stacked(w1s, w1_scales)
         w1w_both = held([P, 2, 2 * H], U8, "w1w")
         nc.sync.dma_start(w1w_both[:].bitcast(I32), w1_words.rearrange("a p c -> p a c").bitcast(I32))
         w1w = [w1w_both[:, a, :] for a in range(2)]
-        t1w = [load_words(tab_words[a], f"t1w{a}") for a in range(2)]
-
+        t1w = [load_words(tab_words[0], "t1w0")]
         v3w = gather(U16, t3w, list3, "v3w")
-        v3s = gather(U8, t3s, list3, "v3s")
+        v3s_apart = gather(U8, t3s, list3, "v3s_apart")
         w2g = [cast_on_vector("w2g0_0", sort_w2, w2raw[0], 0, 2), cast_on_scalar("w2g0_1", sort_w2, w2raw[0], 2, 4)]
         turned = psum.tile([P, 4, P], F32, name="turned", tag="bank")
         for t in range(4):
@@ -311,11 +318,13 @@ def tile_list_volleyball_rally_commentary_kernel(
             spread[:].rearrange("p r (s t) -> p r s t", t=4),
             turned[:, :, 0:4].rearrange("p t r -> p r t").unsqueeze(2).to_broadcast([P, 4, 16, 4]),
         )
-        v2s = gather(U8, t2s, list2, "v2s")
-        w2q = [quantise(w2g[0], "w2q0_0") + quantise(w2g[1], "w2q0_1")]
+        w2q = [quantise(w2g[1], "w2q0_1")]
+        w2q[0] = quantise(w2g[0], "w2q0_0") + w2q[0]
         v2w = gather(U32, t2w, list2, "v2w")
-        v1s_both = gather(U8, t1s, list1, "v1s_both")
-        lift_second_pass(v1s_second, v1s_both)
+        v1s_apart = gather(U8, t1s, list1, "v1s_apart")
+        carry_rows(v1s[0], v1s_apart, 0, 4)
+        t1w.append(load_words(tab_words[1], "t1w1"))
+        carry_rows(v1s[1], v1s_apart, 64, 4)
         th = hidden()
         receiving_tanh(th, 0, range(4))
         w2g = held([P, 2048], BF16, "w2g1", "baton")
@@ -326,20 +335,21 @@ def tile_list_volleyball_rally_commentary_kernel(
         )
         w2q.append(quantise(w2g, "w2q1"))
         lift_second_pass(w1ss_second, w1ss_both)
-        v1s = [v1s_both, v1s_second]
         w1ss = [w1ss_both, w1ss_second]
         w5raw = load_floats(w5, "w5raw")
         load_rows_side_by_side(w4s, w4_scales, W4_ROW)
         w4w = held([P, 2, N], U32, "w4w")
         nc.sync.dma_start(w4w[:].bitcast(I32), w4_words.rearrange("a p c i -> p a (c i)").bitcast(I32))
-        w3raw = [load_floats(w3[512 * b : 512 * (b + 1), :], f"w3raw{b}") for b in range(2)]
+        w3raw = [load_floats(w3[0:512, :], "w3raw0")]
+        carry_rows(v3s, v3s_apart, 0, 8)
+        w3raw.append(load_floats(w3[512:1024, :], "w3raw1"))
 
         parts = gains("h2g0", th, 2)
         w1ws = [sort_w1_words(a, [0, 1]) for a in range(2)]
         th = hidden()
         receiving_tanh(th, 1, range(4))
         v1w = [gather(U32, t1w[0], list1, "v1w0")]
-        opened = open_banks(3)
+        opened = open_banks(2)
         h2q = [quantise_wide(parts, "h2q0")]
         v1w.append(gather_in_halves(U32, t1w[1], list1, "v1w1"))
         quantise_narrow(parts, h2q[0])

@@ -75,8 +75,8 @@ def tile_list_volleyball_rally_commentary_kernel(
             rows = scales.rearrange("a q c -> (a q) c")
             nc.sync.dma_start(plane[0 : P : P // rows.shape[0], :].bitcast(I32), rows.bitcast(I32))
 
-        def carry_rows(plane, picked, first, apart):
-            for r in range(4):
+        def carry_rows(plane, picked, first, apart, rows=range(4)):
+            for r in rows:
                 src = picked[first + apart * r : first + 16 * apart : 4 * apart, :]
                 nc.sync.dma_start(plane[r:P:32, :].bitcast(I32), src.bitcast(I32))
 
@@ -91,6 +91,11 @@ def tile_list_volleyball_rally_commentary_kernel(
         def load_floats(rows, name):
             dst = held([P, 4, 512], F32, name)
             nc.sync.dma_start(dst[:], rows.rearrange("(p j) n -> p j n", j=4))
+            return dst
+
+        def load_float_columns(rows, lo, hi, name):
+            dst = held([P, 4, P * (hi - lo)], F32, name)
+            nc.sync.dma_start(dst[:], rows[:, P * lo : P * hi].rearrange("(p j) n -> p j n", j=4))
             return dst
 
         def gather(dtype, window, offsets, name):
@@ -177,6 +182,18 @@ def tile_list_volleyball_rally_commentary_kernel(
             gain_on_pool(narrow[:], th, 3, row)
             return wide, narrow
 
+        def gains_alone(name, th, lo, row):
+            grouped = for_vector([P, 2 * 512], BF16, name)
+            gain_on_vector(grouped[:], th, lo, lo + 2, row)
+            return grouped
+
+        def quantise_both(parts, name):
+            codes, plane = for_vector([P, 512], U32, name + "_codes"), held([P, 512], U8, name + "_plane")
+            for half in range(2):
+                cols = slice(256 * half, 256 * (half + 1))
+                nc.vector.quantize_mx(out=codes[:, cols].bitcast(FP8X4), scales=plane[:, cols], in_=parts[half][:])
+            return codes, plane
+
         def quantise_wide(parts, name):
             codes, plane = for_vector([P, 512], U32, name + "_codes"), held([P, 512], U8, name + "_plane")
             nc.vector.quantize_mx(out=codes[:, 0:384].bitcast(FP8X4), scales=plane[:, 0:384], in_=parts[0][:])
@@ -239,25 +256,27 @@ def tile_list_volleyball_rally_commentary_kernel(
             )
             return [ordered[:, k, :, :] for k in range(len(blocks))]
 
-        def arena(acc, n):
+        def arena(acc, n, opens):
             codes, plane = w5q[n]
             nc.tensor.matmul_mx(
                 out=acc[:], lhsT=codes, lhsT_scale=plane,
-                rhs=v3w[:].bitcast(FP4X4), rhs_scale=v3s[:], start=True, stop=False,
+                rhs=v3w[:].bitcast(FP4X4), rhs_scale=v3s[:], start=opens, stop=not opens,
             )
 
-        def receiving(n):
+        def receiving_products(n):
             m = slice(128 * n, 128 * (n + 1))
             acc = psum.tile([P, S], F32, name="y2bank", tag="bank")
-            arena(acc, n)
             for a in range(2):
                 nc.tensor.matmul_mx(
                     out=acc[:], lhsT=w4w[:, a, m].bitcast(FP8X4), lhsT_scale=w4s[W4_ROW:P, a, m],
-                    rhs=h2q[a][0][:].bitcast(FP8X4), rhs_scale=h2q[a][1][:], start=False, stop=(a == 1),
+                    rhs=h2q[a][0][:].bitcast(FP8X4), rhs_scale=h2q[a][1][:], start=(a == 0), stop=False,
                 )
-            y2 = for_scalar([P, S], F32, f"y2_{n}")
-            nc.scalar.copy(y2[:], acc[:])
-            return y2
+            return acc
+
+        def receiving(n):
+            result = for_scalar([P, S], F32, f"y2_{n}")
+            nc.scalar.copy(result[:], acc2[n][:])
+            return result
 
         def serving_pass(acc, n, b):
             codes, plane = w3q[b][n]
@@ -295,20 +314,21 @@ def tile_list_volleyball_rally_commentary_kernel(
         load_rows_apart(t2s, tab2_scales)
         load_rows_apart(t3s, tab3_scales)
         w2raw = [load_floats(w2[:, 0:512], "w2raw0")]
+        load_rows_stacked(w1s, w1_scales)
         t2w = load_words(tab2_words[0], "t2w")
         list1 = load_list(offs, "list1")
         load_rows_apart(t1s, tab_scales)
 
         v2s_apart = gather(U8, t2s, list2, "v2s_apart")
+        v3w = gather(U16, t3w, list3, "v3w")
+        v3s_apart = gather(U8, t3s, list3, "v3s_apart")
         carry_rows(v2s, v2s_apart, 0, 8)
         w2raw.append(load_floats(w2[:, 512:1024], "w2raw1"))
-        load_rows_stacked(w1s, w1_scales)
+        carry_rows(v3s, v3s_apart, 0, 8)
         w1w_both = held([P, 2, 2 * H], U8, "w1w")
         nc.sync.dma_start(w1w_both[:].bitcast(I32), w1_words.rearrange("a p c -> p a c").bitcast(I32))
         w1w = [w1w_both[:, a, :] for a in range(2)]
         t1w = [load_words(tab_words[0], "t1w0")]
-        v3w = gather(U16, t3w, list3, "v3w")
-        v3s_apart = gather(U8, t3s, list3, "v3s_apart")
         w2g = [cast_on_vector("w2g0_0", sort_w2, w2raw[0], 0, 2), cast_on_scalar("w2g0_1", sort_w2, w2raw[0], 2, 4)]
         turned = psum.tile([P, 4, P], F32, name="turned", tag="bank")
         for t in range(4):
@@ -322,64 +342,72 @@ def tile_list_volleyball_rally_commentary_kernel(
         w2q[0] = quantise(w2g[0], "w2q0_0") + w2q[0]
         v2w = gather(U32, t2w, list2, "v2w")
         v1s_apart = gather(U8, t1s, list1, "v1s_apart")
-        carry_rows(v1s[0], v1s_apart, 0, 4)
-        t1w.append(load_words(tab_words[1], "t1w1"))
-        carry_rows(v1s[1], v1s_apart, 64, 4)
-        th = hidden()
-        receiving_tanh(th, 0, range(4))
-        w2g = held([P, 2048], BF16, "w2g1", "baton")
-        nc.vector.tensor_copy(*sort_w2(w2g, w2raw[1], 0, 4))
         w1ss_both = for_vector([P, H], U8, "w1ss_both")
         nc.vector.tensor_copy(
             w1ss_both[:].rearrange("p (b t m) -> p b t m", b=2, t=4), w1s[:].rearrange("p (b m t) -> p b t m", b=2, t=4)
         )
-        w2q.append(quantise(w2g, "w2q1"))
+        carry_rows(v1s[0], v1s_apart, 0, 4)
+        t1w.append(load_words(tab_words[1], "t1w1"))
+        carry_rows(v1s[1], v1s_apart, 64, 4)
         lift_second_pass(w1ss_second, w1ss_both)
+        th = hidden()
+        receiving_tanh(th, 0, range(4))
+        w2g = held([P, 2048], BF16, "w2g1", "baton")
+        nc.vector.tensor_copy(*sort_w2(w2g, w2raw[1], 0, 4))
+        w2q.append(quantise(w2g, "w2q1"))
         w1ss = [w1ss_both, w1ss_second]
         w5raw = load_floats(w5, "w5raw")
         load_rows_side_by_side(w4s, w4_scales, W4_ROW)
         w4w = held([P, 2, N], U32, "w4w")
         nc.sync.dma_start(w4w[:].bitcast(I32), w4_words.rearrange("a p c i -> p a (c i)").bitcast(I32))
         w3raw = [load_floats(w3[0:512, :], "w3raw0")]
-        carry_rows(v3s, v3s_apart, 0, 8)
-        w3raw.append(load_floats(w3[512:1024, :], "w3raw1"))
+        w3late = [load_float_columns(w3[512:1024, :], 2 * half, 2 * half + 2, f"w3late{half}") for half in range(2)]
 
         parts = gains("h2g0", th, 2)
-        w1ws = [sort_w1_words(a, [0, 1]) for a in range(2)]
+        w1ws = [sort_w1_words(0, [0, 1])]
         th = hidden()
         receiving_tanh(th, 1, range(4))
+        w1ws.append(sort_w1_words(1, [0, 1]))
         v1w = [gather(U32, t1w[0], list1, "v1w0")]
-        opened = open_banks(2)
+        opened = open_banks(5)
         h2q = [quantise_wide(parts, "h2q0")]
+        alone = [gains_alone("h2g1_0", th, 0, 3)]
         v1w.append(gather_in_halves(U32, t1w[1], list1, "v1w1"))
-        quantise_narrow(parts, h2q[0])
-        parts = gains("h2g1", th, 3)
+        alone.append(gains_alone("h2g1_1", th, 2, 3))
         th = hidden()
         serving_tanh(th, 0, range(4))
-        w5g = [negate_on_vector("w5g_0", w5raw, 0, 2), negate_on_scalar("w5g_1", w5raw, 2, 4)]
-        h2q.append(quantise_wide(parts, "h2q1"))
-        quantise_narrow(parts, h2q[1])
+        h2q.append(quantise_both(alone, "h2q1"))
+        w5g = [negate_on_vector("w5g_0", w5raw, 0, 2)]
+        quantise_narrow(parts, h2q[0])
         parts = gains("h1g0", th, 0)
         th = hidden()
         serving_tanh(th, 1, range(4))
-        w5q = quantise(w5g[0], "w5q_0") + quantise(w5g[1], "w5q_1")
+        w5g.append(negate_on_scalar("w5g_1", w5raw, 2, 4))
+        w5q = quantise(w5g[0], "w5q_0")
         h1q = [quantise_wide(parts, "h1q0")]
         quantise_narrow(parts, h1q[0])
-        w3g = [[cast_on_scalar(f"w3g0_{half}", weave, w3raw[0], 2 * half, 2 * half + 2) for half in range(2)]]
         parts = gains("h1g1", th, 1)
-        w3q = [quantise(w3g[0][0], "w3q0_0")]
-        w3g.append([cast_on_vector("w3g1_0", weave, w3raw[1], 0, 2), cast_on_scalar("w3g1_1", weave, w3raw[1], 2, 4)])
-        y2 = [receiving(n) for n in range(4)]
+        acc2 = [receiving_products(n) for n in range(4)]
+        w5q.extend(quantise(w5g[1], "w5q_1"))
+        for n in range(4):
+            arena(acc2[n], n, False)
+        w3g = [[cast_on_scalar(f"w3g0_{half}", weave, w3raw[0], 2 * half, 2 * half + 2) for half in range(2)]]
         h1q.append(quantise_wide(parts, "h1q1"))
         quantise_narrow(parts, h1q[1])
-        w3q.append(quantise(w3g[1][0], "w3q1_0"))
-        for b in range(2):
-            w3q[b].extend(quantise(w3g[b][1], f"w3q{b}_1"))
+        w3g.append([cast_on_vector("w3g1_0", weave, w3late[0], 0, 2)])
+        w3q = [quantise(w3g[b][0], f"w3q{b}_0") for b in range(2)]
+        y2 = [receiving(0)]
+        w3g[1].extend([cast_on_vector("w3g1_2", weave, w3late[1], 0, 1), cast_on_scalar("w3g1_3", weave, w3late[1], 1, 2)])
+        y2.extend(receiving(n) for n in range(1, 4))
+        w3q[0].extend(quantise(w3g[0][1], "w3q0_1"))
+        w3q[1].extend(quantise(w3g[1][1], "w3q1_2"))
         acc1 = []
         for n in range(4):
             acc1.append(psum.tile([P, S], F32, name="y1bank", tag="bank"))
-            arena(acc1[n], n)
+            arena(acc1[n], n, True)
         for n in range(4):
+            if n == 1:
+                w3q[1].extend(quantise(w3g[1][2], "w3q1_3"))
             serving_pass(acc1[n], n, 0)
             serving_pass(acc1[n], n, 1)
             finish(acc1[n], n, [(0, S)])

@@ -240,14 +240,6 @@ def tile_list_volleyball_rally_commentary_kernel(
                     serving_products(bank, b, P * u, 0, False)
                 activate(th, u, bank)
 
-        def sort_w1_scales(a):
-            ordered = for_vector([P, H], U8, f"w1ss{a}")
-            nc.vector.tensor_copy(
-                ordered[:].rearrange("p (b t m) -> p b t m", b=2, t=4),
-                w1s[:, a, :].rearrange("p (b m t) -> p b t m", b=2, t=4),
-            )
-            return ordered
-
         def sort_w1_words(a, blocks):
             ordered = for_scalar([P, len(blocks), 4, 256], U8, f"w1ws{a}")
             lo, hi = 512 * blocks[0], 512 * (blocks[-1] + 1)
@@ -333,10 +325,10 @@ def tile_list_volleyball_rally_commentary_kernel(
         turned = psum.tile([P, 4, P], F32, name="turned", tag="bank")
         for t in range(4):
             nc.tensor.transpose(turned[:, t, :], grows[:, t:512:4], ident[:])
-        spread = for_scalar([P, 4, 64], F32, "spread")
+        spread = for_scalar([P, 3, 64], F32, "spread")
         nc.scalar.copy(
             spread[:].rearrange("p r (s t) -> p r s t", t=4),
-            turned[:, :, 0:4].rearrange("p t r -> p r t").unsqueeze(2).to_broadcast([P, 4, 16, 4]),
+            turned[:, :, 0:3].rearrange("p t r -> p r t").unsqueeze(2).to_broadcast([P, 3, 16, 4]),
         )
         w2q = [quantise(w2g[1], "w2q0_1")]
         w2q[0] = quantise(w2g[0], "w2q0_0") + w2q[0]

@@ -22,10 +22,8 @@ N = 512
 H = 1024
 T1, T2, T3 = 2048, 2048, 1024
 W4_ROW = 8
-PASS1_ROW = 16
-HALF = 1024
-VECTOR_BUFS = 25
-SCALAR_BUFS = 8
+VECTOR_BUFS = 36
+SCALAR_BUFS = 24
 
 
 def tile_list_volleyball_rally_commentary_kernel(
@@ -53,200 +51,150 @@ def tile_list_volleyball_rally_commentary_kernel(
             nc.sync.dma_start(dst[:], offsets)
             return dst
 
-        def cleared(shape, dtype, name, tag=None):
-            dst = held(shape, dtype, name, tag)
-            nc.vector.memset(dst[:].bitcast(I32), 0)
+        def cleared(shape, dtype, name, engine=nc.gpsimd):
+            dst = held(shape, dtype, name)
+            engine.memset(dst[:].bitcast(I32), 0)
             return dst
 
-        def load_rows_side_by_side(plane, scales, row0):
-            for r in range(4):
-                nc.sync.dma_start(
+        def load_rows_side_by_side(queue, plane, scales, row0, rows=range(4)):
+            for r in rows:
+                queue.dma_start(
                     plane[row0 + r : P : 32, :, :].bitcast(I32),
                     scales[:, r:16:4, :].rearrange("a q c -> q a c").bitcast(I32),
                 )
 
-        def load_rows_stacked(plane, scales):
-            for r in range(4):
+        def load_rows_stacked(plane, scales, rows):
+            for r in rows:
                 nc.sync.dma_start(
-                    plane[r:P:PASS1_ROW, :].bitcast(I32), scales.rearrange("a (q r) c -> r q a c", r=4)[r].bitcast(I32)
+                    plane[r:P:16, :].bitcast(I32), scales.rearrange("a (q r) c -> r q a c", r=4)[r].bitcast(I32)
                 )
 
-        def load_rows_apart(plane, scales):
+        def load_rows_apart(queue, window, scales, first):
             rows = scales.rearrange("a q c -> (a q) c")
-            nc.sync.dma_start(plane[0 : P : P // rows.shape[0], :].bitcast(I32), rows.bitcast(I32))
+            queue.dma_start(window[first : first + 4 * rows.shape[0] : 4, :].bitcast(I32), rows.bitcast(I32))
 
-        def carry_rows(plane, picked, first, apart, rows=range(4)):
-            for r in rows:
-                src = picked[first + apart * r : first + 16 * apart : 4 * apart, :]
-                nc.sync.dma_start(plane[r:P:32, :].bitcast(I32), src.bitcast(I32))
+        def carry_rows(queue, plane, picked, first):
+            for r in range(4):
+                queue.dma_start(plane[r:P:32, :].bitcast(I32), picked[first + 4 * r : first + 64 : 16, :].bitcast(I32))
 
-        def lift_second_pass(dst, both):
-            nc.sync.dma_start(dst[0 : P - PASS1_ROW, :].bitcast(I32), both[PASS1_ROW:P, :].bitcast(I32))
-
-        def load_words(words, name, tag=None):
-            dst = held([P, words.shape[1]], U32, name, tag)
+        def load_words(words, name):
+            dst = held([P, words.shape[1]], U32, name)
             nc.sync.dma_start(dst[:].bitcast(I32), words.rearrange("p c i -> p (c i)").bitcast(I32))
             return dst
 
         def load_floats(rows, name):
-            dst = held([P, 4, 512], F32, name)
+            dst = held([P, 4, rows.shape[1]], F32, name)
             nc.sync.dma_start(dst[:], rows.rearrange("(p j) n -> p j n", j=4))
             return dst
 
-        def load_float_columns(rows, lo, hi, name):
-            dst = held([P, 4, P * (hi - lo)], F32, name)
-            nc.sync.dma_start(dst[:], rows[:, P * lo : P * hi].rearrange("(p j) n -> p j n", j=4))
-            return dst
-
-        def gather(dtype, window, offsets, name):
+        def gather(dtype, window, offsets, name, cuts=(0, 32)):
             picked = for_vector([P, S], dtype, name)
-            nc.vector.tensor_copy(picked[:], window[:].indirect(offsets[:]))
-            return picked
-
-        def gather_in_halves(dtype, window, offsets, name):
-            picked = for_vector([P, S], dtype, name)
-            for half in range(2):
-                nc.vector.tensor_copy(
-                    picked[:, 256 * half : 256 * (half + 1)], window[:].indirect(offsets[:, 16 * half : 16 * (half + 1)])
-                )
+            for lo, hi in zip(cuts, cuts[1:]):
+                nc.vector.tensor_copy(picked[:, 16 * lo : 16 * hi], window[:].indirect(offsets[:, lo:hi]))
             return picked
 
         def quantise(grouped, name):
             words = grouped.shape[1] // 4
             codes, plane = for_vector([P, words], U32, name + "_codes"), held([P, words], U8, name + "_plane")
             nc.vector.quantize_mx(out=codes[:].bitcast(FP8X4), scales=plane[:], in_=grouped[:])
-            return [(codes[:, c : c + P].bitcast(FP8X4), plane[:, c : c + P]) for c in range(0, words, P)]
+            return codes, plane
+
+        def columns(operand):
+            codes, plane = operand
+            return [(codes[:, c : c + P].bitcast(FP8X4), plane[:, c : c + P]) for c in range(0, codes.shape[1], P)]
 
         def sort_w2(grouped, raw, lo, hi):
-            src = raw[:].rearrange("p j (m t) -> p m j t", t=4)[:, :, :, lo:hi]
-            return grouped[:].rearrange("p (t m j) -> p m j t", t=hi - lo, j=4), src
+            src = raw.rearrange("p j (m t) -> p m j t", t=4)[:, :, :, lo:hi]
+            return grouped.rearrange("p (t m j) -> p m j t", t=hi - lo, j=4), src
 
         def weave(grouped, raw, lo, hi):
             src = raw[:, :, P * lo : P * hi].rearrange("p j (c i) -> p c j i", i=4)
-            return grouped[:].rearrange("p (c i j) -> p c j i", i=4, j=4), src
+            return grouped.rearrange("p (c i j) -> p c j i", i=4, j=4), src
 
         def cast_on_vector(name, view, raw, lo, hi):
             grouped = for_vector([P, 512 * (hi - lo)], BF16, name)
-            nc.vector.tensor_copy(*view(grouped, raw, lo, hi))
+            nc.vector.tensor_copy(*view(grouped[:], raw, lo, hi))
             return grouped
 
         def cast_on_scalar(name, view, raw, lo, hi):
             grouped = for_scalar([P, 512 * (hi - lo)], BF16, name)
-            nc.scalar.copy(*view(grouped, raw, lo, hi))
+            nc.scalar.copy(*view(grouped[:], raw, lo, hi))
             return grouped
 
         def negate_on_vector(name, raw, lo, hi):
             grouped = for_vector([P, 512 * (hi - lo)], BF16, name)
-            nc.vector.tensor_scalar(*weave(grouped, raw, lo, hi), -1.0, None, ALU.mult)
+            nc.vector.tensor_scalar(*weave(grouped[:], raw, lo, hi), -1.0, None, ALU.mult)
             return grouped
 
         def negate_on_scalar(name, raw, lo, hi):
             grouped = for_scalar([P, 512 * (hi - lo)], BF16, name)
-            nc.scalar.activation(*weave(grouped, raw, lo, hi), ACT.Copy, scale=-1.0)
+            nc.scalar.activation(*weave(grouped[:], raw, lo, hi), ACT.Copy, scale=-1.0)
             return grouped
 
-        def hidden():
-            return for_scalar([P, 4, 512], F32, "th")
+        def new_bank():
+            return psum.tile([P, 4, P], F32, name="bank", tag="bank")
 
-        def activate(th, u, bank):
-            nc.scalar.activation(
-                th[:, u, :].rearrange("p (s t) -> p s t", t=4), bank[:].rearrange("p t s -> p s t"), ACT.Tanh
-            )
+        def activate(bank, name):
+            th = for_scalar([P, 512], F32, name)
+            nc.scalar.activation(th[:].rearrange("p (s t) -> p s t", t=4), bank[:].rearrange("p t s -> p s t"), ACT.Tanh)
+            return th
 
-        def receiving_tanh(th, b, blocks):
-            for u in blocks:
-                bank = psum.tile([P, 4, P], F32, name="bank", tag="bank")
-                for t in range(4):
-                    products2(bank[:, t, :], b, t, slice(P * u, P * (u + 1)))
-                activate(th, u, bank)
-
-        def gain_on_vector(grouped, th, lo, hi, row):
-            nc.vector.tensor_tensor(
-                grouped.rearrange("p (s t) -> p s t", t=4),
-                th[:, lo:hi, :].rearrange("p u (s t) -> p (u s) t", t=4),
-                turned[:, :, row].unsqueeze(1).to_broadcast([P, P * (hi - lo), 4]),
-                ALU.mult,
-            )
-
-        def gain_on_pool(grouped, th, u, row):
-            nc.gpsimd.tensor_tensor(
-                grouped.rearrange("p (x c) -> p x c", c=64),
-                th[:, u, :].rearrange("p (x c) -> p x c", c=64),
-                spread[:, row, :].unsqueeze(1).to_broadcast([P, 8, 64]),
-                ALU.mult,
-            )
-
-        def gains(name, th, row):
-            wide, narrow = for_vector([P, 3 * 512], BF16, name), held([P, 512], BF16, name + "_pool", "baton")
-            gain_on_vector(wide[:], th, 0, 3, row)
-            gain_on_pool(narrow[:], th, 3, row)
-            return wide, narrow
-
-        def gains_alone(name, th, lo, row):
-            grouped = for_vector([P, 2 * 512], BF16, name)
-            gain_on_vector(grouped[:], th, lo, lo + 2, row)
-            return grouped
-
-        def quantise_both(parts, name):
-            codes, plane = for_vector([P, 512], U32, name + "_codes"), held([P, 512], U8, name + "_plane")
-            for half in range(2):
-                cols = slice(256 * half, 256 * (half + 1))
-                nc.vector.quantize_mx(out=codes[:, cols].bitcast(FP8X4), scales=plane[:, cols], in_=parts[half][:])
-            return codes, plane
-
-        def quantise_wide(parts, name):
-            codes, plane = for_vector([P, 512], U32, name + "_codes"), held([P, 512], U8, name + "_plane")
-            nc.vector.quantize_mx(out=codes[:, 0:384].bitcast(FP8X4), scales=plane[:, 0:384], in_=parts[0][:])
-            return codes, plane
-
-        def quantise_narrow(parts, operand):
-            codes, plane = operand
-            nc.vector.quantize_mx(out=codes[:, 384:512].bitcast(FP8X4), scales=plane[:, 384:512], in_=parts[1][:])
-
-        def products2(acc, b, t, cols):
-            codes, plane = w2q[b][t]
-            nc.tensor.matmul_mx(
-                out=acc, lhsT=codes, lhsT_scale=plane,
-                rhs=v2w[:, cols].bitcast(FP8X4), rhs_scale=v2s[:, cols], start=True, stop=True,
-            )
-
-        def open_banks(count):
-            banks = []
-            for k in range(count):
-                b, first = k // 4, P * (k % 4)
-                banks.append(psum.tile([P, 4, P], F32, name="bank", tag="bank"))
-                serving_products(banks[k], b, first, 0, True)
-            return banks
-
-        def serving_products(bank, b, first, a, opens):
-            cols = slice(first, first + P)
+        def receiving_tanh(k):
+            b, cols = k // 4, slice(P * (k % 4), P * (k % 4 + 1))
+            bank = new_bank()
             for t in range(4):
-                m = slice(512 * b + 128 * t, 512 * b + 128 * (t + 1))
+                codes, plane = w2q[b][t]
                 nc.tensor.matmul_mx(
-                    out=bank[:, t, :], lhsT=w1ws[a][b][:, t, :].bitcast(FP4X4), lhsT_scale=w1ss[a][:, m],
+                    out=bank[:, t, :], lhsT=codes, lhsT_scale=plane,
+                    rhs=v2w[:, cols].bitcast(FP8X4), rhs_scale=v2s[:, cols], start=True, stop=True,
+                )
+            return activate(bank, f"thA{k}")
+
+        def serving_products(bank, k, a, opens):
+            b, cols = k // 4, slice(P * (k % 4), P * (k % 4 + 1))
+            for t in range(4):
+                nc.tensor.matmul_mx(
+                    out=bank[:, t, :], lhsT=w1ws[a][:, b, t, :].bitcast(FP4X4), lhsT_scale=w1ss[a][:, b, t, :],
                     rhs=v1w[a][:, cols].bitcast(FP8X4), rhs_scale=v1s[a][:, cols],
                     start=(opens and t == 0), stop=(not opens and t == 3),
                 )
 
-        def serving_tanh(th, b, blocks):
-            for u in blocks:
-                k = 4 * b + u
-                if k < len(opened):
-                    bank = opened[k]
-                    serving_products(bank, b, P * u, 1, False)
-                else:
-                    bank = psum.tile([P, 4, P], F32, name="bank", tag="bank")
-                    serving_products(bank, b, P * u, 1, True)
-                    serving_products(bank, b, P * u, 0, False)
-                activate(th, u, bank)
+        def open_bank(k):
+            opened[k] = new_bank()
+            serving_products(opened[k], k, 0, True)
 
-        def sort_w1_words(a, blocks):
-            ordered = for_scalar([P, len(blocks), 4, 256], U8, f"w1ws{a}")
-            lo, hi = 512 * blocks[0], 512 * (blocks[-1] + 1)
-            nc.scalar.copy(
-                ordered[:].bitcast(U16), w1w[a].bitcast(U16)[:, lo:hi].rearrange("p (b m t) -> p b t m", m=128, t=4)
+        def serving_tanh(k):
+            if k in opened:
+                bank = opened[k]
+                serving_products(bank, k, 1, False)
+            else:
+                bank = new_bank()
+                serving_products(bank, k, 1, True)
+                serving_products(bank, k, 0, False)
+            return activate(bank, f"thB{k}")
+
+        def gain_on_vector(pair, half, th, row):
+            nc.vector.tensor_tensor(
+                pair[:, 512 * half : 512 * (half + 1)].rearrange("p (s t) -> p s t", t=4),
+                th[:].rearrange("p (s t) -> p s t", t=4),
+                turned[:, :, 4 * row].unsqueeze(1).to_broadcast([P, P, 4]),
+                ALU.mult,
             )
-            return [ordered[:, k, :, :] for k in range(len(blocks))]
+
+        def gain_on_pool(pair, half, th, row):
+            nc.gpsimd.tensor_tensor(
+                pair[:, 512 * half : 512 * (half + 1)].rearrange("p (x c) -> p x c", c=64),
+                th[:].rearrange("p (x c) -> p x c", c=64),
+                spread[:, row, :].unsqueeze(1).to_broadcast([P, 8, 64]),
+                ALU.mult,
+            )
+
+        def sort_w1_words(a):
+            ordered = for_scalar([P, 2, 4, 256], U8, f"w1ws{a}")
+            nc.scalar.copy(
+                ordered[:].bitcast(U16), w1w[:, a, :].bitcast(U16).rearrange("p (b m t) -> p b t m", m=128, t=4)
+            )
+            return ordered
 
         def arena(acc, n, opens):
             codes, plane = w5q[n]
@@ -255,151 +203,177 @@ def tile_list_volleyball_rally_commentary_kernel(
                 rhs=v3w[:].bitcast(FP4X4), rhs_scale=v3s[:], start=opens, stop=not opens,
             )
 
-        def receiving_products(n):
-            m = slice(128 * n, 128 * (n + 1))
-            acc = psum.tile([P, S], F32, name="y2bank", tag="bank")
-            for a in range(2):
+        def second_passes(acc, codes, plane, hq, b, opens, closes):
+            for half in range(2):
+                moving, scale = hq[2 * b + half]
                 nc.tensor.matmul_mx(
-                    out=acc[:], lhsT=w4w[:, a, m].bitcast(FP8X4), lhsT_scale=w4s[W4_ROW:P, a, m],
-                    rhs=h2q[a][0][:].bitcast(FP8X4), rhs_scale=h2q[a][1][:], start=(a == 0), stop=False,
+                    out=acc[:, 256 * half : 256 * (half + 1)], lhsT=codes, lhsT_scale=plane,
+                    rhs=moving[:].bitcast(FP8X4), rhs_scale=scale[:],
+                    start=(opens and half == 0), stop=(closes and half == 1),
                 )
+
+        def arena_bank(n, name):
+            acc = psum.tile([P, S], F32, name=name, tag="bank")
+            arena(acc, n, True)
             return acc
 
-        def receiving(n):
+        def receiving_passes(n):
+            m = slice(128 * n, 128 * (n + 1))
+            acc = psum.tile([P, S], F32, name="y2bank", tag="bank")
+            for b in range(2):
+                second_passes(acc, w4w[:, b, m].bitcast(FP8X4), w4s[W4_ROW:P, b, m], h2q, b, b == 0, False)
+            return acc
+
+        def receiving(acc, n):
             result = for_scalar([P, S], F32, f"y2_{n}")
-            nc.scalar.copy(result[:], acc2[n][:])
+            nc.scalar.copy(result[:], acc[:])
             return result
 
-        def serving_pass(acc, n, b):
-            codes, plane = w3q[b][n]
-            nc.tensor.matmul_mx(
-                out=acc[:], lhsT=codes, lhsT_scale=plane,
-                rhs=h1q[b][0][:].bitcast(FP8X4), rhs_scale=h1q[b][1][:], start=False, stop=(b == 1),
-            )
+        def serving_passes(n, b):
+            second_passes(acc1[n], *w3q[b][n], h1q, b, False, b == 1)
 
-        def finish(acc, n, pieces):
-            for lo, hi in pieces:
-                res = for_vector([P, hi - lo], F32, f"res{n}")
-                nc.vector.tensor_tensor(res[:], acc[:, lo:hi], y2[n][:, lo:hi], ALU.max)
-                nc.sync.dma_start(out[128 * n : 128 * (n + 1), lo:hi], res[:])
+        def finish(acc, n):
+            res = for_vector([P, S], F32, f"res{n}")
+            nc.vector.tensor_tensor(res[:], acc[:], y2[n][:], ALU.max)
+            nc.sync.dma_start(out[128 * n : 128 * (n + 1), :], res[:])
 
-        t2s = cleared([P, T2], U8, "t2s")
-        t3s = cleared([P, T3], U8, "t3s")
-        ident = held([P, P], F32, "ident")
-        make_identity(nc, ident[:])
-        grows = held([P, 512], F32, "grows")
-        nc.vector.memset(grows[:], 0.0)
-        t1s = cleared([P, T1], U8, "t1s")
-        v2s = cleared([P, S], U8, "v2s")
+
+        t2s = cleared([P, T2], U8, "t2s", nc.vector)
+        t3s = cleared([P, T3], U8, "t3s", nc.vector)
+        t1s = cleared([P, T1], U8, "t1s", nc.vector)
         w1s = cleared([P, H], U8, "w1s")
-        v1s = [cleared([P, S], U8, f"v1s{a}") for a in range(2)]
-        v3s = cleared([P, S], U8, "v3s")
+        grows = cleared([P, 512], F32, "grows")
+        planes = cleared([P, 4, S], U8, "planes")
+        v2s, v3s, v1s = planes[:, 0, :], planes[:, 1, :], [planes[:, 2, :], planes[:, 3, :]]
+        w1second = cleared([P, 2, 4, P], U8, "w1second")
         w4s = cleared([P, 2, N], U8, "w4s")
-        w1ss_second = cleared([P, H], U8, "w1ss_second")
-        nc.gpsimd.dma_start(grows[0:2, :], g1.rearrange("(b c) -> b c", b=2))
-        nc.gpsimd.dma_start(grows[2:4, :], g2.rearrange("(b c) -> b c", b=2))
 
         t3w = held([P, T3], U16, "t3w")
         nc.sync.dma_start(t3w[:].bitcast(I32), tab3_words[0].bitcast(I32))
-        list2 = load_list(offs2, "list2")
         list3 = load_list(offs3, "list3")
-        load_rows_apart(t2s, tab2_scales)
-        load_rows_apart(t3s, tab3_scales)
-        w2raw = [load_floats(w2[:, 0:512], "w2raw0")]
-        load_rows_stacked(w1s, w1_scales)
-        t2w = load_words(tab2_words[0], "t2w")
+        list2 = load_list(offs2, "list2")
         list1 = load_list(offs, "list1")
-        load_rows_apart(t1s, tab_scales)
-
+        load_rows_apart(nc.sync, t2s, tab2_scales, 32)
+        w2raw = [load_floats(w2[:, 0:512], "w2raw0")]
+        load_rows_apart(nc.sync, t3s, tab3_scales, 32)
+        load_rows_apart(nc.sync, t1s, tab_scales, 0)
+        load_rows_stacked(w1s, w1_scales, range(2))
+        nc.sync.dma_start(grows[0:8:4, :], g1.rearrange("(b c) -> b c", b=2))
+        nc.sync.dma_start(grows[8:16:4, :], g2.rearrange("(b c) -> b c", b=2))
+        t2w = load_words(tab2_words[0], "t2w")
         v2s_apart = gather(U8, t2s, list2, "v2s_apart")
         v3w = gather(U16, t3w, list3, "v3w")
+        ident = held([P, P], F32, "ident", "t2s")
+        make_identity(nc, ident[:])
         v3s_apart = gather(U8, t3s, list3, "v3s_apart")
-        carry_rows(v2s, v2s_apart, 0, 8)
+        carry_rows(nc.sync, v2s, v2s_apart, 32)
+        load_rows_stacked(w1s, w1_scales, range(2, 4))
         w2raw.append(load_floats(w2[:, 512:1024], "w2raw1"))
-        carry_rows(v3s, v3s_apart, 0, 8)
-        w1w_both = held([P, 2, 2 * H], U8, "w1w")
-        nc.sync.dma_start(w1w_both[:].bitcast(I32), w1_words.rearrange("a p c -> p a c").bitcast(I32))
-        w1w = [w1w_both[:, a, :] for a in range(2)]
+        carry_rows(nc.sync, v3s, v3s_apart, 32)
+        w1w = held([P, 2, 2 * H], U8, "w1w")
+        nc.sync.dma_start(w1w[:].bitcast(I32), w1_words.rearrange("a p c -> p a c").bitcast(I32))
         t1w = [load_words(tab_words[0], "t1w0")]
-        w2g = [cast_on_vector("w2g0_0", sort_w2, w2raw[0], 0, 2), cast_on_scalar("w2g0_1", sort_w2, w2raw[0], 2, 4)]
+        v1s_apart = gather(U8, t1s, list1, "v1s_apart")
+        carry_rows(nc.sync, v1s[0], v1s_apart, 0)
         turned = psum.tile([P, 4, P], F32, name="turned", tag="bank")
         for t in range(4):
             nc.tensor.transpose(turned[:, t, :], grows[:, t:512:4], ident[:])
-        spread = for_scalar([P, 3, 64], F32, "spread")
+
+        g00 = cast_on_scalar("w2g00", sort_w2, w2raw[0][:], 0, 2)
+        g01 = cast_on_scalar("w2g01", sort_w2, w2raw[0][:], 2, 4)
+        spread = for_scalar([P, 4, 64], F32, "spread")
         nc.scalar.copy(
             spread[:].rearrange("p r (s t) -> p r s t", t=4),
-            turned[:, :, 0:3].rearrange("p t r -> p r t").unsqueeze(2).to_broadcast([P, 3, 16, 4]),
+            turned[:, :, 0:16:4].rearrange("p t r -> p r t").unsqueeze(2).to_broadcast([P, 4, 16, 4]),
         )
-        w2q = [quantise(w2g[1], "w2q0_1")]
-        w2q[0] = quantise(w2g[0], "w2q0_0") + w2q[0]
-        v2w = gather(U32, t2w, list2, "v2w")
-        v1s_apart = gather(U8, t1s, list1, "v1s_apart")
-        w1ss_both = for_vector([P, H], U8, "w1ss_both")
-        nc.vector.tensor_copy(
-            w1ss_both[:].rearrange("p (b t m) -> p b t m", b=2, t=4), w1s[:].rearrange("p (b m t) -> p b t m", b=2, t=4)
-        )
-        carry_rows(v1s[0], v1s_apart, 0, 4)
+        w2q = [columns(quantise(g00, "w2q00")) + columns(quantise(g01, "w2q01"))]
+        v2w = gather(U32, t2w, list2, "v2w", (0, 16, 32))
+        A = [receiving_tanh(k) for k in range(4)]
+        w1first = for_vector([P, 2, 4, P], U8, "w1first")
+        nc.vector.tensor_copy(w1first[:], w1s[:].rearrange("p (b m t) -> p b t m", b=2, t=4))
+        w1ss = [w1first, w1second]
         t1w.append(load_words(tab_words[1], "t1w1"))
-        carry_rows(v1s[1], v1s_apart, 64, 4)
-        lift_second_pass(w1ss_second, w1ss_both)
-        th = hidden()
-        receiving_tanh(th, 0, range(4))
-        w2g = held([P, 2048], BF16, "w2g1", "baton")
-        nc.vector.tensor_copy(*sort_w2(w2g, w2raw[1], 0, 4))
-        w2q.append(quantise(w2g, "w2q1"))
-        w1ss = [w1ss_both, w1ss_second]
+        carry_rows(nc.sync, v1s[1], v1s_apart, 64)
+        nc.sync.dma_start(w1second[0 : P - 16].bitcast(I32), w1first[16:P].bitcast(I32))
         w5raw = load_floats(w5, "w5raw")
-        load_rows_side_by_side(w4s, w4_scales, W4_ROW)
+        load_rows_side_by_side(nc.sync, w4s, w4_scales, W4_ROW)
         w4w = held([P, 2, N], U32, "w4w")
         nc.sync.dma_start(w4w[:].bitcast(I32), w4_words.rearrange("a p c i -> p a (c i)").bitcast(I32))
-        w3raw = [load_floats(w3[0:512, :], "w3raw0")]
-        w3late = [load_float_columns(w3[512:1024, :], 2 * half, 2 * half + 2, f"w3late{half}") for half in range(2)]
+        w3raw = load_floats(w3[0:512, :], "w3raw0")
+        w3late = [load_floats(w3[512:1024, 256 * half : 256 * (half + 1)], f"w3late{half}") for half in range(2)]
 
-        parts = gains("h2g0", th, 2)
-        w1ws = [sort_w1_words(0, [0, 1])]
-        th = hidden()
-        receiving_tanh(th, 1, range(4))
-        w1ws.append(sort_w1_words(1, [0, 1]))
-        v1w = [gather(U32, t1w[0], list1, "v1w0")]
-        opened = open_banks(5)
-        h2q = [quantise_wide(parts, "h2q0")]
-        alone = [gains_alone("h2g1_0", th, 0, 3)]
-        v1w.append(gather_in_halves(U32, t1w[1], list1, "v1w1"))
-        alone.append(gains_alone("h2g1_1", th, 2, 3))
-        th = hidden()
-        serving_tanh(th, 0, range(4))
-        h2q.append(quantise_both(alone, "h2q1"))
-        w5g = [negate_on_vector("w5g_0", w5raw, 0, 2)]
-        quantise_narrow(parts, h2q[0])
-        parts = gains("h1g0", th, 0)
-        th = hidden()
-        serving_tanh(th, 1, range(4))
-        w5g.append(negate_on_scalar("w5g_1", w5raw, 2, 4))
-        w5q = quantise(w5g[0], "w5q_0")
-        h1q = [quantise_wide(parts, "h1q0")]
-        quantise_narrow(parts, h1q[0])
-        parts = gains("h1g1", th, 1)
-        acc2 = [receiving_products(n) for n in range(4)]
-        w5q.extend(quantise(w5g[1], "w5q_1"))
-        for n in range(4):
+        g10 = cast_on_vector("w2g10", sort_w2, w2raw[1][:], 0, 2)
+        g11 = held([P, 1024], BF16, "w2g11", "baton")
+        nc.vector.tensor_copy(*sort_w2(g11[:], w2raw[1][:], 2, 4))
+        w2q.append(columns(quantise(g10, "w2q10")) + columns(quantise(g11, "w2q11")))
+        w1ws = [sort_w1_words(0)]
+        A.extend(receiving_tanh(k) for k in range(4, 8))
+        w1ws.append(sort_w1_words(1))
+        pa = [held([P, 1024], BF16, "pa0", "baton")]
+        gain_on_pool(pa[0], 0, A[0], 2)
+        gain_on_vector(pa[0], 1, A[1], 2)
+        pa.append(for_vector([P, 1024], BF16, "pa1"))
+        gain_on_vector(pa[1], 0, A[2], 2)
+        gain_on_vector(pa[1], 1, A[3], 2)
+        h2q = [quantise(pa[0], "h2q0")]
+        v1w = [gather(U32, t1w[0], list1, "v1w0", (0, 16, 32))]
+        pa.append(held([P, 1024], BF16, "pa2", "baton"))
+        gain_on_pool(pa[2], 0, A[4], 3)
+        gain_on_vector(pa[2], 1, A[5], 3)
+        opened = {}
+        for k in range(6):
+            open_bank(k)
+        pa.append(for_vector([P, 1024], BF16, "pa3"))
+        gain_on_vector(pa[3], 0, A[6], 3)
+        gain_on_pool(pa[3], 1, A[7], 3)
+        v1w.append(gather(U32, t1w[1], list1, "v1w1", (0, 8, 16, 32)))
+        B = [serving_tanh(k) for k in range(8)]
+        h2q.extend(quantise(pa[k], f"h2q{k}") for k in (1, 3, 2))
+        h2q[2:4] = [h2q[3], h2q[2]]
+        pb = [for_vector([P, 1024], BF16, "pb0")]
+        gain_on_vector(pb[0], 0, B[0], 0)
+        w5g = [held([P, 1024], BF16, "w5g0", "baton")]
+        nc.vector.tensor_scalar(*weave(w5g[0][:], w5raw[:], 0, 2), -1.0, None, ALU.mult)
+        gain_on_vector(pb[0], 1, B[1], 0)
+        w5q = columns(quantise(w5g[0], "w5q0"))
+        h1q = [quantise(pb[0], "h1q0")]
+        pb.append(held([P, 1024], BF16, "pb1", "baton"))
+        gain_on_pool(pb[1], 0, B[2], 0)
+        gain_on_vector(pb[1], 1, B[3], 0)
+        pb.append(for_vector([P, 1024], BF16, "pb2"))
+        gain_on_vector(pb[2], 0, B[4], 1)
+        gain_on_vector(pb[2], 1, B[5], 1)
+        pb.append(held([P, 1024], BF16, "pb3"))
+        gain_on_pool(pb[3], 0, B[6], 1)
+        gain_on_vector(pb[3], 1, B[7], 1)
+        w5g.append(negate_on_scalar("w5g1", w5raw[:], 2, 4))
+        acc2 = [receiving_passes(n) for n in range(4)]
+        for n in range(2):
             arena(acc2[n], n, False)
-        w3g = [[cast_on_scalar(f"w3g0_{half}", weave, w3raw[0], 2 * half, 2 * half + 2) for half in range(2)]]
-        h1q.append(quantise_wide(parts, "h1q1"))
-        quantise_narrow(parts, h1q[1])
-        w3g.append([cast_on_vector("w3g1_0", weave, w3late[0], 0, 2)])
-        w3q = [quantise(w3g[b][0], f"w3q{b}_0") for b in range(2)]
-        y2 = [receiving(0)]
-        w3g[1].extend([cast_on_vector("w3g1_2", weave, w3late[1], 0, 1), cast_on_scalar("w3g1_3", weave, w3late[1], 1, 2)])
-        y2.extend(receiving(n) for n in range(1, 4))
-        w3q[0].extend(quantise(w3g[0][1], "w3q0_1"))
-        w3q[1].extend(quantise(w3g[1][1], "w3q1_2"))
-        acc1 = []
-        for n in range(4):
-            acc1.append(psum.tile([P, S], F32, name="y1bank", tag="bank"))
-            arena(acc1[n], n, True)
-        for n in range(4):
-            if n == 1:
-                w3q[1].extend(quantise(w3g[1][2], "w3q1_3"))
-            serving_pass(acc1[n], n, 0)
-            serving_pass(acc1[n], n, 1)
-            finish(acc1[n], n, [(0, S)])
+        acc1 = [arena_bank(n, "y1bank") for n in range(2)]
+        h1q.append(quantise(pb[1], "h1q1"))
+        w5q.extend(columns(quantise(w5g[1], "w5q1")))
+        for n in range(2, 4):
+            arena(acc2[n], n, False)
+        acc1.extend(arena_bank(n, "y1bank") for n in range(2, 4))
+        w3g = [cast_on_scalar(f"w3g0{half}", weave, w3raw[:], 2 * half, 2 * half + 2) for half in range(2)]
+        h1q.extend(quantise(pb[k], f"h1q{k}") for k in (2, 3))
+        late = [cast_on_vector("w3g10", weave, w3late[0][:], 0, 2)]
+        w3q = [columns(quantise(w3g[0], "w3q00")), columns(quantise(late[0], "w3q10"))]
+        for n in range(2):
+            serving_passes(n, 0)
+            serving_passes(n, 1)
+        y2 = [receiving(acc2[0], 0)]
+        w3q[0].extend(columns(quantise(w3g[1], "w3q01")))
+        late.append(cast_on_vector("w3g12", weave, w3late[1][:], 0, 1))
+        late.append(cast_on_scalar("w3g13", weave, w3late[1][:], 1, 2))
+        y2.extend(receiving(acc2[n], n) for n in range(1, 4))
+        for n in range(2, 4):
+            serving_passes(n, 0)
+        finish(acc1[0], 0)
+        w3q[1].extend(columns(quantise(late[1], "w3q12")))
+        w3q[1].extend(columns(quantise(late[2], "w3q13")))
+        finish(acc1[1], 1)
+        for n in range(2, 4):
+            serving_passes(n, 1)
+            finish(acc1[n], n)

@@ -22,8 +22,8 @@ N = 512
 H = 1024
 T1, T2, T3 = 2048, 2048, 1024
 W4_ROW = 8
-VECTOR_BUFS = 36
-SCALAR_BUFS = 24
+VECTOR_BUFS = 27
+SCALAR_BUFS = 11
 
 
 def tile_list_volleyball_rally_commentary_kernel(
@@ -51,9 +51,9 @@ def tile_list_volleyball_rally_commentary_kernel(
             nc.sync.dma_start(dst[:], offsets)
             return dst
 
-        def cleared(shape, dtype, name, engine=nc.gpsimd):
+        def cleared(shape, dtype, name):
             dst = held(shape, dtype, name)
-            engine.memset(dst[:].bitcast(I32), 0)
+            nc.vector.memset(dst[:].bitcast(I32), 0)
             return dst
 
         def load_rows_side_by_side(queue, plane, scales, row0, rows=range(4)):
@@ -99,6 +99,14 @@ def tile_list_volleyball_rally_commentary_kernel(
             nc.vector.quantize_mx(out=codes[:].bitcast(FP8X4), scales=plane[:], in_=grouped[:])
             return codes, plane
 
+        def quantise_into(operand, first, grouped):
+            codes, plane = operand
+            cols = slice(first, first + grouped.shape[1] // 4)
+            nc.vector.quantize_mx(out=codes[:, cols].bitcast(FP8X4), scales=plane[:, cols], in_=grouped[:])
+
+        def whole_pass(name):
+            return for_vector([P, S], U32, name + "_codes"), held([P, S], U8, name + "_plane")
+
         def columns(operand):
             codes, plane = operand
             return [(codes[:, c : c + P].bitcast(FP8X4), plane[:, c : c + P]) for c in range(0, codes.shape[1], P)]
@@ -134,12 +142,17 @@ def tile_list_volleyball_rally_commentary_kernel(
         def new_bank():
             return psum.tile([P, 4, P], F32, name="bank", tag="bank")
 
-        def activate(bank, name):
-            th = for_scalar([P, 512], F32, name)
-            nc.scalar.activation(th[:].rearrange("p (s t) -> p s t", t=4), bank[:].rearrange("p t s -> p s t"), ACT.Tanh)
+        def activate(bank, th):
+            nc.scalar.activation(th.rearrange("p (s t) -> p s t", t=4), bank[:].rearrange("p t s -> p s t"), ACT.Tanh)
+
+        def run_of_tanh(step, first, count, name, tag=None):
+            shape = [P, count, 512]
+            th = held(shape, F32, name, tag) if tag else for_scalar(shape, F32, name)
+            for u in range(count):
+                step(first + u, th[:, u, :])
             return th
 
-        def receiving_tanh(k):
+        def receiving_tanh(k, th):
             b, cols = k // 4, slice(P * (k % 4), P * (k % 4 + 1))
             bank = new_bank()
             for t in range(4):
@@ -148,7 +161,7 @@ def tile_list_volleyball_rally_commentary_kernel(
                     out=bank[:, t, :], lhsT=codes, lhsT_scale=plane,
                     rhs=v2w[:, cols].bitcast(FP8X4), rhs_scale=v2s[:, cols], start=True, stop=True,
                 )
-            return activate(bank, f"thA{k}")
+            activate(bank, th)
 
         def serving_products(bank, k, a, opens):
             b, cols = k // 4, slice(P * (k % 4), P * (k % 4 + 1))
@@ -163,7 +176,7 @@ def tile_list_volleyball_rally_commentary_kernel(
             opened[k] = new_bank()
             serving_products(opened[k], k, 0, True)
 
-        def serving_tanh(k):
+        def serving_tanh(k, th):
             if k in opened:
                 bank = opened[k]
                 serving_products(bank, k, 1, False)
@@ -171,23 +184,29 @@ def tile_list_volleyball_rally_commentary_kernel(
                 bank = new_bank()
                 serving_products(bank, k, 1, True)
                 serving_products(bank, k, 0, False)
-            return activate(bank, f"thB{k}")
+            activate(bank, th)
 
-        def gain_on_vector(pair, half, th, row):
+        def gain_on_vector(th, row, name, tag=None):
+            blocks = th.shape[1]
+            shape = [P, 512 * blocks]
+            grouped = held(shape, BF16, name, tag) if tag else for_vector(shape, BF16, name)
             nc.vector.tensor_tensor(
-                pair[:, 512 * half : 512 * (half + 1)].rearrange("p (s t) -> p s t", t=4),
-                th[:].rearrange("p (s t) -> p s t", t=4),
-                turned[:, :, 4 * row].unsqueeze(1).to_broadcast([P, P, 4]),
+                grouped[:].rearrange("p (s t) -> p s t", t=4),
+                th[:].rearrange("p u (s t) -> p (u s) t", t=4),
+                turned[:, :, 4 * row].unsqueeze(1).to_broadcast([P, P * blocks, 4]),
                 ALU.mult,
             )
+            return grouped
 
-        def gain_on_pool(pair, half, th, row):
+        def gain_on_pool(th, row, name, tag=None):
+            grouped = held([P, 512], BF16, name, tag)
             nc.gpsimd.tensor_tensor(
-                pair[:, 512 * half : 512 * (half + 1)].rearrange("p (x c) -> p x c", c=64),
-                th[:].rearrange("p (x c) -> p x c", c=64),
+                grouped[:].rearrange("p (x c) -> p x c", c=64),
+                th[:, 0, :].rearrange("p (x c) -> p x c", c=64),
                 spread[:, row, :].unsqueeze(1).to_broadcast([P, 8, 64]),
                 ALU.mult,
             )
+            return grouped
 
         def sort_w1_words(a):
             ordered = for_scalar([P, 2, 4, 256], U8, f"w1ws{a}")
@@ -203,14 +222,16 @@ def tile_list_volleyball_rally_commentary_kernel(
                 rhs=v3w[:].bitcast(FP4X4), rhs_scale=v3s[:], start=opens, stop=not opens,
             )
 
-        def second_passes(acc, codes, plane, hq, b, opens, closes):
-            for half in range(2):
-                moving, scale = hq[2 * b + half]
+        def second_passes(acc, codes, plane, pieces, opens, closes):
+            first = 0
+            for k, (moving, scale) in enumerate(pieces):
+                width = moving.shape[1]
                 nc.tensor.matmul_mx(
-                    out=acc[:, 256 * half : 256 * (half + 1)], lhsT=codes, lhsT_scale=plane,
+                    out=acc[:, first : first + width], lhsT=codes, lhsT_scale=plane,
                     rhs=moving[:].bitcast(FP8X4), rhs_scale=scale[:],
-                    start=(opens and half == 0), stop=(closes and half == 1),
+                    start=(opens and k == 0), stop=(closes and k == len(pieces) - 1),
                 )
+                first = first + width
 
         def arena_bank(n, name):
             acc = psum.tile([P, S], F32, name=name, tag="bank")
@@ -221,7 +242,7 @@ def tile_list_volleyball_rally_commentary_kernel(
             m = slice(128 * n, 128 * (n + 1))
             acc = psum.tile([P, S], F32, name="y2bank", tag="bank")
             for b in range(2):
-                second_passes(acc, w4w[:, b, m].bitcast(FP8X4), w4s[W4_ROW:P, b, m], h2q, b, b == 0, False)
+                second_passes(acc, w4w[:, b, m].bitcast(FP8X4), w4s[W4_ROW:P, b, m], h2q[b], b == 0, False)
             return acc
 
         def receiving(acc, n):
@@ -230,7 +251,7 @@ def tile_list_volleyball_rally_commentary_kernel(
             return result
 
         def serving_passes(n, b):
-            second_passes(acc1[n], *w3q[b][n], h1q, b, False, b == 1)
+            second_passes(acc1[n], *w3q[b][n], h1q[b], False, b == 1)
 
         def finish(acc, n):
             res = for_vector([P, S], F32, f"res{n}")
@@ -238,36 +259,35 @@ def tile_list_volleyball_rally_commentary_kernel(
             nc.sync.dma_start(out[128 * n : 128 * (n + 1), :], res[:])
 
 
-        t2s = cleared([P, T2], U8, "t2s", nc.vector)
-        t3s = cleared([P, T3], U8, "t3s", nc.vector)
-        t1s = cleared([P, T1], U8, "t1s", nc.vector)
-        w1s = cleared([P, H], U8, "w1s")
+        t2s = cleared([P, T2], U8, "t2s")
+        t3s = cleared([P, T3], U8, "t3s")
+        ident = held([P, P], F32, "ident")
+        make_identity(nc, ident[:])
         grows = cleared([P, 512], F32, "grows")
+        t1s = cleared([P, T1], U8, "t1s")
+        w1s = cleared([P, H], U8, "w1s")
         planes = cleared([P, 4, S], U8, "planes")
         v2s, v3s, v1s = planes[:, 0, :], planes[:, 1, :], [planes[:, 2, :], planes[:, 3, :]]
         w1second = cleared([P, 2, 4, P], U8, "w1second")
         w4s = cleared([P, 2, N], U8, "w4s")
+        nc.gpsimd.dma_start(grows[0:8:4, :], g1.rearrange("(b c) -> b c", b=2))
+        nc.gpsimd.dma_start(grows[8:16:4, :], g2.rearrange("(b c) -> b c", b=2))
 
         t3w = held([P, T3], U16, "t3w")
         nc.sync.dma_start(t3w[:].bitcast(I32), tab3_words[0].bitcast(I32))
         list3 = load_list(offs3, "list3")
         list2 = load_list(offs2, "list2")
-        list1 = load_list(offs, "list1")
         load_rows_apart(nc.sync, t2s, tab2_scales, 32)
-        w2raw = [load_floats(w2[:, 0:512], "w2raw0")]
         load_rows_apart(nc.sync, t3s, tab3_scales, 32)
+        w2raw = [load_floats(w2[:, 0:512], "w2raw0")]
+        list1 = load_list(offs, "list1")
         load_rows_apart(nc.sync, t1s, tab_scales, 0)
-        load_rows_stacked(w1s, w1_scales, range(2))
-        nc.sync.dma_start(grows[0:8:4, :], g1.rearrange("(b c) -> b c", b=2))
-        nc.sync.dma_start(grows[8:16:4, :], g2.rearrange("(b c) -> b c", b=2))
+        load_rows_stacked(w1s, w1_scales, range(4))
         t2w = load_words(tab2_words[0], "t2w")
         v2s_apart = gather(U8, t2s, list2, "v2s_apart")
         v3w = gather(U16, t3w, list3, "v3w")
-        ident = held([P, P], F32, "ident", "t2s")
-        make_identity(nc, ident[:])
         v3s_apart = gather(U8, t3s, list3, "v3s_apart")
         carry_rows(nc.sync, v2s, v2s_apart, 32)
-        load_rows_stacked(w1s, w1_scales, range(2, 4))
         w2raw.append(load_floats(w2[:, 512:1024], "w2raw1"))
         carry_rows(nc.sync, v3s, v3s_apart, 32)
         w1w = held([P, 2, 2 * H], U8, "w1w")
@@ -288,7 +308,7 @@ def tile_list_volleyball_rally_commentary_kernel(
         )
         w2q = [columns(quantise(g00, "w2q00")) + columns(quantise(g01, "w2q01"))]
         v2w = gather(U32, t2w, list2, "v2w", (0, 16, 32))
-        A = [receiving_tanh(k) for k in range(4)]
+        A = [run_of_tanh(receiving_tanh, 0, 3, "thA0", "thA0"), run_of_tanh(receiving_tanh, 3, 1, "thA3")]
         w1first = for_vector([P, 2, 4, P], U8, "w1first")
         nc.vector.tensor_copy(w1first[:], w1s[:].rearrange("p (b m t) -> p b t m", b=2, t=4))
         w1ss = [w1first, w1second]
@@ -307,57 +327,42 @@ def tile_list_volleyball_rally_commentary_kernel(
         nc.vector.tensor_copy(*sort_w2(g11[:], w2raw[1][:], 2, 4))
         w2q.append(columns(quantise(g10, "w2q10")) + columns(quantise(g11, "w2q11")))
         w1ws = [sort_w1_words(0)]
-        A.extend(receiving_tanh(k) for k in range(4, 8))
+        A.extend([run_of_tanh(receiving_tanh, 4, 2, "thA4"), run_of_tanh(receiving_tanh, 6, 1, "thA6"), run_of_tanh(receiving_tanh, 7, 1, "thA7")])
         w1ws.append(sort_w1_words(1))
-        pa = [held([P, 1024], BF16, "pa0", "baton")]
-        gain_on_pool(pa[0], 0, A[0], 2)
-        gain_on_vector(pa[0], 1, A[1], 2)
-        pa.append(for_vector([P, 1024], BF16, "pa1"))
-        gain_on_vector(pa[1], 0, A[2], 2)
-        gain_on_vector(pa[1], 1, A[3], 2)
-        h2q = [quantise(pa[0], "h2q0")]
+        ga = [gain_on_vector(A[0], 2, "ga0"), gain_on_pool(A[1], 2, "ga3", "baton")]
         v1w = [gather(U32, t1w[0], list1, "v1w0", (0, 16, 32))]
-        pa.append(held([P, 1024], BF16, "pa2", "baton"))
-        gain_on_pool(pa[2], 0, A[4], 3)
-        gain_on_vector(pa[2], 1, A[5], 3)
+        h2q = [[whole_pass("h2q0")]]
+        quantise_into(h2q[0][0], 0, ga[0])
+        ga.extend([gain_on_vector(A[2], 3, "ga4"), gain_on_pool(A[3], 3, "ga6", "t1w0")])
         opened = {}
-        for k in range(6):
+        for k in range(5):
             open_bank(k)
-        pa.append(for_vector([P, 1024], BF16, "pa3"))
-        gain_on_vector(pa[3], 0, A[6], 3)
-        gain_on_pool(pa[3], 1, A[7], 3)
         v1w.append(gather(U32, t1w[1], list1, "v1w1", (0, 8, 16, 32)))
-        B = [serving_tanh(k) for k in range(8)]
-        h2q.extend(quantise(pa[k], f"h2q{k}") for k in (1, 3, 2))
-        h2q[2:4] = [h2q[3], h2q[2]]
-        pb = [for_vector([P, 1024], BF16, "pb0")]
-        gain_on_vector(pb[0], 0, B[0], 0)
-        w5g = [held([P, 1024], BF16, "w5g0", "baton")]
-        nc.vector.tensor_scalar(*weave(w5g[0][:], w5raw[:], 0, 2), -1.0, None, ALU.mult)
-        gain_on_vector(pb[0], 1, B[1], 0)
-        w5q = columns(quantise(w5g[0], "w5q0"))
-        h1q = [quantise(pb[0], "h1q0")]
-        pb.append(held([P, 1024], BF16, "pb1", "baton"))
-        gain_on_pool(pb[1], 0, B[2], 0)
-        gain_on_vector(pb[1], 1, B[3], 0)
-        pb.append(for_vector([P, 1024], BF16, "pb2"))
-        gain_on_vector(pb[2], 0, B[4], 1)
-        gain_on_vector(pb[2], 1, B[5], 1)
-        pb.append(held([P, 1024], BF16, "pb3"))
-        gain_on_pool(pb[3], 0, B[6], 1)
-        gain_on_vector(pb[3], 1, B[7], 1)
+        B = [run_of_tanh(serving_tanh, 0, 3, "thB0", "thB0"), run_of_tanh(serving_tanh, 3, 1, "thB3")]
+        B.extend([run_of_tanh(serving_tanh, 4, 3, "thB4", "thA0"), run_of_tanh(serving_tanh, 7, 1, "thB7")])
+        ga.append(gain_on_vector(A[4], 3, "ga7"))
+        h2q.append([quantise(ga[2], "h2q4"), quantise(ga[3], "h2q6"), quantise(ga[4], "h2q7")])
+        w5g = [negate_on_vector("w5g0", w5raw[:], 0, 2)]
+        quantise_into(h2q[0][0], 384, ga[1])
+        gb = [gain_on_vector(B[0], 0, "gb0"), gain_on_pool(B[1], 0, "gb3", "baton")]
         w5g.append(negate_on_scalar("w5g1", w5raw[:], 2, 4))
+        w5q = columns(quantise(w5g[0], "w5q0"))
+        h1q = [[whole_pass("h1q0")]]
+        quantise_into(h1q[0][0], 0, gb[0])
+        quantise_into(h1q[0][0], 384, gb[1])
+        gb.extend([gain_on_vector(B[2], 1, "gb4"), gain_on_pool(B[3], 1, "gb7", "baton")])
         acc2 = [receiving_passes(n) for n in range(4)]
         for n in range(2):
             arena(acc2[n], n, False)
         acc1 = [arena_bank(n, "y1bank") for n in range(2)]
-        h1q.append(quantise(pb[1], "h1q1"))
         w5q.extend(columns(quantise(w5g[1], "w5q1")))
         for n in range(2, 4):
             arena(acc2[n], n, False)
         acc1.extend(arena_bank(n, "y1bank") for n in range(2, 4))
         w3g = [cast_on_scalar(f"w3g0{half}", weave, w3raw[:], 2 * half, 2 * half + 2) for half in range(2)]
-        h1q.extend(quantise(pb[k], f"h1q{k}") for k in (2, 3))
+        h1q.append([whole_pass("h1q1")])
+        quantise_into(h1q[1][0], 0, gb[2])
+        quantise_into(h1q[1][0], 384, gb[3])
         late = [cast_on_vector("w3g10", weave, w3late[0][:], 0, 2)]
         w3q = [columns(quantise(w3g[0], "w3q00")), columns(quantise(late[0], "w3q10"))]
         for n in range(2):

@@ -369,16 +369,16 @@ def tile_list_volleyball_rally_commentary_kernel(
             serving_passes(n, 0)
             serving_passes(n, 1)
         y2 = [receiving(acc2[0], 0)]
-        w3q[0].extend(columns(quantise(w3g[1], "w3q01")))
         late.append(cast_on_vector("w3g12", weave, w3late[1][:], 0, 1))
         late.append(cast_on_scalar("w3g13", weave, w3late[1][:], 1, 2))
         y2.extend(receiving(acc2[n], n) for n in range(1, 4))
-        for n in range(2, 4):
-            serving_passes(n, 0)
-        finish(acc1[0], 0)
+        w3q[0].extend(columns(quantise(w3g[1], "w3q01")))
         w3q[1].extend(columns(quantise(late[1], "w3q12")))
+        serving_passes(2, 0)
+        serving_passes(2, 1)
+        serving_passes(3, 0)
+        finish(acc1[0], 0)
         w3q[1].extend(columns(quantise(late[2], "w3q13")))
-        finish(acc1[1], 1)
-        for n in range(2, 4):
-            serving_passes(n, 1)
+        serving_passes(3, 1)
+        for n in range(1, 4):
             finish(acc1[n], n)

@@ -289,7 +289,6 @@ def tile_list_volleyball_rally_commentary_kernel(
         v3s_apart = gather(U8, t3s, list3, "v3s_apart")
         carry_rows(nc.sync, v2s, v2s_apart, 32)
         w2raw.append(load_floats(w2[:, 512:1024], "w2raw1"))
-        carry_rows(nc.sync, v3s, v3s_apart, 32)
         w1w = held([P, 2, 2 * H], U8, "w1w")
         nc.sync.dma_start(w1w[:].bitcast(I32), w1_words.rearrange("a p c -> p a c").bitcast(I32))
         t1w = [load_words(tab_words[0], "t1w0")]
@@ -320,6 +319,7 @@ def tile_list_volleyball_rally_commentary_kernel(
         w4w = held([P, 2, N], U32, "w4w")
         nc.sync.dma_start(w4w[:].bitcast(I32), w4_words.rearrange("a p c i -> p a (c i)").bitcast(I32))
         w3raw = load_floats(w3[0:512, :], "w3raw0")
+        carry_rows(nc.sync, v3s, v3s_apart, 32)
         w3late = [load_floats(w3[512:1024, 256 * half : 256 * (half + 1)], f"w3late{half}") for half in range(2)]
 
         g10 = cast_on_vector("w2g10", sort_w2, w2raw[1][:], 0, 2)

@@ -331,8 +331,8 @@ def tile_list_volleyball_rally_commentary_kernel(
         w1ws.append(sort_w1_words(1))
         ga = [gain_on_vector(A[0], 2, "ga0"), gain_on_pool(A[1], 2, "ga3", "baton")]
         v1w = [gather(U32, t1w[0], list1, "v1w0", (0, 16, 32))]
-        h2q = [[whole_pass("h2q0")]]
-        quantise_into(h2q[0][0], 0, ga[0])
+        codes, plane = quantise(ga[0], "h2q0")
+        h2q = [[(codes[:, 0:256], plane[:, 0:256]), (codes[:, 256:384], plane[:, 256:384])]]
         ga.extend([gain_on_vector(A[2], 3, "ga4"), gain_on_pool(A[3], 3, "ga6", "t1w0")])
         opened = {}
         for k in range(5):
@@ -343,7 +343,7 @@ def tile_list_volleyball_rally_commentary_kernel(
         ga.append(gain_on_vector(A[4], 3, "ga7"))
         h2q.append([quantise(ga[2], "h2q4"), quantise(ga[3], "h2q6"), quantise(ga[4], "h2q7")])
         w5g = [negate_on_vector("w5g0", w5raw[:], 0, 2)]
-        quantise_into(h2q[0][0], 384, ga[1])
+        h2q[0].append(quantise(ga[1], "h2q3"))
         gb = [gain_on_vector(B[0], 0, "gb0"), gain_on_pool(B[1], 0, "gb3", "baton")]
         w5g.append(negate_on_scalar("w5g1", w5raw[:], 2, 4))
         w5q = columns(quantise(w5g[0], "w5q0"))

@@ -270,8 +270,6 @@ def tile_list_volleyball_rally_commentary_kernel(
         v2s, v3s, v1s = planes[:, 0, :], planes[:, 1, :], [planes[:, 2, :], planes[:, 3, :]]
         w1second = cleared([P, 2, 4, P], U8, "w1second")
         w4s = cleared([P, 2, N], U8, "w4s")
-        nc.gpsimd.dma_start(grows[0:8:4, :], g1.rearrange("(b c) -> b c", b=2))
-        nc.gpsimd.dma_start(grows[8:16:4, :], g2.rearrange("(b c) -> b c", b=2))
 
         t3w = held([P, T3], U16, "t3w")
         nc.sync.dma_start(t3w[:].bitcast(I32), tab3_words[0].bitcast(I32))
@@ -280,14 +278,17 @@ def tile_list_volleyball_rally_commentary_kernel(
         load_rows_apart(nc.sync, t2s, tab2_scales, 32)
         load_rows_apart(nc.sync, t3s, tab3_scales, 32)
         w2raw = [load_floats(w2[:, 0:512], "w2raw0")]
+        nc.sync.dma_start(grows[0:8:4, :], g1.rearrange("(b c) -> b c", b=2))
+        nc.sync.dma_start(grows[8:16:4, :], g2.rearrange("(b c) -> b c", b=2))
         list1 = load_list(offs, "list1")
         load_rows_apart(nc.sync, t1s, tab_scales, 0)
-        load_rows_stacked(w1s, w1_scales, range(4))
+        load_rows_stacked(w1s, w1_scales, range(2))
         t2w = load_words(tab2_words[0], "t2w")
         v2s_apart = gather(U8, t2s, list2, "v2s_apart")
         v3w = gather(U16, t3w, list3, "v3w")
         v3s_apart = gather(U8, t3s, list3, "v3s_apart")
         carry_rows(nc.sync, v2s, v2s_apart, 32)
+        load_rows_stacked(w1s, w1_scales, range(2, 4))
         w2raw.append(load_floats(w2[:, 512:1024], "w2raw1"))
         w1w = held([P, 2, 2 * H], U8, "w1w")
         nc.sync.dma_start(w1w[:].bitcast(I32), w1_words.rearrange("a p c -> p a c").bitcast(I32))

from contextlib import ExitStack

import concourse.mybir as mybir
from concourse.masks import make_identity

FLOPS = 2952790016

F32 = mybir.dt.float32
BF16 = mybir.dt.bfloat16
I32 = mybir.dt.int32
U32 = mybir.dt.uint32
U16 = mybir.dt.uint16
U8 = mybir.dt.uint8
FP8X4 = mybir.dt.float8_e4m3fn_x4
FP4X4 = mybir.dt.float4_e2m1fn_x4
ACT = mybir.ActivationFunctionType
ALU = mybir.AluOpType

P = 128
S = 512
N = 512
H = 1024
T1, T2, T3 = 2048, 2048, 1024
W4_ROW = 8
VECTOR_BUFS = 27
SCALAR_BUFS = 11


def tile_list_volleyball_rally_commentary_kernel(
    tc, tab_words, tab_scales, tab2_words, tab2_scales, tab3_words, tab3_scales, offs, offs2, offs3,
    w1_words, w1_scales, w2, w3, w4_words, w4_scales, w5, g1, g2, out,
):
    nc = tc.nc
    with ExitStack() as ctx:
        keep = ctx.enter_context(tc.tile_pool(name="keep", bufs=1))
        vector_line = ctx.enter_context(tc.tile_pool(name="vector_line", bufs=VECTOR_BUFS))
        scalar_line = ctx.enter_context(tc.tile_pool(name="scalar_line", bufs=SCALAR_BUFS))
        psum = ctx.enter_context(tc.psum_pool(name="psum", bufs=8))

        def held(shape, dtype, name, tag=None):
            return keep.tile(shape, dtype, name=name, tag=tag or name, align_bytes=64)

        def for_vector(shape, dtype, name):
            return vector_line.tile(shape, dtype, name=name, tag="line", align_bytes=64)

        def for_scalar(shape, dtype, name):
            return scalar_line.tile(shape, dtype, name=name, tag="line", align_bytes=64)

        def load_list(offsets, name):
            dst = held([P, S // 16], U16, name)
            nc.sync.dma_start(dst[:], offsets)
            return dst

        def cleared(shape, dtype, name):
            dst = held(shape, dtype, name)
            nc.vector.memset(dst[:].bitcast(I32), 0)
            return dst

        def load_rows_side_by_side(queue, plane, scales, row0, rows=range(4)):
            for r in rows:
                queue.dma_start(
                    plane[row0 + r : P : 32, :, :].bitcast(I32),
                    scales[:, r:16:4, :].rearrange("a q c -> q a c").bitcast(I32),
                )

        def load_rows_stacked(plane, scales, rows):
            for r in rows:
                nc.sync.dma_start(
                    plane[r:P:16, :].bitcast(I32), scales.rearrange("a (q r) c -> r q a c", r=4)[r].bitcast(I32)
                )

        def load_rows_apart(queue, window, scales, first):
            rows = scales.rearrange("a q c -> (a q) c")
            queue.dma_start(window[first : first + 4 * rows.shape[0] : 4, :].bitcast(I32), rows.bitcast(I32))

        def carry_rows(queue, plane, picked, first):
            for r in range(4):
                queue.dma_start(plane[r:P:32, :].bitcast(I32), picked[first + 4 * r : first + 64 : 16, :].bitcast(I32))

        def load_words(words, name):
            dst = held([P, words.shape[1]], U32, name)
            nc.sync.dma_start(dst[:].bitcast(I32), words.rearrange("p c i -> p (c i)").bitcast(I32))
            return dst

        def load_floats(rows, name):
            dst = held([P, 4, rows.shape[1]], F32, name)
            nc.sync.dma_start(dst[:], rows.rearrange("(p j) n -> p j n", j=4))
            return dst

        def gather(dtype, window, offsets, name, cuts=(0, 32)):
            picked = for_vector([P, S], dtype, name)
            for lo, hi in zip(cuts, cuts[1:]):
                nc.vector.tensor_copy(picked[:, 16 * lo : 16 * hi], window[:].indirect(offsets[:, lo:hi]))
            return picked

        def quantise(grouped, name):
            words = grouped.shape[1] // 4
            codes, plane = for_vector([P, words], U32, name + "_codes"), held([P, words], U8, name + "_plane")
            nc.vector.quantize_mx(out=codes[:].bitcast(FP8X4), scales=plane[:], in_=grouped[:])
            return codes, plane

        def quantise_into(operand, first, grouped):
            codes, plane = operand
            cols = slice(first, first + grouped.shape[1] // 4)
            nc.vector.quantize_mx(out=codes[:, cols].bitcast(FP8X4), scales=plane[:, cols], in_=grouped[:])

        def whole_pass(name):
            return for_vector([P, S], U32, name + "_codes"), held([P, S], U8, name + "_plane")

        def columns(operand):
            codes, plane = operand
            return [(codes[:, c : c + P].bitcast(FP8X4), plane[:, c : c + P]) for c in range(0, codes.shape[1], P)]

        def sort_w2(grouped, raw, lo, hi):
            src = raw.rearrange("p j (m t) -> p m j t", t=4)[:, :, :, lo:hi]
            return grouped.rearrange("p (t m j) -> p m j t", t=hi - lo, j=4), src

        def weave(grouped, raw, lo, hi):
            src = raw[:, :, P * lo : P * hi].rearrange("p j (c i) -> p c j i", i=4)
            return grouped.rearrange("p (c i j) -> p c j i", i=4, j=4), src

        def cast_on_vector(name, view, raw, lo, hi):
            grouped = for_vector([P, 512 * (hi - lo)], BF16, name)
            nc.vector.tensor_copy(*view(grouped[:], raw, lo, hi))
            return grouped

        def cast_on_scalar(name, view, raw, lo, hi):
            grouped = for_scalar([P, 512 * (hi - lo)], BF16, name)
            nc.scalar.copy(*view(grouped[:], raw, lo, hi))
            return grouped

        def negate_on_vector(name, raw, lo, hi):
            grouped = for_vector([P, 512 * (hi - lo)], BF16, name)
            nc.vector.tensor_scalar(*weave(grouped[:], raw, lo, hi), -1.0, None, ALU.mult)
            return grouped

        def negate_on_scalar(name, raw, lo, hi):
            grouped = for_scalar([P, 512 * (hi - lo)], BF16, name)
            nc.scalar.activation(*weave(grouped[:], raw, lo, hi), ACT.Copy, scale=-1.0)
            return grouped

        def new_bank():
            return psum.tile([P, 4, P], F32, name="bank", tag="bank")

        def activate(bank, th):
            nc.scalar.activation(th.rearrange("p (s t) -> p s t", t=4), bank[:].rearrange("p t s -> p s t"), ACT.Tanh)

        def run_of_tanh(step, first, count, name, tag=None):
            shape = [P, count, 512]
            th = held(shape, F32, name, tag) if tag else for_scalar(shape, F32, name)
            for u in range(count):
                step(first + u, th[:, u, :])
            return th

        def receiving_tanh(k, th):
            b, cols = k // 4, slice(P * (k % 4), P * (k % 4 + 1))
            bank = new_bank()
            for t in range(4):
                codes, plane = w2q[b][t]
                nc.tensor.matmul_mx(
                    out=bank[:, t, :], lhsT=codes, lhsT_scale=plane,
                    rhs=v2w[:, cols].bitcast(FP8X4), rhs_scale=v2s[:, cols], start=True, stop=True,
                )
            activate(bank, th)

        def serving_products(bank, k, a, opens):
            b, cols = k // 4, slice(P * (k % 4), P * (k % 4 + 1))
            for t in range(4):
                nc.tensor.matmul_mx(
                    out=bank[:, t, :], lhsT=w1ws[a][:, b, t, :].bitcast(FP4X4), lhsT_scale=w1ss[a][:, b, t, :],
                    rhs=v1w[a][:, cols].bitcast(FP8X4), rhs_scale=v1s[a][:, cols],
                    start=(opens and t == 0), stop=(not opens and t == 3),
                )

        def open_bank(k):
            opened[k] = new_bank()
            serving_products(opened[k], k, 0, True)

        def serving_tanh(k, th):
            if k in opened:
                bank = opened[k]
                serving_products(bank, k, 1, False)
            else:
                bank = new_bank()
                serving_products(bank, k, 1, True)
                serving_products(bank, k, 0, False)
            activate(bank, th)

        def gain_on_vector(th, row, name, tag=None):
            blocks = th.shape[1]
            shape = [P, 512 * blocks]
            grouped = held(shape, BF16, name, tag) if tag else for_vector(shape, BF16, name)
            nc.vector.tensor_tensor(
                grouped[:].rearrange("p (s t) -> p s t", t=4),
                th[:].rearrange("p u (s t) -> p (u s) t", t=4),
                turned[:, :, 4 * row].unsqueeze(1).to_broadcast([P, P * blocks, 4]),
                ALU.mult,
            )
            return grouped

        def gain_on_pool(th, row, name, tag=None):
            grouped = held([P, 512], BF16, name, tag)
            nc.gpsimd.tensor_tensor(
                grouped[:].rearrange("p (x c) -> p x c", c=64),
                th[:, 0, :].rearrange("p (x c) -> p x c", c=64),
                spread[:, row, :].unsqueeze(1).to_broadcast([P, 8, 64]),
                ALU.mult,
            )
            return grouped

        def sort_w1_words(a):
            ordered = for_scalar([P, 2, 4, 256], U8, f"w1ws{a}")
            nc.scalar.copy(
                ordered[:].bitcast(U16), w1w[:, a, :].bitcast(U16).rearrange("p (b m t) -> p b t m", m=128, t=4)
            )
            return ordered

        def arena(acc, n, opens):
            codes, plane = w5q[n]
            nc.tensor.matmul_mx(
                out=acc[:], lhsT=codes, lhsT_scale=plane,
                rhs=v3w[:].bitcast(FP4X4), rhs_scale=v3s[:], start=opens, stop=not opens,
            )

        def second_passes(acc, codes, plane, pieces, opens, closes):
            first = 0
            for k, (moving, scale) in enumerate(pieces):
                width = moving.shape[1]
                nc.tensor.matmul_mx(
                    out=acc[:, first : first + width], lhsT=codes, lhsT_scale=plane,
                    rhs=moving[:].bitcast(FP8X4), rhs_scale=scale[:],
                    start=(opens and k == 0), stop=(closes and k == len(pieces) - 1),
                )
                first = first + width

        def arena_bank(n, name):
            acc = psum.tile([P, S], F32, name=name, tag="bank")
            arena(acc, n, True)
            return acc

        def receiving_passes(n):
            m = slice(128 * n, 128 * (n + 1))
            acc = psum.tile([P, S], F32, name="y2bank", tag="bank")
            for b in range(2):
                second_passes(acc, w4w[:, b, m].bitcast(FP8X4), w4s[W4_ROW:P, b, m], h2q[b], b == 0, False)
            return acc

        def receiving(acc, n):
            result = for_scalar([P, S], F32, f"y2_{n}")
            nc.scalar.copy(result[:], acc[:])
            return result

        def serving_passes(n, b):
            second_passes(acc1[n], *w3q[b][n], h1q[b], False, b == 1)

        def finish(acc, n):
            res = for_vector([P, S], F32, f"res{n}")
            nc.vector.tensor_tensor(res[:], acc[:], y2[n][:], ALU.max)
            nc.sync.dma_start(out[128 * n : 128 * (n + 1), :], res[:])


        t2s = cleared([P, T2], U8, "t2s")
        t3s = cleared([P, T3], U8, "t3s")
        ident = held([P, P], F32, "ident")
        make_identity(nc, ident[:])
        grows = cleared([P, 512], F32, "grows")
        t1s = cleared([P, T1], U8, "t1s")
        w1s = cleared([P, H], U8, "w1s")
        planes = cleared([P, 4, S], U8, "planes")
        v2s, v3s, v1s = planes[:, 0, :], planes[:, 1, :], [planes[:, 2, :], planes[:, 3, :]]
        w1second = cleared([P, 2, 4, P], U8, "w1second")
        w4s = cleared([P, 2, N], U8, "w4s")

        t3w = held([P, T3], U16, "t3w")
        nc.sync.dma_start(t3w[:].bitcast(I32), tab3_words[0].bitcast(I32))
        list3 = load_list(offs3, "list3")
        list2 = load_list(offs2, "list2")
        load_rows_apart(nc.sync, t2s, tab2_scales, 32)
        load_rows_apart(nc.sync, t3s, tab3_scales, 32)
        w2raw = [load_floats(w2[:, 0:512], "w2raw0")]
        nc.sync.dma_start(grows[0:8:4, :], g1.rearrange("(b c) -> b c", b=2))
        nc.sync.dma_start(grows[8:16:4, :], g2.rearrange("(b c) -> b c", b=2))
        list1 = load_list(offs, "list1")
        load_rows_apart(nc.sync, t1s, tab_scales, 0)
        load_rows_stacked(w1s, w1_scales, range(2))
        t2w = load_words(tab2_words[0], "t2w")
        v2s_apart = gather(U8, t2s, list2, "v2s_apart")
        v3w = gather(U16, t3w, list3, "v3w")
        v3s_apart = gather(U8, t3s, list3, "v3s_apart")
        carry_rows(nc.sync, v2s, v2s_apart, 32)
        load_rows_stacked(w1s, w1_scales, range(2, 4))
        w2raw.append(load_floats(w2[:, 512:1024], "w2raw1"))
        w1w = held([P, 2, 2 * H], U8, "w1w")
        nc.sync.dma_start(w1w[:].bitcast(I32), w1_words.rearrange("a p c -> p a c").bitcast(I32))
        t1w = [load_words(tab_words[0], "t1w0")]
        v1s_apart = gather(U8, t1s, list1, "v1s_apart")
        carry_rows(nc.sync, v1s[0], v1s_apart, 0)
        turned = psum.tile([P, 4, P], F32, name="turned", tag="bank")
        for t in range(4):
            nc.tensor.transpose(turned[:, t, :], grows[:, t:512:4], ident[:])

        g00 = cast_on_scalar("w2g00", sort_w2, w2raw[0][:], 0, 2)
        g01 = cast_on_scalar("w2g01", sort_w2, w2raw[0][:], 2, 4)
        spread = for_scalar([P, 4, 64], F32, "spread")
        nc.scalar.copy(
            spread[:].rearrange("p r (s t) -> p r s t", t=4),
            turned[:, :, 0:16:4].rearrange("p t r -> p r t").unsqueeze(2).to_broadcast([P, 4, 16, 4]),
        )
        w2q = [columns(quantise(g00, "w2q00")) + columns(quantise(g01, "w2q01"))]
        v2w = gather(U32, t2w, list2, "v2w", (0, 16, 32))
        A = [run_of_tanh(receiving_tanh, 0, 3, "thA0", "thA0"), run_of_tanh(receiving_tanh, 3, 1, "thA3")]
        w1first = for_vector([P, 2, 4, P], U8, "w1first")
        nc.vector.tensor_copy(w1first[:], w1s[:].rearrange("p (b m t) -> p b t m", b=2, t=4))
        w1ss = [w1first, w1second]
        t1w.append(load_words(tab_words[1], "t1w1"))
        carry_rows(nc.sync, v1s[1], v1s_apart, 64)
        nc.sync.dma_start(w1second[0 : P - 16].bitcast(I32), w1first[16:P].bitcast(I32))
        w5raw = load_floats(w5, "w5raw")
        load_rows_side_by_side(nc.sync, w4s, w4_scales, W4_ROW)
        w4w = held([P, 2, N], U32, "w4w")
        nc.sync.dma_start(w4w[:].bitcast(I32), w4_words.rearrange("a p c i -> p a (c i)").bitcast(I32))
        w3raw = load_floats(w3[0:512, :], "w3raw0")
        carry_rows(nc.sync, v3s, v3s_apart, 32)
        w3late = [load_floats(w3[512:1024, 256 * half : 256 * (half + 1)], f"w3late{half}") for half in range(2)]

        g10 = cast_on_vector("w2g10", sort_w2, w2raw[1][:], 0, 2)
        g11 = held([P, 1024], BF16, "w2g11", "baton")
        nc.vector.tensor_copy(*sort_w2(g11[:], w2raw[1][:], 2, 4))
        w2q.append(columns(quantise(g10, "w2q10")) + columns(quantise(g11, "w2q11")))
        w1ws = [sort_w1_words(0)]
        A.extend([run_of_tanh(receiving_tanh, 4, 2, "thA4"), run_of_tanh(receiving_tanh, 6, 1, "thA6"), run_of_tanh(receiving_tanh, 7, 1, "thA7")])
        w1ws.append(sort_w1_words(1))
        ga = [gain_on_vector(A[0], 2, "ga0"), gain_on_pool(A[1], 2, "ga3", "baton")]
        v1w = [gather(U32, t1w[0], list1, "v1w0", (0, 16, 32))]
        codes, plane = quantise(ga[0], "h2q0")
        h2q = [[(codes[:, 0:256], plane[:, 0:256]), (codes[:, 256:384], plane[:, 256:384])]]
        ga.extend([gain_on_vector(A[2], 3, "ga4"), gain_on_pool(A[3], 3, "ga6", "t1w0")])
        opened = {}
        for k in range(5):
            open_bank(k)
        v1w.append(gather(U32, t1w[1], list1, "v1w1", (0, 8, 16, 32)))
        B = [run_of_tanh(serving_tanh, 0, 3, "thB0", "thB0"), run_of_tanh(serving_tanh, 3, 1, "thB3")]
        B.extend([run_of_tanh(serving_tanh, 4, 3, "thB4", "thA0"), run_of_tanh(serving_tanh, 7, 1, "thB7")])
        ga.append(gain_on_vector(A[4], 3, "ga7"))
        h2q.append([quantise(ga[2], "h2q4"), quantise(ga[3], "h2q6"), quantise(ga[4], "h2q7")])
        w5g = [negate_on_vector("w5g0", w5raw[:], 0, 2)]
        h2q[0].append(quantise(ga[1], "h2q3"))
        gb = [gain_on_vector(B[0], 0, "gb0"), gain_on_pool(B[1], 0, "gb3", "baton")]
        w5g.append(negate_on_scalar("w5g1", w5raw[:], 2, 4))
        w5q = columns(quantise(w5g[0], "w5q0"))
        h1q = [[whole_pass("h1q0")]]
        quantise_into(h1q[0][0], 0, gb[0])
        quantise_into(h1q[0][0], 384, gb[1])
        gb.extend([gain_on_vector(B[2], 1, "gb4"), gain_on_pool(B[3], 1, "gb7", "baton")])
        acc2 = [receiving_passes(n) for n in range(4)]
        for n in range(2):
            arena(acc2[n], n, False)
        acc1 = [arena_bank(n, "y1bank") for n in range(2)]
        w5q.extend(columns(quantise(w5g[1], "w5q1")))
        for n in range(2, 4):
            arena(acc2[n], n, False)
        acc1.extend(arena_bank(n, "y1bank") for n in range(2, 4))
        w3g = [cast_on_scalar(f"w3g0{half}", weave, w3raw[:], 2 * half, 2 * half + 2) for half in range(2)]
        h1q.append([whole_pass("h1q1")])
        quantise_into(h1q[1][0], 0, gb[2])
        quantise_into(h1q[1][0], 384, gb[3])
        late = [cast_on_vector("w3g10", weave, w3late[0][:], 0, 2)]
        w3q = [columns(quantise(w3g[0], "w3q00")), columns(quantise(late[0], "w3q10"))]
        for n in range(2):
            serving_passes(n, 0)
            serving_passes(n, 1)
        y2 = [receiving(acc2[0], 0)]
        late.append(cast_on_vector("w3g12", weave, w3late[1][:], 0, 1))
        late.append(cast_on_scalar("w3g13", weave, w3late[1][:], 1, 2))
        y2.extend(receiving(acc2[n], n) for n in range(1, 4))
        w3q[0].extend(columns(quantise(w3g[1], "w3q01")))
        w3q[1].extend(columns(quantise(late[1], "w3q12")))
        serving_passes(2, 0)
        serving_passes(2, 1)
        serving_passes(3, 0)
        finish(acc1[0], 0)
        w3q[1].extend(columns(quantise(late[2], "w3q13")))
        serving_passes(3, 1)
        for n in range(1, 4):
            finish(acc1[n], n)
